import numpy as np, ml_dtypes
CORES = [25,29,65,69,153,157,193,197]
N = 8
BF = ml_dtypes.bfloat16
def f(rng, *shape):
    return (rng.standard_normal(shape, dtype=np.float32) * np.exp2(rng.integers(-2, 3, shape[:-1] + (1,)))).astype(BF)
def wide(rng, *shape):
    v = f(rng, *shape).astype(np.float32); k = shape[:-2] + (1, shape[-1])
    return (v * np.exp2(rng.integers(-6, 7, k)) * (rng.random(k) > 0.0625)).astype(BF)
R, W, S, C = 8, 128, 3, 1
H = N * R
ROW, COL = np.arange(H)[None, :, None], np.arange(W)[None, None, :]
def stored(v):
    return np.ascontiguousarray(v.reshape(8, N, R, W).transpose(1, 0, 2, 3)).reshape(N, 8, R * W).astype(np.int32)
def whole(v):
    return np.ascontiguousarray(v.reshape(N, 8, R, W).transpose(1, 0, 2, 3)).reshape(8, H, W).astype(np.int64)
def field(rng):
    d = np.repeat(np.repeat(rng.integers(-1, 2, (2, 8, H // 8, W // 16)), 8, axis=2), 16, axis=3)
    d = np.roll(d, int(rng.integers(1, 8)), axis=2)
    return np.where(rng.random(d.shape) < 0.125, rng.integers(-1, 2, d.shape), d)
def inputs_of(rng, v):
    return {"vy": stored(v[0]), "vx": stored(v[1]), "img": f(rng, N, 128, C * R * W)}
def setup_inputs(rng):
    return inputs_of(rng, field(rng))
def setup_inputs_far(rng):
    v = np.zeros((2, 8, H, W), np.int64); o = rng.permutation(8)
    for k in range(8):
        v[0, o[k]] = 1 if k & 1 else -1; v[1, o[k]] = 1 if k & 2 else -1
        if k >= 4:
            m = rng.random((2, H, W)) < 0.015625
            v[:, o[k]] = np.where(m, rng.integers(-1, 2, (2, H, W)), v[:, o[k]])
    return inputs_of(rng, v)
def setup_inputs_ends(rng):
    v = field(rng); pm = np.array([-1, 1])
    for e in (0, H - 1): v[0, :, e, :] = rng.choice(pm, (8, W))
    for e in (0, W - 1): v[1, :, :, e] = rng.choice(pm, (8, H))
    v[0, :, 1, :] = np.where(rng.random((8, W)) < 0.75, -1, 1); v[0, :, H - 2, :] = np.where(rng.random((8, W)) < 0.75, 1, -1)
    v[1, :, :, 1] = np.where(rng.random((8, H)) < 0.75, -1, 1); v[1, :, :, W - 2] = np.where(rng.random((8, H)) < 0.75, 1, -1)
    o = rng.permutation(8); g, h = o[0], o[1]
    v[0, g, 0, :] = 2 * (np.arange(W) & 1) - 1; v[1, g, 0, :] = 1
    v[0, g, H - 1, :] = 2 * (np.arange(W) & 1) - 1; v[1, g, H - 1, :] = -1
    v[1, h, :, 0] = 2 * (np.arange(H) & 1) - 1; v[0, h, :, 0] = 1
    v[1, h, :, W - 1] = 2 * (np.arange(H) & 1) - 1; v[0, h, :, W - 1] = -1
    return inputs_of(rng, v)
def setup_inputs_sinks(rng):
    v = np.zeros((2, 8, H, W), np.int64); o = rng.permutation(8)
    v[1, o[1]] = 1 - 2 * (COL[0] & 1)
    v[0, o[2]] = 2 * (ROW[0] & 1) - 1
    for k in range(3, 8):
        r0, c0 = int(rng.integers(0, H)), int(rng.integers(0, W))
        if k == 3: r0 = R * int(rng.integers(1, N))
        if k == 4: r0 = R * int(rng.integers(1, N)) - 1
        v[0, o[k]] = np.sign(r0 - ROW[0]); v[1, o[k]] = np.sign(c0 - COL[0])
    return inputs_of(rng, v)
def setup_inputs_spread(rng):
    d = setup_inputs(rng); d["img"] = wide(rng, N, 128, C * R * W); return d
def check_inputs(d):
    bad = [k for k in ("vy", "vx") if not np.isin(np.asarray(d[k]), [-1, 0, 1]).all()]
    return bad + ([] if np.isfinite(np.asarray(d["img"]).astype(np.float32)).all() else ["finite"])
def place(a, b):
    return np.minimum(np.maximum(ROW + a, 0), H - 1), (COL + b) % W
def reference(vy, vx, img):
    a, b = whole(vy), whole(vx); g = np.arange(8)[:, None, None]
    for s in range(S):
        p, q = place(a, b)
        a, b = a + a[g, p, q], b + b[g, p, q]
    p, q = place(a, b)
    u = np.ascontiguousarray(img.reshape(N, 8, 16, C, R, W).transpose(1, 0, 4, 5, 2, 3)).reshape(8, H, W, 16, C)
    z = u[g, p, q].reshape(8, N, R, W, 16, C)
    return {"y": np.ascontiguousarray(z.transpose(1, 0, 4, 5, 2, 3)).reshape(N, 128, C * R * W)}

@@ -1,0 +1,473 @@
+from concourse.bass import DstId, RemoteDMATransfer
+from concourse.mybir import AluOpType as A, ActivationFunctionType as F
+
+BF, F32, I32, U16 = "bfloat16", "float32", "int32", "uint16"
+SIM_CORES = 256
+W_OUT, W_OVER = 320, 192
+DIG_ENGINES = 4
+SCRATCH = {
+    "vyi": ("sbuf", [128, 4, 16], I32), "vxi": ("sbuf", [128, 4, 16], I32), "ci": ("sbuf", [128, 4, 16], I32),
+    "xiota": ("sbuf", [128, 4, 16], I32), "pidx": ("sbuf", [128, 1], I32), "hi": ("sbuf", [128, 1], I32),
+    "oi": ("sbuf", [128, 1], I32), "mi": ("sbuf", [128, 1], I32),
+    "hrow": ("sbuf", [128, 1], F32), "h128": ("sbuf", [128, 1], F32),
+    "odd": ("sbuf", [128, 1], F32), "even": ("sbuf", [128, 1], F32), "kcol": ("sbuf", [128, 8], F32),
+    "dig": ("sbuf", [128, 8, 16], BF),
+    "dnr": ("dram", [128, 4, 16], BF), "dnc": ("dram", [128, 4, 16], BF),
+    "dfr": ("dram", [128, 4, 16], BF), "dfc": ("dram", [128, 4, 16], BF),
+    "gg": ("sbuf", [128, 4, 16], F32), "blk": ("sbuf", [128, 4, 32], F32), "tb": ("sbuf", [128, 128], F32),
+    "lf": ("sbuf", [128, 64], F32), "lsn": ("sbuf", [128, 64], U16), "lsf": ("sbuf", [128, 64], U16),
+    "ln1": ("sbuf", [128, 48], U16), "lf1": ("sbuf", [128, 48], U16), "rh": ("sbuf", [128, 48], U16),
+    "l0": ("sbuf", [128, 192], U16), "l1": ("sbuf", [128, 192], U16), "l2": ("sbuf", [128, 192], U16),
+    "l2e": ("sbuf", [128, 192], U16), "l3": ("sbuf", [128, 192], U16),
+    "w0": ("sbuf", [128, 3072], BF), "w1": ("sbuf", [128, 3072], BF), "w2": ("sbuf", [128, 3072], BF),
+    "jb": ("sbuf", [128, 3072], BF), "pic": ("sbuf", [128, 3072], BF), "yo": ("sbuf", [128, 1024], BF),
+    "sel": ("sbuf", [128, 144], BF),
+    "rvr": ("dram", [128, 4, 16], BF), "rvc": ("dram", [128, 4, 16], BF), "rg": ("sbuf", [128, 64], U16),
+    "rp": ("sbuf", [128, W_OUT], BF), "rq": ("sbuf", [128, W_OVER], BF),
+    "bp": ("psum", [128, 32, 16], F32), "po": ("psum", [128, 512], F32), "pn": ("psum", [128, 512], F32),
+    "pf": ("psum", [128, 512], F32), "p2": ("psum", [128, 512], F32), "p3": ("psum", [128, 512], F32),
+}
+SEMAPHORES = ["vc", "gi", "ldy", "ldx", "ldi", "ldj", "ms", "msh", "msj", "sb", "sel1", "sel2", "dgr", "dgc", "gd", "lo",
+              "pv", "rs_o", "rs_n", "rs_f", "g_e", "g_n", "g_f", "g_f2", "h_o", "h_m", "h_n", "h_f", "g_2", "g_j", "g_3a",
+              "g_3b", "t_o", "t_n", "t_f", "t_2", "t_3", "c_o", "c_n", "c_f", "c_2", "c_2b", "c_3", "vir0", "vir1", "vir2",
+              "vn", "vfr", "vfc", "gvn", "gvf", "pnr", "pfr", "sent", "sty_a", "sty_b", "rvra", "rvca", "rga", "rpa",
+              "rsent", "gd1", "l1n", "l1f", "rha"]
+
+
+def plan(T, topo):
+    cs = list(T.cores)
+    near, far, flows = {}, {}, []
+    for a, b in zip(cs, cs[1:]):
+        if b in topo.cores_of(a):
+            near[a], near[b] = b, a
+        else:
+            far[a], far[b] = b, a
+            flows += [(a, b), (b, a)]
+    out, over, used = {}, {}, set()
+    for s, d in flows:
+        for way, c in ((out, topo.cores_of(s)), (over, [x for x in range(SIM_CORES) if topo.mates(x, d)])):
+            pair = []
+            for e in (topo.die(s), 1 - topo.die(s)):
+                x = [x for x in c if T.rank_of(x) is None and x not in used and topo.die(x) == e
+                     and topo.may_write(x, d) and topo.may_write(s, x)][0]
+                used.add(x)
+                pair.append(x)
+            way[(s, d)] = pair
+    return near, far, out, over
+
+
+def bits(engines):
+    m = 0
+    for e in engines:
+        m |= 1 << e
+    return m
+
+
+def transfer(topo, src, dst, out, in_, engines, sem):
+    rid, pid = topo.addr(dst, src)
+    return RemoteDMATransfer(dst_ids=[DstId(rid=rid, pnc=pid)], dma_engine_mask=bits(engines), remote_sem=sem,
+                             src=in_, dst=out)
+
+
+def columns(way, i):
+    a = i * W_OVER if way == "over" else 2 * W_OVER + i * W_OUT
+    return a, a + (W_OVER if way == "over" else W_OUT)
+
+
+def split(topo, a, near, b):
+    leave = topo.engines(a, b)
+    return leave, [e for e in topo.engines(a, near) if e not in leave]
+
+
+def list_column(T, s, d):
+    return 128 if T.rank_of(s) > T.rank_of(d) else 0
+
+
+def rank_program(g, core, T, topo):
+    near, far, out, over = plan(T, topo)
+    sem = T.sem
+    if T.rank_of(core) is None:
+        for name, way in (("out", out), ("over", over)):
+            for (s, d), rel in way.items():
+                if core in rel:
+                    hand_on(g, core, T, topo, s, d, name, rel.index(core), near[s])
+        return
+    r = T.rank_of(core)
+    nb, fb = near[core], far.get(core)
+    up = T.rank_of(nb) > r
+    edge = fb is None
+    V, S, TE, SY = g.vector, g.scalar, g.tensor, g.sync
+    top = 8 * r
+    cnt = [0, 0]
+
+    def v(ins, name=None):
+        if name:
+            ins.then_inc(sem[name], 1)
+        else:
+            ins.then_inc(sem.vc, 1)
+            cnt[0] += 1
+
+    def vs():
+        if cnt[0] > cnt[1]:
+            V.wait_ge(sem.vc, cnt[0])
+            cnt[1] = cnt[0]
+
+    def ts(out, in0, s1, op0, s2=None, op1=None):
+        if op1 is None:
+            return V.tensor_scalar(out=out, in0=in0, scalar1=s1, scalar2=None, op0=op0)
+        return V.tensor_scalar(out=out, in0=in0, scalar1=s1, scalar2=s2, op0=op0, op1=op1)
+
+    def near_window(u):
+        return (11, 22) if u else (2, 13)
+
+    def far_window(u):
+        return (2, 16) if u else (9, 22)
+    lo_n = (8, 24) if up else (0, 16)
+    nr0 = (15, 22) if up else (2, 9)
+    nr1 = (15, 17) if up else (7, 9)
+    nra = (13, 15) if up else (9, 11)
+    nrb = (17, 20) if up else (4, 7)
+    nw1 = near_window(up)
+    if edge:
+        lo_f = (7, 16) if up else (8, 17)
+        fr0 = (8, 9) if up else (15, 16)
+        fr1 = (8, 13) if up else (11, 16)
+        hf = fr1
+        fw1 = (6, 15) if up else (9, 18)
+    else:
+        lo_f = (0, 16) if up else (8, 24)
+        fr0, fr0b = ((7, 9), (2, 7)) if up else ((15, 17), (17, 22))
+        fr1 = fr0
+        fra = (9, 11) if up else (13, 15)
+        hf = (4, 11) if up else (13, 20)
+        fw1 = far_window(up)
+
+    cut = 2 * W_OVER
+    SY.dma_start(out=T.vyi[:], in_=T.vy[:]).then_inc(sem.ldy, 16)
+    SY.dma_start(out=T.vxi[:], in_=T.vx[:]).then_inc(sem.ldx, 16)
+    SY.dma_start(out=T.pic[:, 1024:1024 + cut], in_=T.img[:, 0:cut]).then_inc(sem.ldi, 16)
+
+    g.iota(out=T.pidx[:], pattern=[[1, 1]], base=0, channel_multiplier=1).then_inc(sem.gi, 1)
+    g.iota(out=T.xiota[:], pattern=[[16, 4], [1, 16]], base=0, channel_multiplier=64).then_inc(sem.gi, 1)
+    v(V.memset(T.jb[:, 0:512], 0.0), "msj")
+    v(V.memset(T.sel[:], 128.0), "sb")
+    v(V.memset(T.w0[:, 1024:2048], 0.0), "ms")
+    S.wait_ge(sem.msj, 1)
+    S.dma_start(out=T.pic[:, 1024 + cut:2048], in_=T.img[:, cut:1024]).then_inc(sem.ldj, 16)
+    for c in (2048, 2560, 0, 512) if up else (0, 512, 2048, 2560):
+        S.activation(out=T.w0[:, c:c + 512], in_=T.jb[:, 0:512], func=F.Copy).then_inc(sem.msh, 1)
+    V.wait_ge(sem.gi, 2)
+    v(ts(T.hi[:], T.pidx[:], 1, A.arith_shift_right, 7, A.bitwise_and))
+    v(ts(T.oi[:], T.pidx[:], 4, A.arith_shift_right, 1, A.bitwise_and))
+    if edge:
+        v(ts(T.mi[:], T.pidx[:], 15, A.bitwise_and))
+    xi, t1 = T.bp[:, 0:4, :], T.bp[:, 4:8, :]
+    v(V.tensor_copy(out=xi, in_=T.xiota[:]))
+    vs()
+    v(ts(T.hrow[:], T.hi[:], float(8 * r + 8), A.add))
+    v(ts(T.h128[:], T.hi[:], 128.0, A.mult, float(128 * (8 * r + 8)), A.add))
+    v(ts(T.odd[:], T.oi[:], 1.0, A.mult))
+    v(ts(T.even[:], T.oi[:], -1.0, A.mult, 1.0, A.add))
+    vs()
+    g.wait_ge(sem.sb, 1)
+    pat = [[-16, 9], [1000, 16]]
+    g.affine_select(T.sel[:], T.sel[:], pat, A.is_equal, 0.0, -15000, 1).then_inc(sem.sel1, 1)
+    g.wait_ge(sem.sel1, 1)
+    g.affine_select(T.sel[:], T.sel[:], pat, A.not_equal, 1.0, -15001, 1).then_inc(sem.sel2, 1)
+
+    V.wait_ge(sem.ldy, 16)
+    v(ts(T.dig[:, 0:4, :], T.vyi[:], T.hrow[:, 0:1], A.add), "dgr")
+    V.wait_ge(sem.ldx, 16)
+    v(V.tensor_tensor(out=T.ci[:], in0=T.vxi[:], in1=xi, op=A.add))
+    vs()
+    v(ts(T.ci[:], T.ci[:], 127, A.bitwise_and))
+    v(ts(t1, T.vyi[:], 128.0, A.mult, T.h128[:, 0:1], A.add))
+    vs()
+    v(V.tensor_copy(out=T.dig[:, 4:8, :], in_=T.ci[:]), "dgc")
+    v(V.tensor_tensor(out=T.gg[:], in0=t1, in1=T.ci[:], op=A.add))
+    vs()
+    v(ts(T.blk[:, :, 0:16], T.gg[:], T.even[:, 0:1], A.mult))
+    v(ts(T.blk[:, :, 16:32], T.gg[:], T.odd[:, 0:1], A.mult))
+    vs()
+    for b in range(4):
+        v(V.transpose(out=T.tb[:, b:128:4], in_=T.blk[:, b, :]))
+    vs()
+    v(V.tensor_tensor(out=T.lf[:], in0=T.tb[:, 0:64], in1=T.tb[:, 64:128], op=A.add))
+    vs()
+    for lst, d in ((T.lsf, fb), (T.lsn, nb)):
+        if d is not None:
+            first = 8 * T.rank_of(d) + (8 if r > T.rank_of(d) else 0)
+            v(ts(lst[:], T.lf[:], -128.0 * first, A.add), "gd")
+    low = (lo_f if up else lo_n)[0]
+    v(ts(T.l0[:, 72:128], T.lf[:, 8:64], -128.0 * (top + 8), A.add), "lo")
+    v(ts(T.l0[:, 64:72], T.lf[:, 0:8], -128.0 * (top + low), A.add), "lo")
+    if edge:
+        for k in range(1, 5):
+            v(ts(T.kcol[:, k:k + 1], T.mi[:], 0.0, A.is_equal, float(-k if r == 0 else k), A.mult))
+        vs()
+
+    es = topo.engines(core, nb)
+    ref = core if not edge else nb
+    leave, stay = split(topo, ref, near[ref], over[(ref, far[ref])][0])
+    sent = [0]
+
+    def send(dst, to, src, engines, s):
+        rid, pid = topo.addr(dst, core)
+        g.remote_dma(to, src, s, sem.sent, pid, rid, bits(engines))
+        sent[0] += len(engines)
+
+    def fused(tr):
+        g.remote_dma_fused(tr, local_sem=sem.sent)
+        sent[0] += len(tr) * len(stay)
+
+    def image(dst, to, a, b, engines, s):
+        send(dst, to, T.pic[:, 1024 + a:1024 + b], engines, s)
+    g.wait_ge(sem.dgr, 1)
+    if not edge:
+        send(out[(core, fb)][0], T.rvr[:], T.dig[:, 0:4, :], leave, sem.rvra)
+    g.wait_ge(sem.dgc, 1)
+    if not edge:
+        send(out[(core, fb)][0], T.rvc[:], T.dig[:, 4:8, :], leave, sem.rvca)
+    fused([transfer(topo, core, nb, T.dnr[:], T.dig[:, 0:4, :], stay, sem.vn),
+           transfer(topo, core, nb, T.dnc[:], T.dig[:, 4:8, :], leave, sem.vn)])
+    lc = list_column(T, core, nb)
+
+    def lists(ready, name, here, there, at, a, b, relayed):
+        g.wait_ge(sem[ready], 1 if edge else 2)
+        tr = [transfer(topo, core, nb, at[:, a:b], here, stay, sem[name])]
+        if not edge:
+            tr.insert(0, transfer(topo, core, out[(core, fb)][0], relayed[0], there, leave, relayed[1]))
+        fused(tr)
+    lists("gd", "gvn", T.lsn[:], T.lsf[:], T.l0, lc, lc + 64, (T.rg[:], sem.rga))
+    to = 0 if up else 2048
+    g.wait_ge(sem.ldi, 16)
+    second = ("gd1", "l1n", T.ln1[:], T.lf1[:], T.l1, lc + 8, lc + 56, (T.rh[:], sem.rha))
+    if edge:
+        g.wait_ge(sem.ldj, 16)
+        g.wait_ge(sem.vn, len(es))
+        image(nb, T.pic[:, to:to + 1024], 0, 1024, es, sem.pnr)
+        lists(*second)
+    else:
+        ro, rw = out[(core, fb)], over[(core, fb)]
+        image(rw[0], T.rq[:], *columns("over", 0), leave, sem.rpa)
+        g.wait_ge(sem.ldj, 16)
+        image(ro[0], T.rp[:], *columns("out", 0), stay, sem.rpa)
+        g.wait_ge(sem.vn, len(es))
+        image(rw[1], T.rq[:], *columns("over", 1), leave, sem.rpa)
+        image(ro[1], T.rp[:], *columns("out", 1), stay, sem.rpa)
+        lists(*second)
+        g.wait_ge(sem.vfc, DIG_ENGINES)
+        image(nb, T.pic[:, to:to + cut], 0, cut, stay, sem.pnr)
+    pn_inc = len(es) if far.get(nb) is None else (1 + len(out[(nb, far[nb])])) * len(stay)
+
+    def spread(q, h, src, col, name):
+        q.dma_start(out=T.w0[h:128:16, col:col + 1024], in_=src).then_inc(sem[name], 16)
+    ncol, fcol = (2048, 0) if up else (0, 2048)
+    for h, q in enumerate((SY, S)):
+        q.wait_ge(sem.ms, 1)
+        q.wait_ge(sem.dgc if h else sem.dgr, 1)
+        spread(q, h, T.dig[:, 4 * h:4 * h + 4, :], 1024, "rs_o")
+    SY.wait_ge(sem.msh, 4)
+    SY.wait_ge(sem.vn, len(es))
+    spread(SY, 0, T.dnr[:], ncol, "rs_n")
+    spread(SY, 1, T.dnc[:], ncol, "rs_n")
+    if not edge:
+        SY.wait_ge(sem.vfr, DIG_ENGINES)
+        spread(SY, 0, T.dfr[:], fcol, "rs_f")
+        SY.wait_ge(sem.vfc, DIG_ENGINES)
+        spread(SY, 1, T.dfc[:], fcol, "rs_f")
+
+    def part(eng, out, W, lst, a, b, d, name):
+        o, i = out[:, 16 * (a - d):16 * (b - d)], W.indirect(lst[:, a:b])
+        if eng is V:
+            V.tensor_copy(out=o, in_=i).then_inc(sem[name], 1)
+        else:
+            S.activation(out=o, in_=i, func=F.Copy).then_inc(sem[name], 1)
+
+    def gather(out, win, w, lst, rows, name, o0=0):
+        a, b = 8 * rows[0], 8 * rows[1]
+        m = a + (b - a) // 4 * 2
+        part(V, out, win[:, 128 * w[0]:128 * w[1]], lst, a, m, 8 * o0, name)
+        part(S, out, win[:, 128 * w[0]:128 * w[1]], lst, m, b, 8 * o0, name)
+
+    def pick(ps, win, rows, name):
+        a, b = 128 * rows[0], 128 * rows[1]
+        k = (b - a) // 16
+        for q in range(16):
+            ins = TE.matmul(ps[:, 0:k], T.sel[:, 15 - q:143 - q], win[:, a + q:b:16], q == 0, q == 15)
+        ins.then_inc(sem[name], 1)
+
+    def both(name, k):
+        V.wait_ge(sem[name], k)
+        S.wait_ge(sem[name], k)
+
+    def listed(lst, rows, ps, base, waits, name):
+        V.wait_ge(sem[waits], 1)
+        v(ts(lst[:, 8 * rows[0]:8 * rows[1]], ps[:, 0:8 * (rows[1] - rows[0])], -128.0 * (top + base), A.add), name)
+
+    def beyond(win, ks, name):
+        for k in ks:
+            a, b = (8, 8 - k) if up else (15, 15 + k)
+            v(ts(win[:, 128 * b:128 * b + 128], win[:, 128 * a:128 * a + 128], T.kcol[:, k:k + 1], A.add), name)
+
+    V.wait_ge(sem.ms, 1)
+    both("msh", 4)
+    both("lo", 2)
+    both("rs_o", 32)
+    gather(T.w1, T.w0, (8, 16), T.l0, (9, 15), "g_e")
+    TE.wait_ge(sem.sel2, 1)
+    TE.wait_ge(sem.g_e, 2)
+    pick(T.po, T.w1, (9, 15), "t_o")
+    if edge:
+        beyond(T.w0, (1,), "vir0")
+        both("vir0", 1)
+        gather(T.w1, T.w0, lo_f, T.l0, fr0, "g_f")
+        TE.wait_ge(sem.g_f, 2)
+        pick(T.pf, T.w1, fr1, "t_f")
+        V.wait_ge(sem.g_f, 2)
+        beyond(T.w1, (1, 2), "vir1")
+    V.wait_ge(sem.t_o, 1)
+    for lst, d, window in ((T.lf1, fb, far_window), (T.ln1, nb, near_window)):
+        if d is not None:
+            first = 8 * T.rank_of(d) + window(T.rank_of(near[d]) > T.rank_of(d))[0]
+            v(ts(lst[:], T.po[:, 0:48], -128.0 * first, A.add), "gd1")
+    own = [(nra, nw1[0])] if edge else [((11, 13), 9), (nra, nw1[0]), (fra, fw1[0])]
+    for (a, b), base in own:
+        v(ts(T.l1[:, 8 * a:8 * b], T.po[:, 8 * (a - 9):8 * (b - 9)], -128.0 * (top + base), A.add), "c_o")
+    both("c_o", len(own))
+    both("g_e", 2)
+    if edge:
+        both("vir1", 2)
+        both("g_f", 2)
+        listed(T.l1, fr1 if up else (11, 13), T.pf, fw1[0], "t_f", "c_f") if False else None
+        V.wait_ge(sem.t_f, 1)
+        v(ts(T.l3[:, 8 * fr1[0]:8 * fr1[1]], T.pf[:, 0:40], -128.0 * (top + fw1[0]), A.add), "c_f")
+        both("c_f", 1)
+        gather(T.w2, T.w1, fw1, T.l3, fr1, "h_f")
+    else:
+        gather(T.w2, T.w1, (9, 15), T.l1, (11, 13), "h_o")
+
+    both("gvn", len(stay))
+    both("rs_n", 32)
+    gather(T.w1, T.w0, lo_n, T.l0, nr0, "g_n")
+    TE.wait_ge(sem.g_n, 2)
+    pick(T.pn, T.w1, nr1, "t_n")
+    er, fr = ((12, 20), (4, 12)) if up else ((4, 12), (12, 20))
+    ew = (8, 24) if up else (0, 16)
+    if edge:
+        V.wait_ge(sem.h_f, 2)
+        beyond(T.w2, (1, 2, 3, 4), "vir2")
+        TE.wait_ge(sem.h_f, 2)
+        TE.wait_ge(sem.vir2, 4)
+        both("ldi", 16)
+        both("ldj", 16)
+        a, b = (8, 0) if up else (15, 16)
+        for k in range(8):
+            v(V.tensor_copy(out=T.pic[:, 128 * (b + k):128 * (b + k) + 128], in_=T.pic[:, 128 * a:128 * a + 128]), "pv")
+    both("g_n", 2)
+    both("l1n", len(stay))
+    if edge:
+        gather(T.w2, T.w1, nw1, T.l1, nra, "h_m")
+        gather(T.w2, T.w1, nw1, T.l1, nrb, "h_m")
+        pick(T.p3, T.w2, fr, "t_3")
+    else:
+        gather(T.w2, T.w1, nw1, T.l1, nra, "h_m")
+        gather(T.w2, T.w1, nw1, T.l1, nrb, "h_m")
+        both("gvf", len(topo.engines(out[(fb, core)][0], core)))
+        both("rs_f", 32)
+        gather(T.w1, T.w0, lo_f, T.l0, fr0, "g_f")
+        TE.wait_ge(sem.g_f, 2)
+        pick(T.pf, T.w1, fr1, "t_f")
+    listed(T.l1, nr1, T.pn, nw1[0], "t_n", "c_n")
+    if not edge:
+        gather(T.w1, T.w0, lo_f, T.l0, fr0b, "g_f2")
+    both("c_n", 1)
+    gather(T.w2, T.w1, nw1, T.l1, nr1, "h_n")
+    if not edge:
+        listed(T.l1, fr1, T.pf, fw1[0], "t_f", "c_f")
+        both("c_f", 1)
+        both("g_f", 2)
+        both("g_f2", 2)
+        both("l1f", len(topo.engines(out[(fb, core)][0], core)))
+        gather(T.w2, T.w1, fw1, T.l1, hf, "h_f")
+
+    TE.wait_ge(sem.h_f if edge else sem.h_o, 2)
+    TE.wait_ge(sem.h_m, 4)
+    TE.wait_ge(sem.h_n, 2)
+    pick(T.p2, T.w2, er, "t_2")
+    if edge:
+        gw = (0, 16) if up else (8, 24)
+        listed(T.l2e, fr, T.p3, gw[0], "t_3", "c_3")
+        both("c_3", 1)
+        both("pv", 8)
+        gather(T.jb, T.pic, gw, T.l2e, fr, "g_j")
+        v(ts(T.l2[:, 8 * fr[0]:8 * fr[1]], T.p3[:, 0:64], -128.0 * top, A.add), "c_2b")
+    listed(T.l2e, er, T.p2, ew[0], "t_2", "c_2")
+    both("c_2", 1)
+    both("ldi", 16)
+    both("ldj", 16)
+    both("pnr", pn_inc)
+    gather(T.jb, T.pic, ew, T.l2e, er, "g_2")
+    if not edge:
+        TE.wait_ge(sem.h_f, 2)
+        pick(T.p3, T.w2, fr, "t_3")
+        listed(T.l2, fr, T.p3, 0, "t_3", "c_3")
+        both("c_3", 1)
+        both("pfr", sum(len(topo.engines(x, core)) for x in out[(fb, core)] + over[(fb, core)]))
+        gather(T.jb, T.pic, (0, 24), T.l2, fr, "g_j")
+    v(ts(T.l2[:, 8 * er[0]:8 * er[1]], T.p2[:, 0:64], -128.0 * top, A.add), "c_2b")
+    both("g_2", 2)
+    both("g_j", 2)
+    both("c_2b", 2 if edge else 1)
+    both("msj", 1)
+    gather(T.yo, T.jb, (0, 20), T.l2, (8, 12), "g_3a", 8)
+    gather(T.yo, T.jb, (0, 20), T.l2, (12, 16), "g_3b", 8)
+    SY.wait_ge(sem.g_3a, 2)
+    SY.dma_start(out=T.y[:, 0:512], in_=T.yo[:, 0:512]).then_inc(sem.sty_a, 16)
+    S.wait_ge(sem.g_3b, 2)
+    S.dma_start(out=T.y[:, 512:1024], in_=T.yo[:, 512:1024]).then_inc(sem.sty_b, 16)
+    g.wait_ge(sem.sent, sent[0])
+    g.wait_ge(sem.sty_a, 16)
+    g.wait_ge(sem.sty_b, 16)
+
+
+def hand_on(g, core, T, topo, s, d, way, i, nb):
+    sem = T.sem
+    m, ne = topo.mask(core, d), len(topo.engines(core, d))
+    es = topo.engines(s, core)
+    a, b = columns(way, i)
+
+    def pass_on(dst, to, held, arrived, mask):
+        rid, pid = topo.addr(dst, core)
+        g.remote_dma(to, held, arrived, sem.rsent, pid, rid, mask)
+
+    def image(dst, held, arrived, mask):
+        o = 0 if T.rank_of(dst) > T.rank_of(s) else 2048
+        pass_on(dst, T.pic[:, o + a:o + b], held, arrived, mask)
+    if way == "over":
+        g.wait_ge(sem.rpa, len(es))
+        image(d, T.rq[:], sem.pfr, m)
+        g.wait_ge(sem.rsent, ne)
+        return
+    leave, stay = split(topo, core, nb, d)
+    n = ne + len(stay)
+    half = len(es) // 2
+    lc = list_column(T, s, d)
+    if i == 0:
+        g.wait_ge(sem.rvra, half)
+        pass_on(d, T.dfr[:], T.rvr[:], sem.vfr, bits(leave[:DIG_ENGINES]))
+        g.wait_ge(sem.rvca, half)
+        pass_on(d, T.dfc[:], T.rvc[:], sem.vfc, bits(leave[:DIG_ENGINES]))
+        g.wait_ge(sem.rga, half)
+        pass_on(d, T.l0[:, lc:lc + 64], T.rg[:], sem.gvf, m)
+        n += 2 * DIG_ENGINES + 2 * ne
+    g.wait_ge(sem.rpa, half)
+    if i == 0:
+        image(d, T.rp[:], sem.pfr, m)
+    image(nb, T.rp[:], sem.pnr, bits(stay))
+    if i == 0:
+        g.wait_ge(sem.rha, half)
+        pass_on(d, T.l1[:, lc + 8:lc + 56], T.rh[:], sem.l1f, m)
+    else:
+        image(d, T.rp[:], sem.pfr, m)
+    g.wait_ge(sem.rsent, n)

@@ -3,35 +3,33 @@ from concourse.mybir import AluOpType as A, ActivationFunctionType as F
 
 BF, F32, I32, U16 = "bfloat16", "float32", "int32", "uint16"
 SIM_CORES = 256
-W_OUT, W_OVER = 320, 192
-DIG_ENGINES = 4
+EARLY = 64
+NEAR_FIRST = False
+G2_EARLY = False
 SCRATCH = {
-    "vyi": ("sbuf", [128, 4, 16], I32), "vxi": ("sbuf", [128, 4, 16], I32), "ci": ("sbuf", [128, 4, 16], I32),
-    "xiota": ("sbuf", [128, 4, 16], I32), "pidx": ("sbuf", [128, 1], I32), "hi": ("sbuf", [128, 1], I32),
-    "oi": ("sbuf", [128, 1], I32), "mi": ("sbuf", [128, 1], I32),
-    "hrow": ("sbuf", [128, 1], F32), "h128": ("sbuf", [128, 1], F32),
-    "odd": ("sbuf", [128, 1], F32), "even": ("sbuf", [128, 1], F32), "kcol": ("sbuf", [128, 8], F32),
-    "dig": ("sbuf", [128, 8, 16], BF),
-    "dnr": ("dram", [128, 4, 16], BF), "dnc": ("dram", [128, 4, 16], BF),
-    "dfr": ("dram", [128, 4, 16], BF), "dfc": ("dram", [128, 4, 16], BF),
-    "gg": ("sbuf", [128, 4, 16], F32), "blk": ("sbuf", [128, 4, 32], F32), "tb": ("sbuf", [128, 128], F32),
-    "lf": ("sbuf", [128, 64], F32), "lsn": ("sbuf", [128, 64], U16), "lsf": ("sbuf", [128, 64], U16),
-    "ln1": ("sbuf", [128, 48], U16), "lf1": ("sbuf", [128, 48], U16), "rh": ("sbuf", [128, 48], U16),
-    "l0": ("sbuf", [128, 192], U16), "l1": ("sbuf", [128, 192], U16), "l2": ("sbuf", [128, 192], U16),
-    "l2e": ("sbuf", [128, 192], U16), "l3": ("sbuf", [128, 192], U16),
-    "w0": ("sbuf", [128, 3072], BF), "w1": ("sbuf", [128, 3072], BF), "w2": ("sbuf", [128, 3072], BF),
-    "jb": ("sbuf", [128, 3072], BF), "pic": ("sbuf", [128, 3072], BF), "yo": ("sbuf", [128, 1024], BF),
-    "sel": ("sbuf", [128, 144], BF),
-    "rvr": ("dram", [128, 4, 16], BF), "rvc": ("dram", [128, 4, 16], BF), "rg": ("sbuf", [128, 64], U16),
-    "rp": ("sbuf", [128, W_OUT], BF), "rq": ("sbuf", [128, W_OVER], BF),
-    "bp": ("psum", [128, 32, 16], F32), "po": ("psum", [128, 512], F32), "pn": ("psum", [128, 512], F32),
-    "pf": ("psum", [128, 512], F32), "p2": ("psum", [128, 512], F32), "p3": ("psum", [128, 512], F32),
+    "vi": ("sbuf", [128, 8, 16], I32), "ci": ("sbuf", [128, 8, 16], I32), "dig": ("sbuf", [128, 8, 16], BF),
+    "ramp": ("sbuf", [128, 144], I32), "odd2": ("sbuf", [128, 1], I32), "bi": ("sbuf", [128, 4], I32),
+    "bf": ("sbuf", [128, 4], F32), "kcol": ("sbuf", [128, 4], F32), "zero": ("sbuf", [128, 512], BF),
+    "ste": ("sbuf", [128, 144], BF), "sto": ("sbuf", [128, 144], BF), "sel": ("sbuf", [128, 144], BF),
+    "spr": ("sbuf", [128, 144], BF), "wsf": ("sbuf", [128, 256], BF), "wsn": ("sbuf", [128, 384], BF),
+    "tb": ("sbuf", [128, 128], F32), "lf": ("sbuf", [128, 64], F32),
+    "s0n": ("sbuf", [128, 16], U16), "s0f": ("sbuf", [128, 16], U16), "s1": ("sbuf", [128, 24], U16),
+    "r0": ("sbuf", [128, 16], U16), "r1": ("sbuf", [128, 24], U16),
+    "l0": ("sbuf", [128, 192], U16), "l0b": ("sbuf", [128, 192], U16), "l1k": ("sbuf", [128, 192], U16),
+    "l1n": ("sbuf", [128, 192], U16), "l1f": ("sbuf", [128, 192], U16), "l2": ("sbuf", [128, 192], U16),
+    "w0": ("sbuf", [128, 3072], BF), "w1": ("sbuf", [128, 2, 3072], BF), "w2": ("sbuf", [128, 3072], BF),
+    "pic": ("sbuf", [128, 3072], BF), "k1": ("sbuf", [128, 3072], BF), "jb": ("sbuf", [128, 3072], BF),
+    "yo": ("sbuf", [128, 3072], BF), "rp": ("sbuf", [128, 256], BF), "rk": ("sbuf", [128, 256], BF),
+    "rw": ("sbuf", [128, 128], BF), "rv": ("sbuf", [128, 128], BF),
+    "xi": ("psum", [128, 32, 16], F32), "blk": ("psum", [128, 16, 32], F32), "po": ("psum", [128, 512], F32),
+    "pn": ("psum", [128, 16, 32], F32), "pf": ("psum", [128, 512], F32),
+    "psf": ("psum", [128, 32, 16], F32), "psn": ("psum", [128, 32, 16], F32),
 }
-SEMAPHORES = ["vc", "gi", "ldy", "ldx", "ldi", "ldj", "ms", "msh", "msj", "sb", "sel1", "sel2", "dgr", "dgc", "gd", "lo",
-              "pv", "rs_o", "rs_n", "rs_f", "g_e", "g_n", "g_f", "g_f2", "h_o", "h_m", "h_n", "h_f", "g_2", "g_j", "g_3a",
-              "g_3b", "t_o", "t_n", "t_f", "t_2", "t_3", "c_o", "c_n", "c_f", "c_2", "c_2b", "c_3", "vir0", "vir1", "vir2",
-              "vn", "vfr", "vfc", "gvn", "gvf", "pnr", "pfr", "sent", "sty_a", "sty_b", "rvra", "rvca", "rga", "rpa",
-              "rsent", "gd1", "l1n", "l1f", "rha"]
+SEMAPHORES = ["vc", "gi", "ldy", "ldx", "lda", "ldb", "lde", "ms", "fill", "fill2", "sel1", "sel2", "st", "sp", "dg", "t_b",
+              "t_sf", "t_sn", "c_sf", "c_sn", "s0", "lo", "lob", "rs_o", "g_o", "g_e", "g_n", "g_f", "g_q", "h_n", "h_e",
+              "h_q", "h_f", "h_8", "k_o", "k_a", "k_b", "j_n", "j_f", "y_a", "y_b", "t_o", "t_n", "t_f", "c_k", "c_s",
+              "c_o", "c_f", "c_d", "c_e", "vir0", "vir1", "pv", "w0n", "w0f", "w1f", "l0n", "l0f", "l1a", "pnr", "pfr",
+              "kfr", "jnr", "sent", "sty_a", "sty_b", "rea", "rwa", "rva", "r0a", "r1a", "rpa", "rka", "rsent"]
 
 
 def plan(T, topo):
@@ -43,17 +41,16 @@ def plan(T, topo):
         else:
             far[a], far[b] = b, a
             flows += [(a, b), (b, a)]
-    out, over, used = {}, {}, set()
+    relays, used = {}, set()
     for s, d in flows:
-        for way, c in ((out, topo.cores_of(s)), (over, [x for x in range(SIM_CORES) if topo.mates(x, d)])):
-            pair = []
-            for e in (topo.die(s), 1 - topo.die(s)):
-                x = [x for x in c if T.rank_of(x) is None and x not in used and topo.die(x) == e
-                     and topo.may_write(x, d) and topo.may_write(s, x)][0]
-                used.add(x)
-                pair.append(x)
-            way[(s, d)] = pair
-    return near, far, out, over
+        mate = [x for x in range(0, SIM_CORES, len(topo.cores_of(d))) if topo.mates(x, d)][0]
+        relays[(s, d)] = []
+        for c, e in ((s, topo.die(s)), (mate, topo.die(d))):
+            x = [x for x in topo.cores_of(c) if T.rank_of(x) is None and x not in used and topo.die(x) == e
+                 and topo.may_write(x, d) and topo.may_write(s, x)][0]
+            used.add(x)
+            relays[(s, d)].append(x)
+    return near, far, relays
 
 
 def bits(engines):
@@ -69,28 +66,29 @@ def transfer(topo, src, dst, out, in_, engines, sem):
                              src=in_, dst=out)
 
 
-def columns(way, i):
-    a = i * W_OVER if way == "over" else 2 * W_OVER + i * W_OUT
-    return a, a + (W_OVER if way == "over" else W_OUT)
+def turned(up, a, b):
+    return (a, b) if up else (24 - b, 24 - a)
 
 
-def split(topo, a, near, b):
-    leave = topo.engines(a, b)
-    return leave, [e for e in topo.engines(a, near) if e not in leave]
+def first_list(T, s, d):
+    if T.rank_of(s) > T.rank_of(d):
+        return T.l0[:, 128:144], 8, 8
+    return T.l0b[:, 48:64], 5, 14
 
 
-def list_column(T, s, d):
-    return 128 if T.rank_of(s) > T.rank_of(d) else 0
+def cols(t, a, b):
+    if isinstance(t, tuple):
+        return t[0][:, t[1], a + t[2]:b + t[2]]
+    return t[:, a:b]
 
 
 def rank_program(g, core, T, topo):
-    near, far, out, over = plan(T, topo)
+    near, far, relays = plan(T, topo)
     sem = T.sem
     if T.rank_of(core) is None:
-        for name, way in (("out", out), ("over", over)):
-            for (s, d), rel in way.items():
-                if core in rel:
-                    hand_on(g, core, T, topo, s, d, name, rel.index(core), near[s])
+        for (s, d), rel in relays.items():
+            if core in rel:
+                hand_on(g, core, T, topo, s, d, rel.index(core), T.rank_of(near[d]) > T.rank_of(d))
         return
     r = T.rank_of(core)
     nb, fb = near[core], far.get(core)
@@ -98,7 +96,15 @@ def rank_program(g, core, T, topo):
     edge = fb is None
     V, S, TE, SY = g.vector, g.scalar, g.tensor, g.sync
     top = 8 * r
+    w1 = (T.w1, 0, 0)
     cnt = [0, 0]
+
+    def R(a, b):
+        return turned(up, a, b)
+
+    def rows(t, a, b):
+        a, b = R(a, b)
+        return cols(t, 128 * a, 128 * b)
 
     def v(ins, name=None):
         if name:
@@ -117,98 +123,95 @@ def rank_program(g, core, T, topo):
             return V.tensor_scalar(out=out, in0=in0, scalar1=s1, scalar2=None, op0=op0)
         return V.tensor_scalar(out=out, in0=in0, scalar1=s1, scalar2=s2, op0=op0, op1=op1)
 
-    def near_window(u):
-        return (11, 22) if u else (2, 13)
+    S.dma_start(out=T.vi[64:128], in_=T.vx[:]).then_inc(sem.ldx, 16)
+    SY.dma_start(out=T.vi[0:64], in_=T.vy[:]).then_inc(sem.ldy, 16)
+    for (a, b), name in ((R(8, 12), "lda"), (R(12, 16), "ldb")):
+        SY.dma_start(out=T.pic[:, 128 * a:128 * b], in_=T.img[:, 128 * (a - 8):128 * (b - 8)]).then_inc(sem[name], 16)
 
-    def far_window(u):
-        return (2, 16) if u else (9, 22)
-    lo_n = (8, 24) if up else (0, 16)
-    nr0 = (15, 22) if up else (2, 9)
-    nr1 = (15, 17) if up else (7, 9)
-    nra = (13, 15) if up else (9, 11)
-    nrb = (17, 20) if up else (4, 7)
-    nw1 = near_window(up)
-    if edge:
-        lo_f = (7, 16) if up else (8, 17)
-        fr0 = (8, 9) if up else (15, 16)
-        fr1 = (8, 13) if up else (11, 16)
-        hf = fr1
-        fw1 = (6, 15) if up else (9, 18)
+    g.iota(out=T.odd2[:], pattern=[[1, 1]], base=1, channel_multiplier=2).then_inc(sem.gi, 1)
+    g.iota(out=T.ramp[:], pattern=[[1, 144]], base=0, channel_multiplier=0).then_inc(sem.gi, 1)
+    v(V.memset(T.zero[:], 0.0), "ms")
+    S.wait_ge(sem.ms, 1)
+    if up:
+        fills = [(w1, 8, 9)] + ([(T.w0, 5, 7), (T.jb, 0, 4)] if edge else [(T.w0, 5, 6), (T.pic, 2, 4), (w1, 2, 6)])
     else:
-        lo_f = (0, 16) if up else (8, 24)
-        fr0, fr0b = ((7, 9), (2, 7)) if up else ((15, 17), (17, 22))
-        fr1 = fr0
-        fra = (9, 11) if up else (13, 15)
-        hf = (4, 11) if up else (13, 20)
-        fw1 = far_window(up)
+        fills = [(w1, 5, 6)]
+    own = [(T.w0, 8, 12), (T.w0, 12, 16)]
 
-    cut = 2 * W_OVER
-    SY.dma_start(out=T.vyi[:], in_=T.vy[:]).then_inc(sem.ldy, 16)
-    SY.dma_start(out=T.vxi[:], in_=T.vx[:]).then_inc(sem.ldx, 16)
-    SY.dma_start(out=T.pic[:, 1024:1024 + cut], in_=T.img[:, 0:cut]).then_inc(sem.ldi, 16)
-
-    g.iota(out=T.pidx[:], pattern=[[1, 1]], base=0, channel_multiplier=1).then_inc(sem.gi, 1)
-    g.iota(out=T.xiota[:], pattern=[[16, 4], [1, 16]], base=0, channel_multiplier=64).then_inc(sem.gi, 1)
-    v(V.memset(T.jb[:, 0:512], 0.0), "msj")
-    v(V.memset(T.sel[:], 128.0), "sb")
-    v(V.memset(T.w0[:, 1024:2048], 0.0), "ms")
-    S.wait_ge(sem.msj, 1)
-    S.dma_start(out=T.pic[:, 1024 + cut:2048], in_=T.img[:, cut:1024]).then_inc(sem.ldj, 16)
-    for c in (2048, 2560, 0, 512) if up else (0, 512, 2048, 2560):
-        S.activation(out=T.w0[:, c:c + 512], in_=T.jb[:, 0:512], func=F.Copy).then_inc(sem.msh, 1)
-    V.wait_ge(sem.gi, 2)
-    v(ts(T.hi[:], T.pidx[:], 1, A.arith_shift_right, 7, A.bitwise_and))
-    v(ts(T.oi[:], T.pidx[:], 4, A.arith_shift_right, 1, A.bitwise_and))
-    if edge:
-        v(ts(T.mi[:], T.pidx[:], 15, A.bitwise_and))
-    xi, t1 = T.bp[:, 0:4, :], T.bp[:, 4:8, :]
-    v(V.tensor_copy(out=xi, in_=T.xiota[:]))
-    vs()
-    v(ts(T.hrow[:], T.hi[:], float(8 * r + 8), A.add))
-    v(ts(T.h128[:], T.hi[:], 128.0, A.mult, float(128 * (8 * r + 8)), A.add))
-    v(ts(T.odd[:], T.oi[:], 1.0, A.mult))
-    v(ts(T.even[:], T.oi[:], -1.0, A.mult, 1.0, A.add))
-    vs()
-    g.wait_ge(sem.sb, 1)
+    def fill(name, todo):
+        for t, a, b in todo:
+            S.activation(out=cols(t, 128 * a, 128 * b), in_=T.zero[:, 0:128 * (b - a)], func=F.Copy).then_inc(sem[name], 1)
+    fill("fill", own)
+    fill("fill2", fills)
+    g.wait_ge(sem.ms, 1)
     pat = [[-16, 9], [1000, 16]]
-    g.affine_select(T.sel[:], T.sel[:], pat, A.is_equal, 0.0, -15000, 1).then_inc(sem.sel1, 1)
+    g.affine_select(T.sel[:], T.zero[:, 0:144], pat, A.not_equal, 1.0, -15000, 1).then_inc(sem.sel1, 1)
     g.wait_ge(sem.sel1, 1)
     g.affine_select(T.sel[:], T.sel[:], pat, A.not_equal, 1.0, -15001, 1).then_inc(sem.sel2, 1)
+    V.wait_ge(sem.gi, 1)
+    v(ts(T.bi[:, 2:3], T.odd2[:], 1, A.arith_shift_right, 7, A.bitwise_and))
+    v(ts(T.bi[:, 0:1], T.odd2[:], 127, A.bitwise_and))
+    v(ts(T.bi[:, 1:2], T.odd2[:], 4, A.arith_shift_right, 1, A.bitwise_and))
+    if edge:
+        v(ts(T.bi[:, 3:4], T.odd2[:], 31, A.bitwise_and))
+    vs()
+    v(ts(T.bf[:, 2:3], T.bi[:, 2:3], float(top + 8), A.add))
+    v(V.tensor_copy(out=T.bf[:, 0:2], in_=T.bi[:, 0:2]))
+    V.wait_ge(sem.gi, 2)
+    v(V.tensor_copy(out=T.xi[64:128, 0:8, :], in_=T.ramp[64:128, 0:128]))
+    vs()
+    v(ts(T.ste[:], T.ramp[:], T.bf[:, 0:1], A.is_equal, T.bf[:, 1:2], A.is_gt), "st")
+    v(ts(T.sto[:], T.ramp[:], T.bf[:, 0:1], A.is_equal, T.bf[:, 1:2], A.mult), "st")
 
-    V.wait_ge(sem.ldy, 16)
-    v(ts(T.dig[:, 0:4, :], T.vyi[:], T.hrow[:, 0:1], A.add), "dgr")
     V.wait_ge(sem.ldx, 16)
-    v(V.tensor_tensor(out=T.ci[:], in0=T.vxi[:], in1=xi, op=A.add))
+    v(V.tensor_tensor(out=T.ci[64:128], in0=T.vi[64:128], in1=T.xi[64:128, 0:8, :], op=A.add))
+    V.wait_ge(sem.ldy, 16)
+    v(ts(T.dig[0:64], T.vi[0:64], T.bf[0:64, 2:3], A.add, 128.0, A.mult), "dg")
     vs()
-    v(ts(T.ci[:], T.ci[:], 127, A.bitwise_and))
-    v(ts(t1, T.vyi[:], 128.0, A.mult, T.h128[:, 0:1], A.add))
+    v(ts(T.ci[64:128], T.ci[64:128], 127, A.bitwise_and))
     vs()
-    v(V.tensor_copy(out=T.dig[:, 4:8, :], in_=T.ci[:]), "dgc")
-    v(V.tensor_tensor(out=T.gg[:], in0=t1, in1=T.ci[:], op=A.add))
-    vs()
-    v(ts(T.blk[:, :, 0:16], T.gg[:], T.even[:, 0:1], A.mult))
-    v(ts(T.blk[:, :, 16:32], T.gg[:], T.odd[:, 0:1], A.mult))
-    vs()
+    v(V.tensor_copy(out=T.dig[64:128], in_=T.ci[64:128]), "dg")
+    v(ts(T.spr[0:64, 0:142], T.ramp[0:64, 1:143], T.bf[0:64, 0:1], A.is_equal), "sp")
+    v(ts(T.spr[64:128, 0:142], T.ramp[64:128, 0:142], T.bf[64:128, 0:1], A.is_equal), "sp")
+    if edge:
+        for k in (1, 2):
+            v(ts(T.kcol[:, k:k + 1], T.bi[:, 3:4], 1.0, A.is_equal, float(-128 * k if up else 128 * k), A.mult))
+    TE.wait_ge(sem.st, 2)
+    TE.wait_ge(sem.dg, 2)
+    for par, st in enumerate((T.ste, T.sto)):
+        for hf in range(2):
+            ins = TE.matmul(T.blk[:, 0:4, 16 * par:16 * par + 16], st[:, 1 - hf:129 - hf], T.dig[:, 4 * hf:4 * hf + 4, :],
+                            hf == 0, hf == 1)
+    ins.then_inc(sem.t_b, 1)
+    TE.wait_ge(sem.sp, 2)
+    edges = [(R(13, 16), T.psn, T.wsn, "sn")]
+    if not edge:
+        edges.insert(1 if NEAR_FIRST else 0, (R(8, 10), T.psf, T.wsf, "sf"))
+    for (a, b), ps, ws, x in edges:
+        for i in range(a, b):
+            ins = TE.matmul(ps[:, 8 * (i - a):8 * (i - a) + 8, :], T.spr[:, 2 * (i - 8):2 * (i - 8) + 128], T.dig[:],
+                            True, True)
+        ins.then_inc(sem["t_" + x], 1)
+        S.wait_ge(sem["t_" + x], 1)
+        S.activation(out=ws[:], in_=ps[:, 0:8 * (b - a), :], func=F.Copy).then_inc(sem["c_" + x], 1)
+    V.wait_ge(sem.t_b, 1)
     for b in range(4):
         v(V.transpose(out=T.tb[:, b:128:4], in_=T.blk[:, b, :]))
     vs()
     v(V.tensor_tensor(out=T.lf[:], in0=T.tb[:, 0:64], in1=T.tb[:, 64:128], op=A.add))
     vs()
-    for lst, d in ((T.lsf, fb), (T.lsn, nb)):
+    for lst, d in ((T.s0f, fb), (T.s0n, nb)):
         if d is not None:
-            first = 8 * T.rank_of(d) + (8 if r > T.rank_of(d) else 0)
-            v(ts(lst[:], T.lf[:], -128.0 * first, A.add), "gd")
-    low = (lo_f if up else lo_n)[0]
+            _, base, a = first_list(T, core, d)
+            v(ts(lst[:], T.lf[:, 8 * (a - 8):8 * (a - 6)], -128.0 * (8 * T.rank_of(d) + base), A.add), "s0")
     v(ts(T.l0[:, 72:128], T.lf[:, 8:64], -128.0 * (top + 8), A.add), "lo")
-    v(ts(T.l0[:, 64:72], T.lf[:, 0:8], -128.0 * (top + low), A.add), "lo")
-    if edge:
-        for k in range(1, 5):
-            v(ts(T.kcol[:, k:k + 1], T.mi[:], 0.0, A.is_equal, float(-k if r == 0 else k), A.mult))
-        vs()
+    v(ts(T.l0b[:, 64:80], T.lf[:, 0:16], -128.0 * (top + 5), A.add), "lob")
 
     es = topo.engines(core, nb)
     ref = core if not edge else nb
-    leave, stay = split(topo, ref, near[ref], over[(ref, far[ref])][0])
+    leave = topo.engines(ref, relays[(ref, far[ref])][1])
+    stay = [e for e in es if e not in leave]
+    rel = None if edge else relays[(core, fb)]
     sent = [0]
 
     def send(dst, to, src, engines, s):
@@ -220,254 +223,258 @@ def rank_program(g, core, T, topo):
         g.remote_dma_fused(tr, local_sem=sem.sent)
         sent[0] += len(tr) * len(stay)
 
-    def image(dst, to, a, b, engines, s):
-        send(dst, to, T.pic[:, 1024 + a:1024 + b], engines, s)
-    g.wait_ge(sem.dgr, 1)
-    if not edge:
-        send(out[(core, fb)][0], T.rvr[:], T.dig[:, 0:4, :], leave, sem.rvra)
-    g.wait_ge(sem.dgc, 1)
-    if not edge:
-        send(out[(core, fb)][0], T.rvc[:], T.dig[:, 4:8, :], leave, sem.rvca)
-    fused([transfer(topo, core, nb, T.dnr[:], T.dig[:, 0:4, :], stay, sem.vn),
-           transfer(topo, core, nb, T.dnc[:], T.dig[:, 4:8, :], leave, sem.vn)])
-    lc = list_column(T, core, nb)
+    def there(t, d, a, b):
+        a, b = R(a, b)
+        o = 8 * (r - T.rank_of(d))
+        return t[:, 128 * (a + o):128 * (b + o)]
 
-    def lists(ready, name, here, there, at, a, b, relayed):
-        g.wait_ge(sem[ready], 1 if edge else 2)
-        tr = [transfer(topo, core, nb, at[:, a:b], here, stay, sem[name])]
-        if not edge:
-            tr.insert(0, transfer(topo, core, out[(core, fb)][0], relayed[0], there, leave, relayed[1]))
-        fused(tr)
-    lists("gd", "gvn", T.lsn[:], T.lsf[:], T.l0, lc, lc + 64, (T.rg[:], sem.rga))
-    to = 0 if up else 2048
-    g.wait_ge(sem.ldi, 16)
-    second = ("gd1", "l1n", T.ln1[:], T.lf1[:], T.l1, lc + 8, lc + 56, (T.rh[:], sem.rha))
-    if edge:
-        g.wait_ge(sem.ldj, 16)
-        g.wait_ge(sem.vn, len(es))
-        image(nb, T.pic[:, to:to + 1024], 0, 1024, es, sem.pnr)
-        lists(*second)
-    else:
-        ro, rw = out[(core, fb)], over[(core, fb)]
-        image(rw[0], T.rq[:], *columns("over", 0), leave, sem.rpa)
-        g.wait_ge(sem.ldj, 16)
-        image(ro[0], T.rp[:], *columns("out", 0), stay, sem.rpa)
-        g.wait_ge(sem.vn, len(es))
-        image(rw[1], T.rq[:], *columns("over", 1), leave, sem.rpa)
-        image(ro[1], T.rp[:], *columns("out", 1), stay, sem.rpa)
-        lists(*second)
-        g.wait_ge(sem.vfc, DIG_ENGINES)
-        image(nb, T.pic[:, to:to + cut], 0, cut, stay, sem.pnr)
-    pn_inc = len(es) if far.get(nb) is None else (1 + len(out[(nb, far[nb])])) * len(stay)
-
-    def spread(q, h, src, col, name):
-        q.dma_start(out=T.w0[h:128:16, col:col + 1024], in_=src).then_inc(sem[name], 16)
-    ncol, fcol = (2048, 0) if up else (0, 2048)
-    for h, q in enumerate((SY, S)):
-        q.wait_ge(sem.ms, 1)
-        q.wait_ge(sem.dgc if h else sem.dgr, 1)
-        spread(q, h, T.dig[:, 4 * h:4 * h + 4, :], 1024, "rs_o")
-    SY.wait_ge(sem.msh, 4)
-    SY.wait_ge(sem.vn, len(es))
-    spread(SY, 0, T.dnr[:], ncol, "rs_n")
-    spread(SY, 1, T.dnc[:], ncol, "rs_n")
+    def halves(t, c, n, a, b, held, arrived):
+        fused([transfer(topo, core, rel[1], held[:, a:b], t[:, c + a:c + b], leave, arrived),
+               transfer(topo, core, rel[0], held[:, a:b], t[:, c + n + a:c + n + b], stay, arrived)])
+    pf0 = 128 * R(8, 12)[0]
+    if EARLY and not edge:
+        g.wait_ge(sem.lda, 16)
+        halves(T.pic, pf0, 256, 0, EARLY, T.rp, sem.rea)
+    for _, _, ws, x in edges:
+        g.wait_ge(sem["c_" + x], 1)
+        if x == "sf":
+            halves(ws, 0, 128, 0, 128, T.rw, sem.rwa)
+        else:
+            send(nb, there(T.w0, nb, 13, 16), ws[:], es, sem.w0n)
+    g.wait_ge(sem.s0, 1 if edge else 2)
+    tr = [transfer(topo, core, nb, first_list(T, core, nb)[0], T.s0n[:], leave, sem.l0n)]
     if not edge:
-        SY.wait_ge(sem.vfr, DIG_ENGINES)
-        spread(SY, 0, T.dfr[:], fcol, "rs_f")
-        SY.wait_ge(sem.vfc, DIG_ENGINES)
-        spread(SY, 1, T.dfc[:], fcol, "rs_f")
+        tr.insert(0, transfer(topo, core, rel[0], T.r0[:], T.s0f[:], stay, sem.r0a))
+    fused(tr)
+    if not edge:
+        g.wait_ge(sem.lda, 16)
+        halves(T.pic, pf0, 256, EARLY, 256, T.rp, sem.rpa)
+        g.wait_ge(sem.g_o, 2)
+        send(rel[0], T.rv[:], rows(w1, 9, 10), stay, sem.rva)
+    g.wait_ge(sem.ldb, 16)
+    send(nb, there(T.pic, nb, 12, 16), rows(T.pic, 12, 16), es, sem.pnr)
+    if not edge:
+        g.wait_ge(sem.c_s, 1)
+        send(rel[0], T.r1[:], T.s1[:], stay, sem.r1a)
+        g.wait_ge(sem.k_o, 2)
+        halves(T.k1, 128 * 10, 256, 0, 256, T.rk, sem.rka)
+    g.wait_ge(sem.j_n, 2)
+    send(nb, there(T.jb, nb, 12, 16), rows(T.jb, 12, 16), es, sem.jnr)
 
-    def part(eng, out, W, lst, a, b, d, name):
-        o, i = out[:, 16 * (a - d):16 * (b - d)], W.indirect(lst[:, a:b])
+    SY.wait_ge(sem.fill, 2)
+    SY.wait_ge(sem.dg, 2)
+    for h in range(2):
+        SY.dma_start(out=T.w0[h:128:16, 1024:2048], in_=T.dig[64 * h:64 * h + 64]).then_inc(sem.rs_o, 16)
+
+    def part(eng, out, W, lst, a, b, name):
+        o, i = cols(out, 16 * a, 16 * b), W.indirect(lst[:, a:b])
         if eng is V:
             V.tensor_copy(out=o, in_=i).then_inc(sem[name], 1)
         else:
             S.activation(out=o, in_=i, func=F.Copy).then_inc(sem[name], 1)
 
-    def gather(out, win, w, lst, rows, name, o0=0):
-        a, b = 8 * rows[0], 8 * rows[1]
-        m = a + (b - a) // 4 * 2
-        part(V, out, win[:, 128 * w[0]:128 * w[1]], lst, a, m, 8 * o0, name)
-        part(S, out, win[:, 128 * w[0]:128 * w[1]], lst, m, b, 8 * o0, name)
+    def gather(out, win, w, lst, rr, name, less=0):
+        a, b = 8 * rr[0], 8 * rr[1]
+        m = a + (b - a) // 4 * 2 - less
+        part(V, out, cols(win, 128 * w[0], 128 * w[1]), lst, a, m, name)
+        part(S, out, cols(win, 128 * w[0], 128 * w[1]), lst, m, b, name)
 
-    def pick(ps, win, rows, name):
-        a, b = 128 * rows[0], 128 * rows[1]
-        k = (b - a) // 16
+    def one(eng, out, win, w, lst, row, name):
+        a = 8 * R(row, row + 1)[0]
+        part(eng, out, cols(win, 128 * w[0], 128 * w[1]), lst, a, a + 8, name)
+
+    def pick(ps, moving, name):
         for q in range(16):
-            ins = TE.matmul(ps[:, 0:k], T.sel[:, 15 - q:143 - q], win[:, a + q:b:16], q == 0, q == 15)
+            ins = TE.matmul(ps, T.sel[:, 15 - q:143 - q], moving(q), q == 0, q == 15)
         ins.then_inc(sem[name], 1)
 
     def both(name, k):
         V.wait_ge(sem[name], k)
         S.wait_ge(sem[name], k)
 
-    def listed(lst, rows, ps, base, waits, name):
-        V.wait_ge(sem[waits], 1)
-        v(ts(lst[:, 8 * rows[0]:8 * rows[1]], ps[:, 0:8 * (rows[1] - rows[0])], -128.0 * (top + base), A.add), name)
+    def listed(lst, rr, ps, first, base, name, at=None):
+        at = rr[0] if at is None else at
+        v(ts(lst[:, 8 * at:8 * (at + rr[1] - rr[0])], cols(ps, 8 * (rr[0] - first), 8 * (rr[1] - first)), -128.0 * base,
+             A.add), name)
 
-    def beyond(win, ks, name):
-        for k in ks:
-            a, b = (8, 8 - k) if up else (15, 15 + k)
-            v(ts(win[:, 128 * b:128 * b + 128], win[:, 128 * a:128 * a + 128], T.kcol[:, k:k + 1], A.add), name)
+    def side(high, n):
+        return (T.l0, (8, 16 + n)) if high else (T.l0b, (5, 10))
 
-    V.wait_ge(sem.ms, 1)
-    both("msh", 4)
-    both("lo", 2)
+    def beyond(win, k, name):
+        v(ts(rows(win, 8 - k, 9 - k), rows(win, 8, 9), T.kcol[:, k:k + 1], A.add), name)
+
+    def near_side(stage):
+        l0, w = side(up, 3)
+        if stage == 0:
+            both("l0n", len(leave))
+            both("w0n", len(es))
+            gather(w1, T.w0, w, l0, R(15, 18), "g_n")
+        else:
+            both("g_n", 2)
+            both("g_o", 2)
+            gather(T.w0, w1, (8, 18) if up else (5, 11), l0, R(14, 17), "g_q")
+
+    both("lo", 1)
     both("rs_o", 32)
-    gather(T.w1, T.w0, (8, 16), T.l0, (9, 15), "g_e")
+    gather(w1, T.w0, (8, 16), T.l0, (9, 15), "g_o")
+    both("fill2", len(fills))
+    both("lob", 1)
     TE.wait_ge(sem.sel2, 1)
-    TE.wait_ge(sem.g_e, 2)
-    pick(T.po, T.w1, (9, 15), "t_o")
+    TE.wait_ge(sem.g_o, 2)
+    ro = R(8, 15) if edge else (9, 15)
+    fw = R(6, 14) if edge else R(2, 14)
+    nw = (8, 17) if up else (7, 14)
     if edge:
-        beyond(T.w0, (1,), "vir0")
+        vs()
+        beyond(T.w0, 1, "vir0")
         both("vir0", 1)
-        gather(T.w1, T.w0, lo_f, T.l0, fr0, "g_f")
-        TE.wait_ge(sem.g_f, 2)
-        pick(T.pf, T.w1, fr1, "t_f")
-        V.wait_ge(sem.g_f, 2)
-        beyond(T.w1, (1, 2), "vir1")
-    V.wait_ge(sem.t_o, 1)
-    for lst, d, window in ((T.lf1, fb, far_window), (T.ln1, nb, near_window)):
-        if d is not None:
-            first = 8 * T.rank_of(d) + window(T.rank_of(near[d]) > T.rank_of(d))[0]
-            v(ts(lst[:], T.po[:, 0:48], -128.0 * first, A.add), "gd1")
-    own = [(nra, nw1[0])] if edge else [((11, 13), 9), (nra, nw1[0]), (fra, fw1[0])]
-    for (a, b), base in own:
-        v(ts(T.l1[:, 8 * a:8 * b], T.po[:, 8 * (a - 9):8 * (b - 9)], -128.0 * (top + base), A.add), "c_o")
-    both("c_o", len(own))
-    both("g_e", 2)
+        gather(w1, T.w0, (5, 10) if up else (8, 17), T.l0b if up else T.l0, R(8, 9), "g_e")
+        TE.wait_ge(sem.g_e, 2)
+    pick(T.po[:, 0:8 * (ro[1] - ro[0])], lambda q: T.w1[:, 0, 128 * ro[0] + q:128 * ro[1]:16], "t_o")
     if edge:
-        both("vir1", 2)
-        both("g_f", 2)
-        listed(T.l1, fr1 if up else (11, 13), T.pf, fw1[0], "t_f", "c_f") if False else None
-        V.wait_ge(sem.t_f, 1)
-        v(ts(T.l3[:, 8 * fr1[0]:8 * fr1[1]], T.pf[:, 0:40], -128.0 * (top + fw1[0]), A.add), "c_f")
-        both("c_f", 1)
-        gather(T.w2, T.w1, fw1, T.l3, fr1, "h_f")
-    else:
-        gather(T.w2, T.w1, (9, 15), T.l1, (11, 13), "h_o")
-
-    both("gvn", len(stay))
-    both("rs_n", 32)
-    gather(T.w1, T.w0, lo_n, T.l0, nr0, "g_n")
-    TE.wait_ge(sem.g_n, 2)
-    pick(T.pn, T.w1, nr1, "t_n")
-    er, fr = ((12, 20), (4, 12)) if up else ((4, 12), (12, 20))
-    ew = (8, 24) if up else (0, 16)
-    if edge:
-        V.wait_ge(sem.h_f, 2)
-        beyond(T.w2, (1, 2, 3, 4), "vir2")
-        TE.wait_ge(sem.h_f, 2)
-        TE.wait_ge(sem.vir2, 4)
-        both("ldi", 16)
-        both("ldj", 16)
-        a, b = (8, 0) if up else (15, 16)
+        V.wait_ge(sem.g_e, 2)
+        beyond(w1, 1, "vir1")
+        beyond(w1, 2, "vir1")
+        both("lda", 16)
         for k in range(8):
-            v(V.tensor_copy(out=T.pic[:, 128 * (b + k):128 * (b + k) + 128], in_=T.pic[:, 128 * a:128 * a + 128]), "pv")
-    both("g_n", 2)
-    both("l1n", len(stay))
+            o, i = rows(T.pic, k, k + 1), rows(T.pic, 8, 9)
+            if k % 2:
+                v(V.tensor_copy(out=o, in_=i), "pv")
+            else:
+                S.activation(out=o, in_=i, func=F.Copy).then_inc(sem.pv, 1)
+        S.wait_ge(sem.g_e, 2)
+    if G2_EARLY:
+        near_side(0)
+    V.wait_ge(sem.t_o, 1)
     if edge:
-        gather(T.w2, T.w1, nw1, T.l1, nra, "h_m")
-        gather(T.w2, T.w1, nw1, T.l1, nrb, "h_m")
-        pick(T.p3, T.w2, fr, "t_3")
+        listed(T.l1f, R(8, 12), T.po, ro[0], top + fw[0], "c_o")
+        listed(T.l1n, R(12, 15), T.po, ro[0], top + nw[0], "c_o")
+        both("c_o", 2)
+        both("vir1", 2)
+        both("g_o", 2)
+        gather(T.w2, w1, fw, T.l1f, R(8, 12), "h_e")
+        n_o = 2
     else:
-        gather(T.w2, T.w1, nw1, T.l1, nra, "h_m")
-        gather(T.w2, T.w1, nw1, T.l1, nrb, "h_m")
-        both("gvf", len(topo.engines(out[(fb, core)][0], core)))
-        both("rs_f", 32)
-        gather(T.w1, T.w0, lo_f, T.l0, fr0, "g_f")
-        TE.wait_ge(sem.g_f, 2)
-        pick(T.pf, T.w1, fr1, "t_f")
-    listed(T.l1, nr1, T.pn, nw1[0], "t_n", "c_n")
-    if not edge:
-        gather(T.w1, T.w0, lo_f, T.l0, fr0b, "g_f2")
-    both("c_n", 1)
-    gather(T.w2, T.w1, nw1, T.l1, nr1, "h_n")
-    if not edge:
-        listed(T.l1, fr1, T.pf, fw1[0], "t_f", "c_f")
-        both("c_f", 1)
-        both("g_f", 2)
-        both("g_f2", 2)
-        both("l1f", len(topo.engines(out[(fb, core)][0], core)))
-        gather(T.w2, T.w1, fw1, T.l1, hf, "h_f")
-
-    TE.wait_ge(sem.h_f if edge else sem.h_o, 2)
-    TE.wait_ge(sem.h_m, 4)
+        l1k = T.l1n if up else T.l1k
+        listed(l1k, (10, 15) if up else (10, 14), T.po, 9, top + 8, "c_k")
+        listed(T.s1, R(9, 12), T.po, 9, 8 * T.rank_of(fb) + turned(not up, 2, 14)[0], "c_s", 0)
+        both("c_k", 1)
+        both("lda", 16)
+        both("ldb", 16)
+        gather(T.k1, T.pic, (8, 16), l1k, (10, 14), "k_o", less=2)
+        listed(T.l1f, R(9, 12), T.po, 9, top + fw[0], "c_o")
+        n_o = 1
+        if not up:
+            listed(T.l1n, R(12, 15), T.po, 9, top + nw[0], "c_o")
+            n_o = 2
+    if not G2_EARLY:
+        near_side(0)
+    near_side(1)
+    wn = T.w2 if edge else (T.w1, 1, -640 if up else 640)
+    both("c_o", n_o)
+    gather(wn, w1, nw, T.l1n, R(12, 15), "h_n")
+    both("g_q", 2)
+    gather(wn, T.w0, (8, 17) if up else (5, 10), side(up, 3)[0], R(15, 16), "h_q")
     TE.wait_ge(sem.h_n, 2)
-    pick(T.p2, T.w2, er, "t_2")
+    TE.wait_ge(sem.h_q, 2)
+    dw, ew = R(8, 20), R(0 if edge else 4, 16)
+
+    def shared(less):
+        both("c_d", 1)
+        both("lda", 16)
+        both("ldb", 16)
+        both("pnr", len(es))
+        gather(T.jb, T.pic, dw, T.l2, R(12, 16), "j_n", less)
     if edge:
-        gw = (0, 16) if up else (8, 24)
-        listed(T.l2e, fr, T.p3, gw[0], "t_3", "c_3")
-        both("c_3", 1)
+        TE.wait_ge(sem.h_e, 2)
+        pick(T.pf[:, 0:64], lambda q: T.w2[:, 1024 + q:2048:16], "t_n")
+        V.wait_ge(sem.t_n, 1)
+        listed(T.l2, R(12, 16), T.pf, 8, top + dw[0], "c_d")
+        shared(10)
+        listed(T.l2, R(8, 12), T.pf, 8, top + ew[0], "c_e")
+        for k in range(1, 5):
+            listed(T.l2, R(8, 9), T.pf, 8, top + ew[0] + (k if up else -k), "c_e", R(8 - k, 9 - k)[0])
+        both("c_e", 5)
         both("pv", 8)
-        gather(T.jb, T.pic, gw, T.l2e, fr, "g_j")
-        v(ts(T.l2[:, 8 * fr[0]:8 * fr[1]], T.p3[:, 0:64], -128.0 * top, A.add), "c_2b")
-    listed(T.l2e, er, T.p2, ew[0], "t_2", "c_2")
-    both("c_2", 1)
-    both("ldi", 16)
-    both("ldj", 16)
-    both("pnr", pn_inc)
-    gather(T.jb, T.pic, ew, T.l2e, er, "g_2")
-    if not edge:
-        TE.wait_ge(sem.h_f, 2)
-        pick(T.p3, T.w2, fr, "t_3")
-        listed(T.l2, fr, T.p3, 0, "t_3", "c_3")
-        both("c_3", 1)
-        both("pfr", sum(len(topo.engines(x, core)) for x in out[(fb, core)] + over[(fb, core)]))
-        gather(T.jb, T.pic, (0, 24), T.l2, fr, "g_j")
-    v(ts(T.l2[:, 8 * er[0]:8 * er[1]], T.p2[:, 0:64], -128.0 * top, A.add), "c_2b")
-    both("g_2", 2)
-    both("g_j", 2)
-    both("c_2b", 2 if edge else 1)
-    both("msj", 1)
-    gather(T.yo, T.jb, (0, 20), T.l2, (8, 12), "g_3a", 8)
-    gather(T.yo, T.jb, (0, 20), T.l2, (12, 16), "g_3b", 8)
-    SY.wait_ge(sem.g_3a, 2)
-    SY.dma_start(out=T.y[:, 0:512], in_=T.yo[:, 0:512]).then_inc(sem.sty_a, 16)
-    S.wait_ge(sem.g_3b, 2)
-    S.dma_start(out=T.y[:, 512:1024], in_=T.yo[:, 512:1024]).then_inc(sem.sty_b, 16)
-    g.wait_ge(sem.sent, sent[0])
-    g.wait_ge(sem.sty_a, 16)
-    g.wait_ge(sem.sty_b, 16)
-
-
-def hand_on(g, core, T, topo, s, d, way, i, nb):
-    sem = T.sem
-    m, ne = topo.mask(core, d), len(topo.engines(core, d))
-    es = topo.engines(s, core)
-    a, b = columns(way, i)
-
-    def pass_on(dst, to, held, arrived, mask):
-        rid, pid = topo.addr(dst, core)
-        g.remote_dma(to, held, arrived, sem.rsent, pid, rid, mask)
-
-    def image(dst, held, arrived, mask):
-        o = 0 if T.rank_of(dst) > T.rank_of(s) else 2048
-        pass_on(dst, T.pic[:, o + a:o + b], held, arrived, mask)
-    if way == "over":
-        g.wait_ge(sem.rpa, len(es))
-        image(d, T.rq[:], sem.pfr, m)
-        g.wait_ge(sem.rsent, ne)
-        return
-    leave, stay = split(topo, core, nb, d)
-    n = ne + len(stay)
-    half = len(es) // 2
-    lc = list_column(T, s, d)
-    if i == 0:
-        g.wait_ge(sem.rvra, half)
-        pass_on(d, T.dfr[:], T.rvr[:], sem.vfr, bits(leave[:DIG_ENGINES]))
-        g.wait_ge(sem.rvca, half)
-        pass_on(d, T.dfc[:], T.rvc[:], sem.vfc, bits(leave[:DIG_ENGINES]))
-        g.wait_ge(sem.rga, half)
-        pass_on(d, T.l0[:, lc:lc + 64], T.rg[:], sem.gvf, m)
-        n += 2 * DIG_ENGINES + 2 * ne
-    g.wait_ge(sem.rpa, half)
-    if i == 0:
-        image(d, T.rp[:], sem.pfr, m)
-    image(nb, T.rp[:], sem.pnr, bits(stay))
-    if i == 0:
-        g.wait_ge(sem.rha, half)
-        pass_on(d, T.l1[:, lc + 8:lc + 56], T.rh[:], sem.l1f, m)
+        gather(T.jb, T.pic, ew, T.l2, R(4, 12), "j_f")
     else:
-        image(d, T.rp[:], sem.pfr, m)
+        l0, w = side(not up, 2)
+        relayed = len(topo.engines(relays[(fb, core)][0], core))
+        both("l0f", relayed)
+        both("w0f", 2 * relayed)
+        both("h_n", 2)
+        gather(w1, T.w0, w, l0, R(7, 9), "g_f")
+        TE.wait_ge(sem.g_f, 2)
+        rn = R(7, 11)
+        pick(T.pn[:, 0:2, :], lambda q: T.w1[:, 0:2, 128 * rn[0] + q:128 * rn[1]:16], "t_n")
+        both("g_f", 2)
+        both("w1f", relayed)
+        hw, iw = (fw, fw) if up else (R(6, 14), R(4, 14))
+        gather(T.w2, w1, hw, T.l1f, R(9, 12), "h_f")
+        both("pfr", (4 if EARLY else 2) * relayed)
+        one(V, T.k1, T.pic, iw, T.l1f, 9, "k_a")
+        S.wait_ge(sem.l1a, relayed)
+        one(S, T.k1, T.pic, iw, T.l1f, 6, "k_a")
+        V.wait_ge(sem.t_n, 1)
+        listed(T.l1f, R(7, 9), (T.pn, 0, 0), rn[0], top + fw[0], "c_f")
+        listed(T.l2, R(12, 16), (T.pn, 1, 0), R(12, 16)[0], top + dw[0], "c_d")
+        S.wait_ge(sem.c_f, 1)
+        one(S, T.w2, w1, hw, T.l1f, 8, "h_8")
+        TE.wait_ge(sem.h_f, 2)
+        TE.wait_ge(sem.h_8, 1)
+        re_ = R(8, 12)
+        pick(T.pf[:, 0:32], lambda q: T.w2[:, 128 * re_[0] + q:128 * re_[1]:16], "t_f")
+        shared(-2)
+        V.wait_ge(sem.c_f, 1)
+        gather(T.k1, T.pic, iw, T.l1f, R(7, 9), "k_b")
+        both("k_o", 2)
+        both("k_a", 2)
+        both("k_b", 2)
+        both("kfr", 2 * relayed)
+        V.wait_ge(sem.l1a, relayed)
+        gather(T.jb, T.k1, fw, T.l1f, R(4, 12), "j_f", less=2)
+        V.wait_ge(sem.t_f, 1)
+        listed(T.l2, re_, T.pf, re_[0], top + ew[0], "c_e")
+        both("c_e", 1)
+    both("j_f", 2)
+    both("j_n", 2)
+    pieces = ((R(8, 12), ew if up else R(4, 16), "a"), (R(12, 16), dw, "b"))
+    for rr, w, x in pieces:
+        if x == "b":
+            both("jnr", len(es))
+        gather(T.yo, T.jb, w, T.l2, rr, "y_" + x)
+    for rr, w, x in pieces:
+        SY.wait_ge(sem["y_" + x], 2)
+        SY.dma_start(out=T.y[:, 128 * (rr[0] - 8):128 * (rr[1] - 8)], in_=T.yo[:, 128 * rr[0]:128 * rr[1]]).then_inc(
+            sem["sty_" + x], 16)
+    g.wait_ge(sem.sent, sent[0])
+    for rr, w, x in pieces:
+        g.wait_ge(sem["sty_" + x], 16)
+
+
+def hand_on(g, core, T, topo, s, d, i, up):
+    sem = T.sem
+    es = topo.engines(core, d)
+    rid, pid = topo.addr(d, core)
+
+    def half(t, a, b, lo=0, hi=None):
+        a, b = turned(up, a, b)
+        n = 64 * (b - a)
+        c = 128 * a + n * (1 - i)
+        return t[:, c + lo:c + (n if hi is None else hi)]
+    a, b = turned(up, 4, 7)
+    c = 128 * turned(up, 6, 7)[0]
+    jobs = [("rea", half(T.pic, 4, 8, 0, EARLY), T.rp[:, 0:EARLY], sem.pfr)] if EARLY else []
+    jobs += [("rwa", half(T.w0, 6, 8), T.rw[:], sem.w0f),
+             ("r0a", first_list(T, s, d)[0], T.r0[:], sem.l0f),
+             ("rpa", half(T.pic, 4, 8, EARLY), T.rp[:, EARLY:256], sem.pfr),
+             ("rva", T.w1[:, 0, c:c + 128], T.rv[:], sem.w1f),
+             ("r1a", T.l1f[:, 8 * a:8 * b], T.r1[:], sem.l1a),
+             ("rka", half(T.k1, 2, 6), T.rk[:], sem.kfr)]
+    n = 0
+    for came, to, held, arrived in jobs:
+        if i == 0 or came in ("rea", "rwa", "rpa", "rka"):
+            g.wait_ge(sem[came], len(es))
+            g.remote_dma(to, held, arrived, sem.rsent, pid, rid, bits(es))
+            n += len(es)
     g.wait_ge(sem.rsent, n)

@@ -4,32 +4,47 @@ from concourse.mybir import AluOpType as A, ActivationFunctionType as F
 BF, F32, I32, U16 = "bfloat16", "float32", "int32", "uint16"
 SIM_CORES = 256
 EARLY = 64
-NEAR_FIRST = False
-G2_EARLY = False
+OWN_LOAD = True
+I_FIRST = 1
+K_SHADOW = True
+H_FIRST = False
+FAR3 = False
+FARI = True
+SPLIT = True
+STAGE = True
+LOADS = "Sx Yy Se Ya Yb Ys"
+Y_B_FIRST = False
+STEPS = ["i_f", "c_m", "k_b", "c_d", "h_f", "k_1", "j_n", "j_o", "j_f", "c_e", "y_b"]
+ORDER = ["early", "w0n", "w0f", "s0", "img", "rv", "w1n", "k1", "s1", "imgn", "jb"]
+WAYS = {"early": "1L 0S", "w0f": "1L 0S", "s0": "0A", "img": "1L 0S", "rv": "0A", "s1": "0A", "k1": "1L 0S"}
+MORE = {"g_o": 0, "i_o": 0, "k_o": 0, "h_n": 0, "h_f": 0, "k_b": 0, "j_n": 0, "j_f": 0}
+HELD = {"early": 0, "w0f": 128, "img": 512, "rv": 1024, "k1": 1152, "s0": 0, "s1": 32}
 SCRATCH = {
-    "vi": ("sbuf", [128, 8, 16], I32), "ci": ("sbuf", [128, 8, 16], I32), "dig": ("sbuf", [128, 8, 16], BF),
-    "ramp": ("sbuf", [128, 144], I32), "odd2": ("sbuf", [128, 1], I32), "bi": ("sbuf", [128, 4], I32),
-    "bf": ("sbuf", [128, 4], F32), "kcol": ("sbuf", [128, 4], F32), "zero": ("sbuf", [128, 512], BF),
-    "ste": ("sbuf", [128, 144], BF), "sto": ("sbuf", [128, 144], BF), "sel": ("sbuf", [128, 144], BF),
-    "spr": ("sbuf", [128, 144], BF), "wsf": ("sbuf", [128, 256], BF), "wsn": ("sbuf", [128, 384], BF),
-    "tb": ("sbuf", [128, 128], F32), "lf": ("sbuf", [128, 64], F32),
-    "s0n": ("sbuf", [128, 16], U16), "s0f": ("sbuf", [128, 16], U16), "s1": ("sbuf", [128, 24], U16),
-    "r0": ("sbuf", [128, 16], U16), "r1": ("sbuf", [128, 24], U16),
-    "l0": ("sbuf", [128, 192], U16), "l0b": ("sbuf", [128, 192], U16), "l1k": ("sbuf", [128, 192], U16),
+    "vi": ("sbuf", [128, 128], I32), "xr": ("sbuf", [128, 160], BF), "r2": ("sbuf", [128, 4, 64], BF),
+    "pcol": ("sbuf", [128, 1], I32), "bi": ("sbuf", [128, 4], I32),
+    "bf": ("sbuf", [128, 12], F32), "wrap": ("sbuf", [128, 4], F32), "zero": ("sbuf", [128, 512], BF),
+    "lt": ("sbuf", [128, 2, 144], BF), "sel": ("sbuf", [128, 144], BF), "spr": ("sbuf", [128, 144], BF),
+    "wsf": ("sbuf", [128, 384], BF), "wsn": ("sbuf", [128, 128], BF), "tb": ("sbuf", [128, 64], F32),
+    "s0": ("sbuf", [128, 24], U16), "s1": ("sbuf", [128, 24], U16), "heldl": ("sbuf", [128, 64], U16),
+    "l0": ("sbuf", [128, 192], U16), "l0b": ("sbuf", [128, 192], U16),
     "l1n": ("sbuf", [128, 192], U16), "l1f": ("sbuf", [128, 192], U16), "l2": ("sbuf", [128, 192], U16),
-    "w0": ("sbuf", [128, 3072], BF), "w1": ("sbuf", [128, 2, 3072], BF), "w2": ("sbuf", [128, 3072], BF),
-    "pic": ("sbuf", [128, 3072], BF), "k1": ("sbuf", [128, 3072], BF), "jb": ("sbuf", [128, 3072], BF),
-    "yo": ("sbuf", [128, 3072], BF), "rp": ("sbuf", [128, 256], BF), "rk": ("sbuf", [128, 256], BF),
-    "rw": ("sbuf", [128, 128], BF), "rv": ("sbuf", [128, 128], BF),
-    "xi": ("psum", [128, 32, 16], F32), "blk": ("psum", [128, 16, 32], F32), "po": ("psum", [128, 512], F32),
-    "pn": ("psum", [128, 16, 32], F32), "pf": ("psum", [128, 512], F32),
-    "psf": ("psum", [128, 32, 16], F32), "psn": ("psum", [128, 32, 16], F32),
+    "w0": ("sbuf", [128, 3072], BF), "w1": ("sbuf", [128, 3072], BF), "w2": ("sbuf", [128, 3072], BF),
+    "pic": ("sbuf", [128, 3072], BF), "i1": ("sbuf", [128, 3072], BF), "k1": ("sbuf", [128, 3072], BF),
+    "jb": ("sbuf", [128, 3072], BF), "yo": ("sbuf", [128, 3072], BF), "held": ("sbuf", [128, 2048], BF),
+    "stage": ("dram", [2, 128, (512 - EARLY) // 2], BF),
+    "cx": ("psum", [128, 512], F32), "blk": ("psum", [128, 16, 32], F32), "psf": ("psum", [128, 512], F32),
+    "psn": ("psum", [128, 512], F32), "po": ("psum", [128, 512], F32), "pm": ("psum", [128, 512], F32),
+    "pa": ("psum", [128, 512], F32), "pf": ("psum", [128, 512], F32),
 }
-SEMAPHORES = ["vc", "gi", "ldy", "ldx", "lda", "ldb", "lde", "ms", "fill", "fill2", "sel1", "sel2", "st", "sp", "dg", "t_b",
-              "t_sf", "t_sn", "c_sf", "c_sn", "s0", "lo", "lob", "rs_o", "g_o", "g_e", "g_n", "g_f", "g_q", "h_n", "h_e",
-              "h_q", "h_f", "h_8", "k_o", "k_a", "k_b", "j_n", "j_f", "y_a", "y_b", "t_o", "t_n", "t_f", "c_k", "c_s",
-              "c_o", "c_f", "c_d", "c_e", "vir0", "vir1", "pv", "w0n", "w0f", "w1f", "l0n", "l0f", "l1a", "pnr", "pfr",
-              "kfr", "jnr", "sent", "sty_a", "sty_b", "rea", "rwa", "rva", "r0a", "r1a", "rpa", "rka", "rsent"]
+FAR = ["early", "w0f", "s0", "img", "rv", "s1", "k1"]
+SEMAPHORES = ["vc", "gi", "gx", "g2", "ldy", "ldx", "lde", "lda", "ldb", "ms", "fill", "fill2", "sel", "va", "vb", "lt",
+              "spr", "dg", "t_b", "t_sf", "t_sn", "c_sf", "c_sn", "c_0", "lo", "lob", "rs_o", "g_o", "g_e", "g_n", "g_f",
+              "i_o", "i_f", "h_n", "h_e", "h_f", "h_8", "k_o", "k_b", "j_n", "j_f", "j_o", "y_a", "y_b", "t_o", "t_m", "t_a",
+              "t_f", "c_s", "c_o", "c_m", "c_7", "c_d", "c_e", "lds", "vir0", "vir1", "pv", "w0n", "w1n", "imgn", "jb", "sent", "sty_a",
+              "sty_b", "rsent"] + FAR + ["at_" + x for x in FAR]
+N0 = 3 if FAR3 else 2
+NL0 = 3 if FARI else N0 - 1
+NL1 = 2 if FAR3 else 3
 
 
 def plan(T, topo):
@@ -45,7 +60,7 @@ def plan(T, topo):
     for s, d in flows:
         mate = [x for x in range(0, SIM_CORES, len(topo.cores_of(d))) if topo.mates(x, d)][0]
         relays[(s, d)] = []
-        for c, e in ((s, topo.die(s)), (mate, topo.die(d))):
+        for c, e in ((s, topo.die(s)), (mate, topo.die(d))) * 2:
             x = [x for x in topo.cores_of(c) if T.rank_of(x) is None and x not in used and topo.die(x) == e
                  and topo.may_write(x, d) and topo.may_write(s, x)][0]
             used.add(x)
@@ -60,26 +75,33 @@ def bits(engines):
     return m
 
 
-def transfer(topo, src, dst, out, in_, engines, sem):
-    rid, pid = topo.addr(dst, src)
-    return RemoteDMATransfer(dst_ids=[DstId(rid=rid, pnc=pid)], dma_engine_mask=bits(engines), remote_sem=sem,
-                             src=in_, dst=out)
-
-
 def turned(up, a, b):
     return (a, b) if up else (24 - b, 24 - a)
 
 
-def first_list(T, s, d):
-    if T.rank_of(s) > T.rank_of(d):
-        return T.l0[:, 128:144], 8, 8
-    return T.l0b[:, 48:64], 5, 14
+def low_row(up, edge):
+    return (4 if FARI else 8 - N0) if up and not edge else 7
 
 
-def cols(t, a, b):
-    if isinstance(t, tuple):
-        return t[0][:, t[1], a + t[2]:b + t[2]]
-    return t[:, a:b]
+def landing(T, name, up):
+    def at(t, a, b, w=128):
+        a, b = turned(up, a, b)
+        return t, w * a, w * (b - a)
+    if name in ("early", "img"):
+        c = at(T.pic, 4, 8)[1]
+        return (T.pic, c, EARLY) if name == "early" else (T.pic, c + EARLY, 512 - EARLY)
+    return {"w0f": at(T.w0, 8 - N0, 8), "s0": at(T.l0b if up else T.l0, 8 - NL0, 8, 8), "rv": at(T.w1, 6, 7),
+            "s1": at(T.l1f, 4, 4 + NL1, 8), "k1": at(T.k1, 2, 6)}[name]
+
+
+def messages():
+    return [x for x in ORDER if not (x == "rv" and FAR3) and not (x == "early" and not EARLY)]
+
+
+def held(T, name, n):
+    if name == "img" and STAGE:
+        return T.stage[0]
+    return (T.heldl if name in ("s0", "s1") else T.held)[:, HELD[name]:HELD[name] + n]
 
 
 def rank_program(g, core, T, topo):
@@ -96,385 +118,440 @@ def rank_program(g, core, T, topo):
     edge = fb is None
     V, S, TE, SY = g.vector, g.scalar, g.tensor, g.sync
     top = 8 * r
-    w1 = (T.w1, 0, 0)
-    cnt = [0, 0]
+    cnt = {}
 
     def R(a, b):
         return turned(up, a, b)
 
     def rows(t, a, b):
         a, b = R(a, b)
-        return cols(t, 128 * a, 128 * b)
+        return t[:, 128 * a:128 * b]
 
-    def v(ins, name=None):
-        if name:
-            ins.then_inc(sem[name], 1)
-        else:
-            ins.then_inc(sem.vc, 1)
-            cnt[0] += 1
+    def v(ins, name="vc"):
+        ins.then_inc(sem[name], 1)
+        cnt[name] = cnt.get(name, 0) + 1
 
     def vs():
-        if cnt[0] > cnt[1]:
-            V.wait_ge(sem.vc, cnt[0])
-            cnt[1] = cnt[0]
+        V.wait_ge(sem.vc, cnt["vc"])
 
     def ts(out, in0, s1, op0, s2=None, op1=None):
         if op1 is None:
             return V.tensor_scalar(out=out, in0=in0, scalar1=s1, scalar2=None, op0=op0)
         return V.tensor_scalar(out=out, in0=in0, scalar1=s1, scalar2=s2, op0=op0, op1=op1)
 
-    S.dma_start(out=T.vi[64:128], in_=T.vx[:]).then_inc(sem.ldx, 16)
-    SY.dma_start(out=T.vi[0:64], in_=T.vy[:]).then_inc(sem.ldy, 16)
-    for (a, b), name in ((R(8, 12), "lda"), (R(12, 16), "ldb")):
-        SY.dma_start(out=T.pic[:, 128 * a:128 * b], in_=T.img[:, 128 * (a - 8):128 * (b - 8)]).then_inc(sem[name], 16)
+    def both(name, k):
+        V.wait_ge(sem[name], k)
+        S.wait_ge(sem[name], k)
 
-    g.iota(out=T.odd2[:], pattern=[[1, 1]], base=1, channel_multiplier=2).then_inc(sem.gi, 1)
-    g.iota(out=T.ramp[:], pattern=[[1, 144]], base=0, channel_multiplier=0).then_inc(sem.gi, 1)
+    fa, na = 128 * R(8, 12)[0], 128 * R(12, 16)[0]
+    first = EARLY if OWN_LOAD and not edge else 0
+
+    def load(q, a, b, name):
+        q.dma_start(out=T.pic[:, a:b], in_=T.img[:, a - 1024:b - 1024]).then_inc(sem[name], 16)
+    for x in LOADS.split():
+        q = S if x[0] == "S" else SY
+        if x[1] == "x":
+            q.dma_start(out=T.vi[64:128], in_=T.vx[:]).then_inc(sem.ldx, 16)
+        elif x[1] == "y":
+            q.dma_start(out=T.vi[0:64], in_=T.vy[:]).then_inc(sem.ldy, 16)
+        elif x[1] == "e" and first:
+            load(q, fa, fa + first, "lde")
+        elif x[1] == "a":
+            load(q, fa + first, fa + 512, "lda")
+        elif x[1] == "b":
+            load(q, na, na + 512, "ldb")
+        elif x[1] == "s" and STAGE and not edge:
+            n = (512 - EARLY) // 2
+            for k in range(2):
+                c = fa - 1024 + EARLY + k * n
+                q.dma_start(out=T.stage[k], in_=T.img[:, c:c + n]).then_inc(sem.lds, 16)
+
+    def images(q):
+        for name in ("lde", "lda", "ldb")[0 if first else 1:]:
+            q.wait_ge(sem[name], 16)
+
+    def iota(out, pattern, base, cm, name):
+        g.iota(out=out, pattern=pattern, base=base, channel_multiplier=cm,
+               allow_small_or_imprecise_dtypes=True).then_inc(sem[name], 1)
+    iota(T.pcol[:], [[1, 1]], 0, 1, "gi")
+    iota(T.xr[:, 0:145], [[1, 145]], -1, 0, "gx")
+    iota(T.r2[:], [[1, 256]], -3, 0, "g2")
     v(V.memset(T.zero[:], 0.0), "ms")
     S.wait_ge(sem.ms, 1)
-    if up:
-        fills = [(w1, 8, 9)] + ([(T.w0, 5, 7), (T.jb, 0, 4)] if edge else [(T.w0, 5, 6), (T.pic, 2, 4), (w1, 2, 6)])
-    else:
-        fills = [(w1, 5, 6)]
-    own = [(T.w0, 8, 12), (T.w0, 12, 16)]
+    low = low_row(up, edge)
 
     def fill(name, todo):
         for t, a, b in todo:
-            S.activation(out=cols(t, 128 * a, 128 * b), in_=T.zero[:, 0:128 * (b - a)], func=F.Copy).then_inc(sem[name], 1)
-    fill("fill", own)
-    fill("fill2", fills)
-    g.wait_ge(sem.ms, 1)
-    pat = [[-16, 9], [1000, 16]]
-    g.affine_select(T.sel[:], T.zero[:, 0:144], pat, A.not_equal, 1.0, -15000, 1).then_inc(sem.sel1, 1)
-    g.wait_ge(sem.sel1, 1)
-    g.affine_select(T.sel[:], T.sel[:], pat, A.not_equal, 1.0, -15001, 1).then_inc(sem.sel2, 1)
-    V.wait_ge(sem.gi, 1)
-    v(ts(T.bi[:, 2:3], T.odd2[:], 1, A.arith_shift_right, 7, A.bitwise_and))
-    v(ts(T.bi[:, 0:1], T.odd2[:], 127, A.bitwise_and))
-    v(ts(T.bi[:, 1:2], T.odd2[:], 4, A.arith_shift_right, 1, A.bitwise_and))
-    if edge:
-        v(ts(T.bi[:, 3:4], T.odd2[:], 31, A.bitwise_and))
-    vs()
-    v(ts(T.bf[:, 2:3], T.bi[:, 2:3], float(top + 8), A.add))
-    v(V.tensor_copy(out=T.bf[:, 0:2], in_=T.bi[:, 0:2]))
-    V.wait_ge(sem.gi, 2)
-    v(V.tensor_copy(out=T.xi[64:128, 0:8, :], in_=T.ramp[64:128, 0:128]))
-    vs()
-    v(ts(T.ste[:], T.ramp[:], T.bf[:, 0:1], A.is_equal, T.bf[:, 1:2], A.is_gt), "st")
-    v(ts(T.sto[:], T.ramp[:], T.bf[:, 0:1], A.is_equal, T.bf[:, 1:2], A.mult), "st")
+            S.activation(out=t[:, 128 * a:128 * b], in_=T.zero[:, 0:128 * (b - a)], func=F.Copy).then_inc(sem[name], 1)
+    fills = []
+    if up:
+        fills = [(T.jb, 0, 4)] if edge else ([] if SPLIT else [(T.w1, 2, 6)]) + (
+            [(T.w0, 4, 8 - N0), (T.i1, 4, 5)] if FARI else [(T.pic, 2, 4)])
+    fill("fill", [(T.w0, 8, 12), (T.w0, 12, 16)])
+    S.activation(out=T.lt[:, :, 128:144], in_=T.zero[:, 0:32], func=F.Copy).then_inc(sem.lt, 1)
+    RC, WT, K1, K2, P15, KP, W0, WP, C4 = range(9)
 
+    def bf(k):
+        return T.bf[:, k:k + 1]
+    q16 = T.bi[:, 1:2]
+    V.wait_ge(sem.gi, 1)
+    v(ts(T.bi[:, 0:1], T.pcol[:], 7, A.bitwise_and), "va")
+    v(ts(T.bi[:, 2:3], T.pcol[:], 63, A.bitwise_and), "va")
+    v(V.memset(T.wrap[0:64, 0:2], 0.0))
+    v(V.memset(T.bf[0:64, WT:WT + 1], 128.0))
+    v(V.memset(T.bf[64:128, WT:WT + 1], 1.0))
+    V.wait_ge(sem.va, 2)
+    v(ts(bf(RC), T.bi[:, 0:1], float(top + 8), A.add), "vb")
+    v(ts(bf(C4), T.bi[:, 2:3], 4.0, A.mult), "vb")
+    V.wait_ge(sem.gx, 1)
+    v(V.tensor_copy(out=T.cx[64:128, 0:128], in_=T.xr[64:128, 1:129]))
+    V.wait_ge(sem.vb, 2)
+    V.wait_ge(sem.ms, 1)
+    v(ts(T.cx[0:64, 0:128], T.zero[0:64, 0:128], T.bf[0:64, RC:RC + 1], A.add))
+    for c in range(2):
+        h = slice(64 * c, 64 * c + 64)
+        v(ts(T.spr[h], T.xr[h, 1 - c:145 - c], 2.0, A.mult, T.bf[h, C4:C4 + 1], A.is_equal), "spr")
+
+    dig = T.i1[:, 1024:1152]
     V.wait_ge(sem.ldx, 16)
-    v(V.tensor_tensor(out=T.ci[64:128], in0=T.vi[64:128], in1=T.xi[64:128, 0:8, :], op=A.add))
+    v(ts(T.wrap[64:128, 0:1], T.vi[64:128, 0:1], 0.0, A.is_lt, 128.0, A.mult), "ms")
+    v(ts(T.wrap[64:128, 1:2], T.vi[64:128, 127:128], 0.0, A.is_gt, -128.0, A.mult), "ms")
+    vs()
     V.wait_ge(sem.ldy, 16)
-    v(ts(T.dig[0:64], T.vi[0:64], T.bf[0:64, 2:3], A.add, 128.0, A.mult), "dg")
+    v(V.tensor_tensor(out=T.i1[:, 1025:1151], in0=T.vi[:, 1:127], in1=T.cx[:, 1:127], op=A.add), "dg")
+    V.wait_ge(sem.ms, 3)
+    for k, x in enumerate((0, 127)):
+        v(ts(T.i1[:, 1024 + x:1025 + x], T.vi[:, x:x + 1], T.cx[:, x:x + 1], A.add, T.wrap[:, k:k + 1], A.add), "dg")
+    V.wait_ge(sem.g2, 1)
+    for e in range(2):
+        v(ts(T.lt[:, e, 0:128], T.r2[:, :, 32 * e:32 * e + 32], bf(C4), A.is_equal, bf(WT), A.mult), "lt")
+    v(ts(q16, T.pcol[:], 15, A.bitwise_and))
+    v(ts(bf(P15), T.pcol[:], 15.0, A.add))
     vs()
-    v(ts(T.ci[64:128], T.ci[64:128], 127, A.bitwise_and))
-    vs()
-    v(V.tensor_copy(out=T.dig[64:128], in_=T.ci[64:128]), "dg")
-    v(ts(T.spr[0:64, 0:142], T.ramp[0:64, 1:143], T.bf[0:64, 0:1], A.is_equal), "sp")
-    v(ts(T.spr[64:128, 0:142], T.ramp[64:128, 0:142], T.bf[64:128, 0:1], A.is_equal), "sp")
+    v(ts(bf(W0), q16, 0.0, A.is_equal, 127.0, A.mult))
+    v(ts(bf(KP), q16, -1.0, A.mult, bf(P15), A.add))
     if edge:
         for k in (1, 2):
-            v(ts(T.kcol[:, k:k + 1], T.bi[:, 3:4], 1.0, A.is_equal, float(-128 * k if up else 128 * k), A.mult))
-    TE.wait_ge(sem.st, 2)
-    TE.wait_ge(sem.dg, 2)
-    for par, st in enumerate((T.ste, T.sto)):
-        for hf in range(2):
-            ins = TE.matmul(T.blk[:, 0:4, 16 * par:16 * par + 16], st[:, 1 - hf:129 - hf], T.dig[:, 4 * hf:4 * hf + 4, :],
-                            hf == 0, hf == 1)
-    ins.then_inc(sem.t_b, 1)
-    TE.wait_ge(sem.sp, 2)
-    edges = [(R(13, 16), T.psn, T.wsn, "sn")]
-    if not edge:
-        edges.insert(1 if NEAR_FIRST else 0, (R(8, 10), T.psf, T.wsf, "sf"))
-    for (a, b), ps, ws, x in edges:
+            v(ts(bf(WT + k), q16, 0.0, A.is_equal, float(-k if up else k), A.mult))
+    vs()
+    v(ts(bf(WP), q16, 1.0, A.is_le, bf(W0), A.add))
+
+    def spread(ps, ws, a, b, x):
+        a, b = R(a, b)
         for i in range(a, b):
-            ins = TE.matmul(ps[:, 8 * (i - a):8 * (i - a) + 8, :], T.spr[:, 2 * (i - 8):2 * (i - 8) + 128], T.dig[:],
-                            True, True)
+            ins = TE.matmul(ps[:, 128 * (i - a):128 * (i - a + 1)], T.spr[:, 2 * (i - 8):2 * (i - 8) + 128], dig, True, True)
         ins.then_inc(sem["t_" + x], 1)
         S.wait_ge(sem["t_" + x], 1)
-        S.activation(out=ws[:], in_=ps[:, 0:8 * (b - a), :], func=F.Copy).then_inc(sem["c_" + x], 1)
+        n = 128 * (b - a)
+        S.activation(out=ws[:, 0:n], in_=ps[:, 0:n], func=F.Copy).then_inc(sem["c_" + x], 1)
+    TE.wait_ge(sem.spr, 2)
+    TE.wait_ge(sem.dg, 3)
+    spread(T.psn, T.wsn, 15, 16, "sn")
+    TE.wait_ge(sem.lt, 3)
+    for e in range(2):
+        for u in range(4):
+            ins = TE.matmul(T.blk[:, 0:2, 16 * e:16 * e + 16], T.lt[:, e, 3 - u:131 - u],
+                            T.i1[:, 1024 + 32 * u:1056 + 32 * u], u == 0, u == 3)
+    ins.then_inc(sem.t_b, 1)
+    if not edge:
+        spread(T.psf, T.wsf, 8, 8 + N0, "sf")
+    fill("fill2", fills)
     V.wait_ge(sem.t_b, 1)
-    for b in range(4):
-        v(V.transpose(out=T.tb[:, b:128:4], in_=T.blk[:, b, :]))
+    for w in range(2):
+        v(V.transpose(out=T.tb[:, w:64:2], in_=T.blk[:, w, :]))
     vs()
-    v(V.tensor_tensor(out=T.lf[:], in0=T.tb[:, 0:64], in1=T.tb[:, 64:128], op=A.add))
-    vs()
-    for lst, d in ((T.s0f, fb), (T.s0n, nb)):
-        if d is not None:
-            _, base, a = first_list(T, core, d)
-            v(ts(lst[:], T.lf[:, 8 * (a - 8):8 * (a - 6)], -128.0 * (8 * T.rank_of(d) + base), A.add), "s0")
-    v(ts(T.l0[:, 72:128], T.lf[:, 8:64], -128.0 * (top + 8), A.add), "lo")
-    v(ts(T.l0b[:, 64:80], T.lf[:, 0:16], -128.0 * (top + 5), A.add), "lob")
+    v(ts(T.l0[:, 72:128], T.tb[:, 8:64], -128.0 * (top + 8), A.add), "lo")
+    if not edge:
+        a, b = R(8, 8 + NL0)
+        there = 8 * T.rank_of(fb) + (8 if up else low_row(True, False))
+        v(ts(T.s0[:, 0:8 * NL0], T.tb[:, 8 * (a - 8):8 * (b - 8)], -128.0 * there, A.add), "c_0")
+    v(ts(T.l0b[:, 64:80], T.tb[:, 0:16], -128.0 * (top + low), A.add), "lob")
+    v(ts(T.sel[:], T.xr[:, 1:145], bf(KP), A.is_equal, bf(WP), A.mult), "sel")
 
     es = topo.engines(core, nb)
-    ref = core if not edge else nb
-    leave = topo.engines(ref, relays[(ref, far[ref])][1])
-    stay = [e for e in es if e not in leave]
-    rel = None if edge else relays[(core, fb)]
-    sent = [0]
-
-    def send(dst, to, src, engines, s):
-        rid, pid = topo.addr(dst, core)
-        g.remote_dma(to, src, s, sem.sent, pid, rid, bits(engines))
-        sent[0] += len(engines)
-
-    def fused(tr):
-        g.remote_dma_fused(tr, local_sem=sem.sent)
-        sent[0] += len(tr) * len(stay)
-
-    def there(t, d, a, b):
-        a, b = R(a, b)
-        o = 8 * (r - T.rank_of(d))
-        return t[:, 128 * (a + o):128 * (b + o)]
-
-    def halves(t, c, n, a, b, held, arrived):
-        fused([transfer(topo, core, rel[1], held[:, a:b], t[:, c + a:c + b], leave, arrived),
-               transfer(topo, core, rel[0], held[:, a:b], t[:, c + n + a:c + n + b], stay, arrived)])
-    pf0 = 128 * R(8, 12)[0]
-    if EARLY and not edge:
-        g.wait_ge(sem.lda, 16)
-        halves(T.pic, pf0, 256, 0, EARLY, T.rp, sem.rea)
-    for _, _, ws, x in edges:
-        g.wait_ge(sem["c_" + x], 1)
-        if x == "sf":
-            halves(ws, 0, 128, 0, 128, T.rw, sem.rwa)
+    groups = engine_groups(topo, near, far, relays, core)
+    sent = 0
+    ready = {"early": [("lde" if first else "lda", 16)], "w0n": [("c_sn", 1)], "w0f": [("c_sf", 1)], "s0": [("c_0", 1)],
+             "img": [("lds", 32) if STAGE else ("lda", 16)], "rv": [("g_o", 2)], "w1n": [("g_o", 2), ("g_n", 2)], "k1": [("k_o", 2)],
+             "s1": [("c_s", 1)], "imgn": [("ldb", 16)], "jb": [("j_n", 2)]}
+    source = {"early": (T.pic, fa), "img": (T.pic, fa + EARLY), "w0f": (T.wsf, 0), "s0": (T.s0, 0), "s1": (T.s1, 0),
+              "rv": (T.w1, 128 * R(9, 10)[0]), "k1": (T.k1, 1280)}
+    to_near = {"w0n": (T.w0, 15), "w1n": (T.w1, 14), "imgn": (T.pic, 12), "jb": (T.jb, 12)}
+    for name in messages():
+        if edge and name in FAR:
+            continue
+        for s, k in ready[name]:
+            g.wait_ge(sem[s], k)
+        if name in FAR:
+            t, c = source[name]
+            ways = WAYS[name].split()
+            n = landing(T, name, up)[2] // len(ways)
+            tr = []
+            for k, way in enumerate(ways):
+                rid, pid = topo.addr(relays[(core, fb)][int(way[0])], core)
+                tr.append(RemoteDMATransfer(dst_ids=[DstId(rid=rid, pnc=pid)], dma_engine_mask=bits(groups[way[1:]]),
+                                            remote_sem=sem["at_" + name], dst=held(T, name, n),
+                                            src=T.stage[k] if name == "img" and STAGE else t[:, c + k * n:c + (k + 1) * n]))
+                sent += len(groups[way[1:]])
+            g.remote_dma_fused(tr, local_sem=sem.sent)
         else:
-            send(nb, there(T.w0, nb, 13, 16), ws[:], es, sem.w0n)
-    g.wait_ge(sem.s0, 1 if edge else 2)
-    tr = [transfer(topo, core, nb, first_list(T, core, nb)[0], T.s0n[:], leave, sem.l0n)]
-    if not edge:
-        tr.insert(0, transfer(topo, core, rel[0], T.r0[:], T.s0f[:], stay, sem.r0a))
-    fused(tr)
-    if not edge:
-        g.wait_ge(sem.lda, 16)
-        halves(T.pic, pf0, 256, EARLY, 256, T.rp, sem.rpa)
-        g.wait_ge(sem.g_o, 2)
-        send(rel[0], T.rv[:], rows(w1, 9, 10), stay, sem.rva)
-    g.wait_ge(sem.ldb, 16)
-    send(nb, there(T.pic, nb, 12, 16), rows(T.pic, 12, 16), es, sem.pnr)
-    if not edge:
-        g.wait_ge(sem.c_s, 1)
-        send(rel[0], T.r1[:], T.s1[:], stay, sem.r1a)
-        g.wait_ge(sem.k_o, 2)
-        halves(T.k1, 128 * 10, 256, 0, 256, T.rk, sem.rka)
-    g.wait_ge(sem.j_n, 2)
-    send(nb, there(T.jb, nb, 12, 16), rows(T.jb, 12, 16), es, sem.jnr)
+            t, a = to_near[name]
+            c, d = R(a, 16)
+            o = 8 * (r - T.rank_of(nb))
+            rid, pid = topo.addr(nb, core)
+            g.remote_dma(t[:, 128 * (c + o):128 * (d + o)], T.wsn[:] if name == "w0n" else rows(t, a, 16), sem[name],
+                         sem.sent, pid, rid, bits(es))
+            sent += len(es)
+
+    def came(name, q=None):
+        k = len(WAYS[name].split()) * len(topo.engines(relays[(fb, core)][0], core)) if name in FAR else len(es)
+        if name in messages():
+            for x in ((V, S) if q is None else (q,)):
+                x.wait_ge(sem[name], k)
 
     SY.wait_ge(sem.fill, 2)
-    SY.wait_ge(sem.dg, 2)
+    SY.wait_ge(sem.dg, 3)
     for h in range(2):
-        SY.dma_start(out=T.w0[h:128:16, 1024:2048], in_=T.dig[64 * h:64 * h + 64]).then_inc(sem.rs_o, 16)
+        SY.dma_start(out=T.w0[h:128:16, 1024:2048], in_=T.i1[64 * h:64 * h + 64, 1024:1152]).then_inc(sem.rs_o, 16)
 
-    def part(eng, out, W, lst, a, b, name):
-        o, i = cols(out, 16 * a, 16 * b), W.indirect(lst[:, a:b])
+    def part(eng, out, win, lst, a, b, name):
+        o, i = out[:, 16 * a:16 * b], win.indirect(lst[:, a:b])
         if eng is V:
             V.tensor_copy(out=o, in_=i).then_inc(sem[name], 1)
         else:
             S.activation(out=o, in_=i, func=F.Copy).then_inc(sem[name], 1)
 
-    def gather(out, win, w, lst, rr, name, less=0):
+    def gather(out, win, w, lst, rr, name):
         a, b = 8 * rr[0], 8 * rr[1]
-        m = a + (b - a) // 4 * 2 - less
-        part(V, out, cols(win, 128 * w[0], 128 * w[1]), lst, a, m, name)
-        part(S, out, cols(win, 128 * w[0], 128 * w[1]), lst, m, b, name)
+        m = (a + b) // 2 + MORE.get(name, 0)
+        part(V, out, win[:, 128 * w[0]:128 * w[1]], lst, a, m, name)
+        part(S, out, win[:, 128 * w[0]:128 * w[1]], lst, m, b, name)
 
-    def one(eng, out, win, w, lst, row, name):
-        a = 8 * R(row, row + 1)[0]
-        part(eng, out, cols(win, 128 * w[0], 128 * w[1]), lst, a, a + 8, name)
-
-    def pick(ps, moving, name):
+    def pick(ps, w, rr, name):
         for q in range(16):
-            ins = TE.matmul(ps, T.sel[:, 15 - q:143 - q], moving(q), q == 0, q == 15)
+            ins = TE.matmul(ps[:, 0:8 * (rr[1] - rr[0])], T.sel[:, 15 - q:143 - q], w[:, 128 * rr[0] + q:128 * rr[1]:16],
+                            q == 0, q == 15)
         ins.then_inc(sem[name], 1)
-
-    def both(name, k):
-        V.wait_ge(sem[name], k)
-        S.wait_ge(sem[name], k)
 
     def listed(lst, rr, ps, first, base, name, at=None):
         at = rr[0] if at is None else at
-        v(ts(lst[:, 8 * at:8 * (at + rr[1] - rr[0])], cols(ps, 8 * (rr[0] - first), 8 * (rr[1] - first)), -128.0 * base,
+        v(ts(lst[:, 8 * at:8 * (at + rr[1] - rr[0])], ps[:, 8 * (rr[0] - first):8 * (rr[1] - first)], -128.0 * base,
              A.add), name)
 
-    def side(high, n):
-        return (T.l0, (8, 16 + n)) if high else (T.l0b, (5, 10))
+    def side(high, n, m=10):
+        return (T.l0, (8, 16 + n)) if high else (T.l0b, (low, m))
 
     def beyond(win, k, name):
-        v(ts(rows(win, 8 - k, 9 - k), rows(win, 8, 9), T.kcol[:, k:k + 1], A.add), name)
+        v(ts(rows(win, 8 - k, 9 - k), rows(win, 8, 9), T.bf[:, WT + k:WT + k + 1], A.add), name)
 
-    def near_side(stage):
-        l0, w = side(up, 3)
-        if stage == 0:
-            both("l0n", len(leave))
-            both("w0n", len(es))
-            gather(w1, T.w0, w, l0, R(15, 18), "g_n")
-        else:
-            both("g_n", 2)
-            both("g_o", 2)
-            gather(T.w0, w1, (8, 18) if up else (5, 11), l0, R(14, 17), "g_q")
+    ro = R(8 if edge else 9, 16)
+    fw, nw = R(6 if edge else 2, 14), R(10, 18)
+    dw, ew = R(8, 20), R(0 if edge else 4, 16)
+    ra, rb = R(12, 16), R(8, 12)
 
     both("lo", 1)
+
+    def twice(stage):
+        if stage == 0:
+            images(V)
+            images(S)
+            gather(T.i1, T.pic, (8, 16), T.l0, (9, 15), "i_o")
+        else:
+            both("i_o", 2)
+            gather(T.k1, T.i1, (8, 15), T.l0, (10, 14), "k_o")
+    for stage in range(0 if edge else I_FIRST):
+        twice(stage)
     both("rs_o", 32)
-    gather(w1, T.w0, (8, 16), T.l0, (9, 15), "g_o")
-    both("fill2", len(fills))
+    gather(T.w1, T.w0, (8, 16), T.l0, (9, 15), "g_o")
     both("lob", 1)
-    TE.wait_ge(sem.sel2, 1)
-    TE.wait_ge(sem.g_o, 2)
-    ro = R(8, 15) if edge else (9, 15)
-    fw = R(6, 14) if edge else R(2, 14)
-    nw = (8, 17) if up else (7, 14)
     if edge:
-        vs()
         beyond(T.w0, 1, "vir0")
         both("vir0", 1)
-        gather(w1, T.w0, (5, 10) if up else (8, 17), T.l0b if up else T.l0, R(8, 9), "g_e")
-        TE.wait_ge(sem.g_e, 2)
-    pick(T.po[:, 0:8 * (ro[1] - ro[0])], lambda q: T.w1[:, 0, 128 * ro[0] + q:128 * ro[1]:16], "t_o")
+        l0, w = side(not up, 1)
+        gather(T.w1, T.w0, w, l0, R(8, 9), "g_e")
+    came("w0n")
+    l0, w = side(up, 1)
+    gather(T.w1, T.w0, w, l0, R(15, 16), "g_n")
+    TE.wait_ge(sem.sel, 1)
+    TE.wait_ge(sem.g_o, 2)
+    TE.wait_ge(sem.g_n, 2)
     if edge:
+        TE.wait_ge(sem.g_e, 2)
+    pick(T.po, T.w1, ro, "t_o")
+    if edge:
+        images(V)
+        images(S)
         V.wait_ge(sem.g_e, 2)
-        beyond(w1, 1, "vir1")
-        beyond(w1, 2, "vir1")
-        both("lda", 16)
+        beyond(T.w1, 1, "vir1")
+        beyond(T.w1, 2, "vir1")
         for k in range(8):
             o, i = rows(T.pic, k, k + 1), rows(T.pic, 8, 9)
             if k % 2:
                 v(V.tensor_copy(out=o, in_=i), "pv")
             else:
                 S.activation(out=o, in_=i, func=F.Copy).then_inc(sem.pv, 1)
-        S.wait_ge(sem.g_e, 2)
-    if G2_EARLY:
-        near_side(0)
-    V.wait_ge(sem.t_o, 1)
-    if edge:
-        listed(T.l1f, R(8, 12), T.po, ro[0], top + fw[0], "c_o")
-        listed(T.l1n, R(12, 15), T.po, ro[0], top + nw[0], "c_o")
-        both("c_o", 2)
-        both("vir1", 2)
-        both("g_o", 2)
-        gather(T.w2, w1, fw, T.l1f, R(8, 12), "h_e")
-        n_o = 2
     else:
-        l1k = T.l1n if up else T.l1k
-        listed(l1k, (10, 15) if up else (10, 14), T.po, 9, top + 8, "c_k")
-        listed(T.s1, R(9, 12), T.po, 9, 8 * T.rank_of(fb) + turned(not up, 2, 14)[0], "c_s", 0)
-        both("c_k", 1)
-        both("lda", 16)
-        both("ldb", 16)
-        gather(T.k1, T.pic, (8, 16), l1k, (10, 14), "k_o", less=2)
-        listed(T.l1f, R(9, 12), T.po, 9, top + fw[0], "c_o")
-        n_o = 1
-        if not up:
-            listed(T.l1n, R(12, 15), T.po, 9, top + nw[0], "c_o")
-            n_o = 2
-    if not G2_EARLY:
-        near_side(0)
-    near_side(1)
-    wn = T.w2 if edge else (T.w1, 1, -640 if up else 640)
-    both("c_o", n_o)
-    gather(wn, w1, nw, T.l1n, R(12, 15), "h_n")
-    both("g_q", 2)
-    gather(wn, T.w0, (8, 17) if up else (5, 10), side(up, 3)[0], R(15, 16), "h_q")
-    TE.wait_ge(sem.h_n, 2)
-    TE.wait_ge(sem.h_q, 2)
-    dw, ew = R(8, 20), R(0 if edge else 4, 16)
+        for stage in range(I_FIRST, 2 if K_SHADOW else 1):
+            twice(stage)
+    V.wait_ge(sem.t_o, 1)
+    if not edge:
+        listed(T.s1, R(12 - NL1, 12), T.po, ro[0], 8 * T.rank_of(fb) + turned(not up, 2, 14)[0], "c_s", 0)
+    listed(T.l1n, ra, T.po, ro[0], top + nw[0], "c_o")
+    split = SPLIT and not edge
+    l1m, mw = (T.l1n if up else T.l1f, R(6, 14)) if split else (T.l1f, fw)
+    listed(l1m, R(8 if edge else 9, 12), T.po, ro[0], top + mw[0], "c_o")
+    if fills:
+        both("fill2", len(fills))
 
-    def shared(less):
+    def near_rows():
+        both("c_o", 2)
+        both("g_o", 2)
+        both("g_n", 2)
+        came("w1n")
+        gather(T.w2, T.w1, nw, T.l1n, ra, "h_n")
+        TE.wait_ge(sem.h_n, 2)
+        pick(T.pa, T.w2, ra, "t_a")
+
+    def shared():
         both("c_d", 1)
-        both("lda", 16)
-        both("ldb", 16)
-        both("pnr", len(es))
-        gather(T.jb, T.pic, dw, T.l2, R(12, 16), "j_n", less)
+        came("imgn")
+        gather(T.jb, T.pic, dw, T.l2, ra, "j_n")
     if edge:
+        near_rows()
+        both("vir1", 2)
+        both("g_e", 2)
+        gather(T.w2, T.w1, fw, T.l1f, rb, "h_e")
         TE.wait_ge(sem.h_e, 2)
-        pick(T.pf[:, 0:64], lambda q: T.w2[:, 1024 + q:2048:16], "t_n")
-        V.wait_ge(sem.t_n, 1)
-        listed(T.l2, R(12, 16), T.pf, 8, top + dw[0], "c_d")
-        shared(10)
-        listed(T.l2, R(8, 12), T.pf, 8, top + ew[0], "c_e")
+        pick(T.pf, T.w2, rb, "t_f")
+        V.wait_ge(sem.t_a, 1)
+        listed(T.l2, ra, T.pa, ra[0], top + dw[0], "c_d")
+        shared()
+        V.wait_ge(sem.t_f, 1)
+        listed(T.l2, rb, T.pf, rb[0], top + ew[0], "c_e")
         for k in range(1, 5):
-            listed(T.l2, R(8, 9), T.pf, 8, top + ew[0] + (k if up else -k), "c_e", R(8 - k, 9 - k)[0])
+            listed(T.l2, R(8, 9), T.pf, rb[0], top + ew[0] + (k if up else -k), "c_e", R(8 - k, 9 - k)[0])
         both("c_e", 5)
         both("pv", 8)
         gather(T.jb, T.pic, ew, T.l2, R(4, 12), "j_f")
     else:
-        l0, w = side(not up, 2)
-        relayed = len(topo.engines(relays[(fb, core)][0], core))
-        both("l0f", relayed)
-        both("w0f", 2 * relayed)
-        both("h_n", 2)
-        gather(w1, T.w0, w, l0, R(7, 9), "g_f")
+        if not K_SHADOW and I_FIRST < 2:
+            twice(1)
+        if H_FIRST:
+            near_rows()
+        l0, w = side(not up, N0)
+        rm = R(9 - N0, 9)
+        came("s0")
+        came("w0f")
+        gather(T.w1, T.w0, w, l0, rm, "g_f")
         TE.wait_ge(sem.g_f, 2)
-        rn = R(7, 11)
-        pick(T.pn[:, 0:2, :], lambda q: T.w1[:, 0:2, 128 * rn[0] + q:128 * rn[1]:16], "t_n")
-        both("g_f", 2)
-        both("w1f", relayed)
-        hw, iw = (fw, fw) if up else (R(6, 14), R(4, 14))
-        gather(T.w2, w1, hw, T.l1f, R(9, 12), "h_f")
-        both("pfr", (4 if EARLY else 2) * relayed)
-        one(V, T.k1, T.pic, iw, T.l1f, 9, "k_a")
-        S.wait_ge(sem.l1a, relayed)
-        one(S, T.k1, T.pic, iw, T.l1f, 6, "k_a")
-        V.wait_ge(sem.t_n, 1)
-        listed(T.l1f, R(7, 9), (T.pn, 0, 0), rn[0], top + fw[0], "c_f")
-        listed(T.l2, R(12, 16), (T.pn, 1, 0), R(12, 16)[0], top + dw[0], "c_d")
-        S.wait_ge(sem.c_f, 1)
-        one(S, T.w2, w1, hw, T.l1f, 8, "h_8")
-        TE.wait_ge(sem.h_f, 2)
-        TE.wait_ge(sem.h_8, 1)
-        re_ = R(8, 12)
-        pick(T.pf[:, 0:32], lambda q: T.w2[:, 128 * re_[0] + q:128 * re_[1]:16], "t_f")
-        shared(-2)
-        V.wait_ge(sem.c_f, 1)
-        gather(T.k1, T.pic, iw, T.l1f, R(7, 9), "k_b")
-        both("k_o", 2)
-        both("k_a", 2)
-        both("k_b", 2)
-        both("kfr", 2 * relayed)
-        V.wait_ge(sem.l1a, relayed)
-        gather(T.jb, T.k1, fw, T.l1f, R(4, 12), "j_f", less=2)
-        V.wait_ge(sem.t_f, 1)
-        listed(T.l2, re_, T.pf, re_[0], top + ew[0], "c_e")
+        pick(T.pm, T.w1, rm, "t_m")
+        if not H_FIRST:
+            near_rows()
+        hw, iw = (mw, (2, 12)) if up else (R(6, 14), R(4, 14))
+
+        def step(x):
+            if x == "i_f" and FARI:
+                came("early")
+                came("img")
+                both("k_o", 2)
+                V.wait_ge(sem.t_sf, 1)
+                gather(T.i1, T.pic, side(not up, 4)[1], l0, R(5, 9), "i_f")
+            elif x == "c_m":
+                V.wait_ge(sem.t_m, 1)
+                if split and up:
+                    listed(l1m, (8, 9), T.pm, rm[0], top + mw[0], "c_m")
+                    listed(T.l1f, (rm[0], 8), T.pm, rm[0], top + fw[0], "c_7")
+                else:
+                    listed(T.l1f, rm, T.pm, rm[0], top + fw[0], "c_m")
+            elif x == "k_b" and FARI:
+                both("i_f", 2)
+                gather(T.k1, T.i1, side(not up, 3, 11)[1], l0, R(6, 10), "k_b")
+            elif x == "c_d":
+                V.wait_ge(sem.t_a, 1)
+                listed(T.l2, ra, T.pa, ra[0], top + dw[0], "c_d")
+            elif x == "h_f":
+                both("g_f", 2)
+                came("rv")
+                both("c_m", 1)
+                gather(T.w2, T.w1, hw, l1m, rb, "h_f")
+                TE.wait_ge(sem.h_f, 2)
+                pick(T.pf, T.w2, rb, "t_f")
+            elif x == "k_1" and not FARI:
+                came("s1")
+                came("early")
+                came("img")
+                gather(T.k1, T.pic, iw, T.l1f, R(6, 10), "k_b")
+            elif x == "j_n":
+                shared()
+            elif x == "j_o" and split:
+                both("k_o", 2)
+                both("k_b", 2)
+                both("c_m", 1)
+                gather(T.jb, T.k1, mw, l1m, rb, "j_o")
+            elif x == "c_e":
+                V.wait_ge(sem.t_f, 1)
+                listed(T.l2, rb, T.pf, rb[0], top + ew[0], "c_e")
+            elif x == "j_f":
+                both("k_o", 2)
+                both("k_b", 2)
+                both("c_m", 1)
+                if split and up:
+                    both("c_7", 1)
+                came("s1")
+                came("k1")
+                gather(T.jb, T.k1, fw, T.l1f, R(4, 8 if split else 12), "j_f")
+            elif x == "y_b" and Y_B_FIRST:
+                both("j_o", 2)
+                both("j_n", 2)
+                came("jb")
+                gather(T.yo, T.jb, dw, T.l2, ra, "y_b")
+        for x in STEPS:
+            step(x)
         both("c_e", 1)
+        if split:
+            both("j_o", 2)
     both("j_f", 2)
     both("j_n", 2)
-    pieces = ((R(8, 12), ew if up else R(4, 16), "a"), (R(12, 16), dw, "b"))
+    pieces = ((rb, ew if up else R(4, 16), "a"), (ra, dw, "b"))
     for rr, w, x in pieces:
         if x == "b":
-            both("jnr", len(es))
+            if Y_B_FIRST and not edge:
+                pieces = pieces[::-1]
+                break
+            came("jb")
         gather(T.yo, T.jb, w, T.l2, rr, "y_" + x)
     for rr, w, x in pieces:
         SY.wait_ge(sem["y_" + x], 2)
         SY.dma_start(out=T.y[:, 128 * (rr[0] - 8):128 * (rr[1] - 8)], in_=T.yo[:, 128 * rr[0]:128 * rr[1]]).then_inc(
             sem["sty_" + x], 16)
-    g.wait_ge(sem.sent, sent[0])
+    g.wait_ge(sem.sent, sent)
     for rr, w, x in pieces:
-        g.wait_ge(sem["sty_" + x], 16)
+        SY.wait_ge(sem["sty_" + x], 16)
+
+
+def engine_groups(topo, near, far, relays, core):
+    ref = core if core in far else near[core]
+    leave = topo.engines(ref, relays[(ref, far[ref])][1])
+    every = topo.engines(core, near[core])
+    stay = [e for e in every if e not in leave]
+    h = len(stay) // 2
+    return {"L": leave, "S": stay, "A": every, "L1": leave[:h], "L2": leave[h:], "S1": stay[:h], "S2": stay[h:]}
 
 
 def hand_on(g, core, T, topo, s, d, i, up):
     sem = T.sem
     es = topo.engines(core, d)
     rid, pid = topo.addr(d, core)
-
-    def half(t, a, b, lo=0, hi=None):
-        a, b = turned(up, a, b)
-        n = 64 * (b - a)
-        c = 128 * a + n * (1 - i)
-        return t[:, c + lo:c + (n if hi is None else hi)]
-    a, b = turned(up, 4, 7)
-    c = 128 * turned(up, 6, 7)[0]
-    jobs = [("rea", half(T.pic, 4, 8, 0, EARLY), T.rp[:, 0:EARLY], sem.pfr)] if EARLY else []
-    jobs += [("rwa", half(T.w0, 6, 8), T.rw[:], sem.w0f),
-             ("r0a", first_list(T, s, d)[0], T.r0[:], sem.l0f),
-             ("rpa", half(T.pic, 4, 8, EARLY), T.rp[:, EARLY:256], sem.pfr),
-             ("rva", T.w1[:, 0, c:c + 128], T.rv[:], sem.w1f),
-             ("r1a", T.l1f[:, 8 * a:8 * b], T.r1[:], sem.l1a),
-             ("rka", half(T.k1, 2, 6), T.rk[:], sem.kfr)]
-    n = 0
-    for came, to, held, arrived in jobs:
-        if i == 0 or came in ("rea", "rwa", "rpa", "rka"):
-            g.wait_ge(sem[came], len(es))
-            g.remote_dma(to, held, arrived, sem.rsent, pid, rid, bits(es))
-            n += len(es)
-    g.wait_ge(sem.rsent, n)
+    groups = engine_groups(topo, *plan(T, topo), s)
+    sent = 0
+    for name in messages():
+        ways = WAYS.get(name, "").split()
+        for k, way in enumerate(ways):
+            if int(way[0]) == i:
+                t, c, n = landing(T, name, up)
+                n //= len(ways)
+                g.wait_ge(sem["at_" + name], len(groups[way[1:]]))
+                g.remote_dma(t[:, c + k * n:c + (k + 1) * n], held(T, name, n), sem[name], sem.rsent, pid, rid, bits(es))
+                sent += len(es)
+    if sent:
+        g.wait_ge(sem.rsent, sent)

@@ -4,47 +4,107 @@ from concourse.mybir import AluOpType as A, ActivationFunctionType as F
 BF, F32, I32, U16 = "bfloat16", "float32", "int32", "uint16"
 SIM_CORES = 256
 EARLY = 64
-OWN_LOAD = True
-I_FIRST = 1
-K_SHADOW = True
-H_FIRST = False
-FAR3 = False
-FARI = True
-SPLIT = True
-STAGE = True
+BIG = 16384.0
 LOADS = "Sx Yy Se Ya Yb Ys"
-Y_B_FIRST = False
-STEPS = ["i_f", "c_m", "k_b", "c_d", "h_f", "k_1", "j_n", "j_o", "j_f", "c_e", "y_b"]
-ORDER = ["early", "w0n", "w0f", "s0", "img", "rv", "w1n", "k1", "s1", "imgn", "jb"]
-WAYS = {"early": "1L 0S", "w0f": "1L 0S", "s0": "0A", "img": "1L 0S", "rv": "0A", "s1": "0A", "k1": "1L 0S"}
-MORE = {"g_o": 0, "i_o": 0, "k_o": 0, "h_n": 0, "h_f": 0, "k_b": 0, "j_n": 0, "j_f": 0}
-HELD = {"early": 0, "w0f": 128, "img": 512, "rv": 1024, "k1": 1152, "s0": 0, "s1": 32}
-SCRATCH = {
-    "vi": ("sbuf", [128, 128], I32), "xr": ("sbuf", [128, 160], BF), "r2": ("sbuf", [128, 4, 64], BF),
-    "pcol": ("sbuf", [128, 1], I32), "bi": ("sbuf", [128, 4], I32),
-    "bf": ("sbuf", [128, 12], F32), "wrap": ("sbuf", [128, 4], F32), "zero": ("sbuf", [128, 512], BF),
-    "lt": ("sbuf", [128, 2, 144], BF), "sel": ("sbuf", [128, 144], BF), "spr": ("sbuf", [128, 144], BF),
-    "wsf": ("sbuf", [128, 384], BF), "wsn": ("sbuf", [128, 128], BF), "tb": ("sbuf", [128, 64], F32),
-    "s0": ("sbuf", [128, 24], U16), "s1": ("sbuf", [128, 24], U16), "heldl": ("sbuf", [128, 64], U16),
-    "l0": ("sbuf", [128, 192], U16), "l0b": ("sbuf", [128, 192], U16),
-    "l1n": ("sbuf", [128, 192], U16), "l1f": ("sbuf", [128, 192], U16), "l2": ("sbuf", [128, 192], U16),
-    "w0": ("sbuf", [128, 3072], BF), "w1": ("sbuf", [128, 3072], BF), "w2": ("sbuf", [128, 3072], BF),
-    "pic": ("sbuf", [128, 3072], BF), "i1": ("sbuf", [128, 3072], BF), "k1": ("sbuf", [128, 3072], BF),
-    "jb": ("sbuf", [128, 3072], BF), "yo": ("sbuf", [128, 3072], BF), "held": ("sbuf", [128, 2048], BF),
-    "stage": ("dram", [2, 128, (512 - EARLY) // 2], BF),
-    "cx": ("psum", [128, 512], F32), "blk": ("psum", [128, 16, 32], F32), "psf": ("psum", [128, 512], F32),
-    "psn": ("psum", [128, 512], F32), "po": ("psum", [128, 512], F32), "pm": ("psum", [128, 512], F32),
-    "pa": ("psum", [128, 512], F32), "pf": ("psum", [128, 512], F32),
+FARIMG = 2
+SPREAD = {"0": (8, 10, "S", "ws"), "1": (15, 16, "S", "ws")}
+FRONT = "1 l 0"
+KEEP_AFTER = "1"
+EDGE_FIRST = "A"
+OWN_QUEUES = "YS"
+EARLY_DRAM = False
+SPLIT_DG = False
+OWN_DMA = True
+GATHERS = {
+    "ia": ("i1", "pic", 0, (9, 11), (8, 16), "own"),
+    "io": ("i1", "pic", 0, (11, 15), (8, 16), "own"),
+    "go": ("w1", "w0", 0, (9, 12), (8, 16), "w0"),
+    "gn": ("w1", "w0", 0, (12, 16), (11, 17), "w0 w0n"),
+    "ko": ("k1", "i1", 0, (10, 14), (9, 15), "io ia"),
+    "hn": ("w2", "w1", 1, (12, 16), (10, 18), "go gn w1n"),
+    "ha": ("w2", "w1", 1, (9, 12), (7, 14), "go gn gf"),
+    "gf": ("w1", "w0", 0, (7, 9), (6, 10), "w0 s0 w0f"),
+    "if": ("i1", "pic", 0, (7, 9), (6, 10), "own s0 early img ko"),
+    "kb": ("k1", "i1", 0, (6, 10), (5, 11), "io ia if i1f s0"),
+    "hf": ("w2", "w1", 1, (8, 9), (6, 11), "go gf rv"),
+    "jn": ("jb", "pic", 2, (12, 16), (8, 20), "own imgn"),
+    "jo": ("jb", "k1", 1, (9, 12), (7, 14), "ko kb"),
+    "jf": ("jb", "k1", 1, (4, 9), (2, 11), "ko kb k1f s1"),
+    "ya": ("yo", "jb", 2, (8, 12), (4, 16), "jn jo jf"),
+    "yb": ("yo", "jb", 2, (12, 16), (8, 20), "jn jo jbn"),
 }
-FAR = ["early", "w0f", "s0", "img", "rv", "s1", "k1"]
-SEMAPHORES = ["vc", "gi", "gx", "g2", "ldy", "ldx", "lde", "lda", "ldb", "ms", "fill", "fill2", "sel", "va", "vb", "lt",
-              "spr", "dg", "t_b", "t_sf", "t_sn", "c_sf", "c_sn", "c_0", "lo", "lob", "rs_o", "g_o", "g_e", "g_n", "g_f",
-              "i_o", "i_f", "h_n", "h_e", "h_f", "h_8", "k_o", "k_b", "j_n", "j_f", "j_o", "y_a", "y_b", "t_o", "t_m", "t_a",
-              "t_f", "c_s", "c_o", "c_m", "c_7", "c_d", "c_e", "lds", "vir0", "vir1", "pv", "w0n", "w1n", "imgn", "jb", "sent", "sty_a",
-              "sty_b", "rsent"] + FAR + ["at_" + x for x in FAR]
-N0 = 3 if FAR3 else 2
-NL0 = 3 if FARI else N0 - 1
-NL1 = 2 if FAR3 else 3
+STARTS = {True: {"gn": 8, "ko": 8, "gf": 5, "if": 5, "hf": 2},
+          False: {"ko": 16, "gf": 16, "if": 16, "kb": 16, "jf": 14, "hf": 14}}
+FILLS = {True: [("i1", 8, 9), ("w0", 5, 6), ("pic", 5, 6), ("w1", 2, 6)], False: [("i1", 15, 16)]}
+PICKS = {"N": (1, (12, 16), "pa", "gn", 1), "O": (1, (9, 12), "pb", "go", 1), "M": (1, (7, 9), "cx", "gf", 2),
+         "A": (2, (12, 16), "pc", "hn", 1), "F": (2, (8, 12), "sp2", "hf ha", 1)}
+STEPS = "l0io s0 l0 ia gn N io go O ko lN gf M hn A if s1 lO kM kb lM ha lA hf F jn jo jf lF ya yb"
+EDGE_GATHERS = {
+    "go": ("w1", "w0", 0, (8, 12), (7, 13), "w0 v0"),
+    "gn": ("w1", "w0", 0, (12, 16), (11, 17), "w0 w0n v0"),
+    "hn": ("w2", "w1", 1, (12, 16), (10, 18), "go gn w1n"),
+    "hf": ("w2", "w1", 1, (8, 12), (6, 14), "go gn v1"),
+    "jn": ("jb", "pic", 2, (12, 16), (8, 20), "own imgn"),
+    "jo": ("jb", "pic", 2, (8, 12), (0, 16), "own vp"),
+    "jf": ("jb", "pic", 2, (4, 8), (0, 12), "own vp"),
+    "ya": ("yo", "jb", 2, (8, 12), (0, 16), "jn jo jf"),
+    "yb": ("yo", "jb", 2, (12, 16), (8, 20), "jn jo jbn"),
+}
+EDGE_STARTS = {True: {"gn": 7}, False: {"jf": 16}}
+EDGE_FILLS = {True: [("jb", 0, 4)], False: [("jb", 0, 4)]}
+EDGE_PICKS = {"N": (1, (12, 16), "pa", "gn", 1), "O": (1, (8, 12), "pb", "go", 1),
+              "A": (2, (12, 16), "pc", "hn", 1), "F": (2, (8, 12), "sp2", "hf", 1)}
+EDGE_STEPS = "l0 v0 gn N go O vp lN v1 hn A lO hf F lA jn lFjo lF jo jf yb ya"
+SENDS = {"early": ("pic", None, "lde", "1L 0S"), "w0n": ("w0", (15, 16), "c_sp1", "A"), "w0f": ("w0", (8, 10), "c_sp0", "1L 0S"),
+         "s0": ("00", (8, 10), "c_s0", "1L"), "img": ("pic", None, "lds", "1L 0S"), "i1f": ("i1", (9, 11), "g_ia", "1L 0S"),
+         "rv": ("w1", (9, 10), "g_go", "0A"), "w1n": ("w1", (14, 16), "g_gn", "S"), "k1f": ("k1", (10, 14), "g_ko", "1L 0S"),
+         "s1": ("1O", (9, 12), "c_s1", "1L"), "imgn": ("pic", (12, 16), "lda ldb", "S"), "jbn": ("jb", (12, 16), "g_jn", "A")}
+ORDER = "early w0n w0f s0 img i1f w1n imgn rv k1f s1 jbn"
+USER = {"s0": "kb", "s1": "jf"}
+MORE = {"kb": -4}
+EDGE_MORE = {}
+GATHERS.pop("ia")
+GATHERS.pop("ha")
+GATHERS.update({'io': ('i1', 'pic', 0, (9, 15), (8, 16), 'own'), 'gn': ('w1', 'w0', 0, (14, 16), (13, 17), 'w0 w0n'), 'ko': ('k1', 'i1', 0, (10, 14), (9, 15), 'io'), 'hn': ('w2', 'w1', 1, (12, 16), (10, 18), 'go ga gn w1n'), 'kb': ('k1', 'i1', 0, (6, 10), (5, 11), 'io if i1f s0'), 'hf': ('w2', 'w1', 1, (8, 12), (6, 14), 'go ga gf rv'), 'jo': ('jb', 'k1', 1, (8, 12), (6, 14), 'ko kb'), 'jf': ('jb', 'k1', 1, (4, 8), (2, 10), 'ko kb k1f s1'), 'ga': ('w1', 'w0', 0, (12, 14), (8, 16), 'w0')})
+STARTS = {True: {'gn': 8, 'ko': 8, 'gf': 5, 'if': 5}, False: {'ko': 16, 'gf': 16, 'if': 16, 'kb': 16, 'jf': 14}}
+FILLS = {True: [('i1', 8, 9), ('w0', 5, 6), ('pic', 5, 6)], False: [('i1', 15, 16)]}
+PICKS = {'N': (1, (12, 16), 'pa', 'ga gn', 1), 'O': (1, (9, 12), 'pb', 'go', 1), 'M': (1, (7, 9), 'cx', 'gf', 1), 'A': (2, (12, 16), 'pc', 'hn', 1), 'F': (2, (8, 12), 'sp2', 'hf', 1)}
+EDGE_GATHERS.update({'gn': ('w1', 'w0', 0, (14, 16), (13, 17), 'w0 w0n'), 'hn': ('w2', 'w1', 1, (12, 16), (10, 18), 'go ga gn w1n'), 'hf': ('w2', 'w1', 1, (8, 12), (6, 14), 'go ga v1'), 'ga': ('w1', 'w0', 0, (12, 14), (11, 15), 'w0')})
+EDGE_PICKS['N'] = PICKS['N']
+SENDS = {'early': ('pic', None, 'lde', '1L1 0S1'), 'w0n': ('w0', (15, 16), 'c_sp1', 'A'), 'w0f': ('w0', (8, 10), 'c_sp0', '1L 0S'), 's0': ('00', (8, 10), 'c_s0', '0A'), 'img': ('pic', None, 'lds', '1L1 0S1'), 'i1f': ('i1', (9, 11), 'g_io', '1L 0S'), 'rv': ('w1', (9, 10), 'g_go', '1L'), 'w1n': ('w1', (14, 16), 'g_gn', 'A'), 'k1f': ('k1', (10, 14), 'g_ko', '1L 0S'), 's1': ('1O', (9, 12), 'c_s1', '0A'), 'imgn': ('pic', (12, 16), 'lda ldb', 'A'), 'jbn': ('jb', (12, 16), 'g_jn', 'A')}
+EDGE_STARTS = {True: {'gn': 8, 'ga': 8}, False: {'ga': 16, 'go': 16, 'jf': 16}}
+STEPS = 'l0io s0 l0 io ga gn N go O ko lN hn A s1 lO gf M if lA jn lM kb hf F jo jf lF yb ya'
+EDGE_STEPS = 'l0 vp v0 ga gn N go O lN v1 hn A lO hf F lA jn lFjo lF jo jf yb ya'
+ORDER = 'early w0n w0f s0 img i1f w1n rv imgn k1f s1 jbn'
+MORE = {'jn': -2, 'gf': -2}
+SPLIT_DG = True
+EARLY_DRAM = True
+LOADS = 'Sx Yy Se Yf Ya Yb Ys'
+WIDE = ["w0", "w1", "w2", "pic", "i1", "k1", "jb", "yo"]
+SCRATCH = {
+    "vi": ("sbuf", [128, 128], I32), "xr": ("sbuf", [128, 160], BF), "r2": ("sbuf", [128, 128], BF),
+    "pcol": ("sbuf", [128, 1], I32), "bi": ("sbuf", [128, 4], I32), "dig": ("sbuf", [128, 128], BF),
+    "bf": ("sbuf", [128, 16], F32), "wrap": ("sbuf", [128, 4], F32), "zero": ("sbuf", [128, 144], BF),
+    "lt": ("sbuf", [128, 2, 144], BF), "sel": ("sbuf", [128, 2, 144], BF), "spr": ("sbuf", [128, 144], BF),
+    "keep": ("sbuf", [128, 64], F32), "kept": ("sbuf", [128, 8, 64], F32),
+    "tb": ("sbuf", [128, 64], F32), "ws": ("sbuf", [128, 3072], BF),
+    "s0n": ("sbuf", [128, 32], U16), "s0": ("sbuf", [128, 32], U16), "s1": ("sbuf", [128, 32], U16), "heldl": ("sbuf", [128, 64], U16),
+    "l0": ("sbuf", [128, 960], U16), "l1": ("sbuf", [128, 960], U16), "l2": ("sbuf", [128, 960], U16),
+    "held": ("sbuf", [128, 4096], BF), "stage": ("dram", [2, 128, (128 * FARIMG - EARLY) // 2], BF),
+    "stage0": ("dram", [2, 128, EARLY // 2], BF),
+    "cx": ("psum", [128, 512], F32), "blk": ("psum", [128, 16, 32], F32), "sp0": ("psum", [128, 512], F32),
+    "sp1": ("psum", [128, 512], F32), "sp2": ("psum", [128, 512], F32), "pa": ("psum", [128, 512], F32),
+    "pb": ("psum", [128, 512], F32), "pc": ("psum", [128, 512], F32),
+}
+SCRATCH.update({x: ("sbuf", [128, 3072], BF) for x in WIDE})
+NAMES = ["early", "w0n", "w0f", "s0", "img", "i1f", "rv", "w1n", "k1f", "s1", "imgn", "jbn", "k1g", "s0n", "k1n"]
+SEMAPHORES = (["vc", "gi", "gx", "g2", "ldy", "ldx", "lde", "lda", "ldb", "lds", "ms", "sel", "va", "vb", "lt", "spr", "dg",
+               "t_b", "c_s0", "c_s1", "sent", "rsent", "sty_ya", "sty_yb", "sty_yc", "fill", "fill2", "rs_o", "keep",
+               "sc", "vl", "wr", "ve", "hi", "kp", "tr", "wt", "c4", "c5", "v7", "v6", "dy"]
+              + NAMES + ["at_" + x for x in NAMES if x[-1] != "n"] + ["c_s0n"]
+              + ["g_" + x for x in "io ia in go ga gn ko kn ka ha hn gf if kb hf jn jo jf jc ya yb yc v0 v1 vp".split()]
+              + [y + x for x in "NOMAF" for y in ("t_", "k_")] + [y + x for x in "012" for y in ("t_sp", "c_sp")]
+              + ["l_%s%d" % (x, k) for x in "0NOMAF" for k in range(5)])
 
 
 def plan(T, topo):
@@ -79,29 +139,41 @@ def turned(up, a, b):
     return (a, b) if up else (24 - b, 24 - a)
 
 
-def low_row(up, edge):
-    return (4 if FARI else 8 - N0) if up and not edge else 7
+def window(name, up, edge):
+    a, b = (EDGE_GATHERS if edge else GATHERS)[name][4]
+    x = (EDGE_STARTS if edge else STARTS)[up].get(name)
+    return turned(up, *((a, b) if x is None else (x, b) if up else (a, x)))
+
+
+def place(name, up, edge):
+    gathers = EDGE_GATHERS if edge else GATHERS
+    starts = sorted({window(x, up, edge)[0] for x in gathers if gathers[x][2] == gathers[name][2]})
+    return 192 * starts.index(window(name, up, edge)[0])
+
+
+def is_far(name):
+    return SENDS[name][3][0] in "0123"
 
 
 def landing(T, name, up):
-    def at(t, a, b, w=128):
-        a, b = turned(up, a, b)
-        return t, w * a, w * (b - a)
-    if name in ("early", "img"):
-        c = at(T.pic, 4, 8)[1]
-        return (T.pic, c, EARLY) if name == "early" else (T.pic, c + EARLY, 512 - EARLY)
-    return {"w0f": at(T.w0, 8 - N0, 8), "s0": at(T.l0b if up else T.l0, 8 - NL0, 8, 8), "rv": at(T.w1, 6, 7),
-            "s1": at(T.l1f, 4, 4 + NL1, 8), "k1": at(T.k1, 2, 6)}[name]
-
-
-def messages():
-    return [x for x in ORDER if not (x == "rv" and FAR3) and not (x == "early" and not EARLY)]
+    t, rr = SENDS[name][:2]
+    if rr is None:
+        c = 128 * turned(up, 8 - FARIMG, 8)[0]
+        return (T.pic, c, EARLY) if name == "early" else (T.pic, c + EARLY, 128 * FARIMG - EARLY)
+    a, b = turned(up, 16 - rr[1], 16 - rr[0])
+    if name in USER:
+        return T["l" + t[0]], place(USER[name], up, False) + 8 * a, 8 * (b - a)
+    return T[t], 128 * a, 128 * (b - a)
 
 
 def held(T, name, n):
-    if name == "img" and STAGE:
+    if name == "img":
         return T.stage[0]
-    return (T.heldl if name in ("s0", "s1") else T.held)[:, HELD[name]:HELD[name] + n]
+    if name == "early" and EARLY_DRAM:
+        return T.stage0[0]
+    before = [x for x in SENDS if is_far(x) and x != "img" and (x in USER) == (name in USER)]
+    c = sum(landing(T, x, True)[2] for x in before[:before.index(name)])
+    return (T.heldl if name in USER else T.held)[:, c:c + n]
 
 
 def rank_program(g, core, T, topo):
@@ -118,7 +190,8 @@ def rank_program(g, core, T, topo):
     edge = fb is None
     V, S, TE, SY = g.vector, g.scalar, g.tensor, g.sync
     top = 8 * r
-    cnt = {}
+    gathers, picks, steps, fills = (EDGE_GATHERS, EDGE_PICKS, EDGE_STEPS, EDGE_FILLS) if edge else (GATHERS, PICKS, STEPS, FILLS)
+    cnt, seen, made = {}, set(), {}
 
     def R(a, b):
         return turned(up, a, b)
@@ -127,406 +200,366 @@ def rank_program(g, core, T, topo):
         a, b = R(a, b)
         return t[:, 128 * a:128 * b]
 
-    def v(ins, name="vc"):
-        ins.then_inc(sem[name], 1)
-        cnt[name] = cnt.get(name, 0) + 1
+    def v(ins, name="vc", n=1):
+        ins.then_inc(sem[name], n)
+        cnt[name] = cnt.get(name, 0) + n
 
-    def vs():
-        V.wait_ge(sem.vc, cnt["vc"])
+    def wait(q, name, k=None):
+        k = cnt[name] if k is None else k
+        key = ([x is q for x in (V, S, TE, SY, g)].index(True), name, k)
+        if key not in seen:
+            seen.add(key)
+            q.wait_ge(sem[name], k)
 
     def ts(out, in0, s1, op0, s2=None, op1=None):
         if op1 is None:
             return V.tensor_scalar(out=out, in0=in0, scalar1=s1, scalar2=None, op0=op0)
         return V.tensor_scalar(out=out, in0=in0, scalar1=s1, scalar2=s2, op0=op0, op1=op1)
 
-    def both(name, k):
-        V.wait_ge(sem[name], k)
-        S.wait_ge(sem[name], k)
+    def both(name, k=None):
+        wait(V, name, k)
+        wait(S, name, k)
 
-    fa, na = 128 * R(8, 12)[0], 128 * R(12, 16)[0]
-    first = EARLY if OWN_LOAD and not edge else 0
-
-    def load(q, a, b, name):
-        q.dma_start(out=T.pic[:, a:b], in_=T.img[:, a - 1024:b - 1024]).then_inc(sem[name], 16)
+    first = 0 if EARLY_DRAM and not edge else EARLY
+    fa = 128 * (R(*SENDS["imgn"][1]) if edge else R(8, 8 + FARIMG))[0] - 1024
+    cuts = [(0, fa), (fa + first, 1024)] if fa and first else [(first, 1024), (1024, 1024)]
     for x in LOADS.split():
         q = S if x[0] == "S" else SY
         if x[1] == "x":
-            q.dma_start(out=T.vi[64:128], in_=T.vx[:]).then_inc(sem.ldx, 16)
+            v(q.dma_start(out=T.vi[64:128], in_=T.vx[:]), "ldx", 16)
         elif x[1] == "y":
-            q.dma_start(out=T.vi[0:64], in_=T.vy[:]).then_inc(sem.ldy, 16)
-        elif x[1] == "e" and first:
-            load(q, fa, fa + first, "lde")
-        elif x[1] == "a":
-            load(q, fa + first, fa + 512, "lda")
-        elif x[1] == "b":
-            load(q, na, na + 512, "ldb")
-        elif x[1] == "s" and STAGE and not edge:
-            n = (512 - EARLY) // 2
+            v(q.dma_start(out=T.vi[0:64], in_=T.vy[:]), "ldy", 16)
+        elif x[1] in "ef" and not first:
+            k = "ef".index(x[1])
+            c = fa + k * EARLY // 2
+            v(q.dma_start(out=T.stage0[k], in_=T.img[:, c:c + EARLY // 2]), "lde", 16)
+        elif x[1] == "e":
+            v(q.dma_start(out=T.pic[:, 1024 + fa:1024 + fa + first], in_=T.img[:, fa:fa + first]), "lde", 16)
+        elif x[1] in "ab":
+            a, b = cuts["ab".index(x[1])]
+            if a < b:
+                v(q.dma_start(out=T.pic[:, 1024 + a:1024 + b], in_=T.img[:, a:b]), "ld" + x[1], 16)
+        elif x[1] == "s" and not edge and "img" in SENDS:
+            n = (128 * FARIMG - EARLY) // 2
             for k in range(2):
-                c = fa - 1024 + EARLY + k * n
-                q.dma_start(out=T.stage[k], in_=T.img[:, c:c + n]).then_inc(sem.lds, 16)
-
-    def images(q):
-        for name in ("lde", "lda", "ldb")[0 if first else 1:]:
-            q.wait_ge(sem[name], 16)
+                c = fa + EARLY + k * n
+                v(q.dma_start(out=T.stage[k], in_=T.img[:, c:c + n]), "lds", 16)
 
     def iota(out, pattern, base, cm, name):
         g.iota(out=out, pattern=pattern, base=base, channel_multiplier=cm,
                allow_small_or_imprecise_dtypes=True).then_inc(sem[name], 1)
     iota(T.pcol[:], [[1, 1]], 0, 1, "gi")
     iota(T.xr[:, 0:145], [[1, 145]], -1, 0, "gx")
-    iota(T.r2[:], [[1, 256]], -3, 0, "g2")
+    iota(T.r2[:], [[64, 4], [1, 32]], -3, 0, "g2")
     v(V.memset(T.zero[:], 0.0), "ms")
+    v(V.memset(T.w0[:, 1024:1536], 0.0), "fill")
     S.wait_ge(sem.ms, 1)
-    low = low_row(up, edge)
+    RC, WT, KP, W0, WP, C4, C5, HI, LO, K1 = range(10)
+
+    def bf(k, h=slice(0, 128)):
+        return T.bf[h, k:k + 1]
+
+    def const(out, like, bias, name, scale=1.0):
+        v(S.activation(out=out, in_=like, func=F.Identity, bias=bias, scale=scale), name)
 
     def fill(name, todo):
         for t, a, b in todo:
-            S.activation(out=t[:, 128 * a:128 * b], in_=T.zero[:, 0:128 * (b - a)], func=F.Copy).then_inc(sem[name], 1)
-    fills = []
-    if up:
-        fills = [(T.jb, 0, 4)] if edge else ([] if SPLIT else [(T.w1, 2, 6)]) + (
-            [(T.w0, 4, 8 - N0), (T.i1, 4, 5)] if FARI else [(T.pic, 2, 4)])
-    fill("fill", [(T.w0, 8, 12), (T.w0, 12, 16)])
-    S.activation(out=T.lt[:, :, 128:144], in_=T.zero[:, 0:32], func=F.Copy).then_inc(sem.lt, 1)
-    RC, WT, K1, K2, P15, KP, W0, WP, C4 = range(9)
-
-    def bf(k):
-        return T.bf[:, k:k + 1]
+            v(V.memset(rows(T[t], a, b), 0.0), name)
+    ys, xs = slice(0, 64), slice(64, 128)
     q16 = T.bi[:, 1:2]
+    const(T.lt[:, :, 128:144], T.zero[:, 0:32], 0.0, "lt")
+    const(bf(WT, ys), T.zero[ys, 0:1], 128.0, "wt")
+    const(bf(WT, xs), T.zero[xs, 0:1], 1.0, "wt")
     V.wait_ge(sem.gi, 1)
-    v(ts(T.bi[:, 0:1], T.pcol[:], 7, A.bitwise_and), "va")
-    v(ts(T.bi[:, 2:3], T.pcol[:], 63, A.bitwise_and), "va")
-    v(V.memset(T.wrap[0:64, 0:2], 0.0))
-    v(V.memset(T.bf[0:64, WT:WT + 1], 128.0))
-    v(V.memset(T.bf[64:128, WT:WT + 1], 1.0))
-    V.wait_ge(sem.va, 2)
+    for k, x, op, s in ((0, 7, A.bitwise_and, "v7"), (2, 63, A.bitwise_and, "v6"), (1, 15, A.bitwise_and, "va"),
+                        (3, 4, A.arith_shift_right, "va")):
+        v(ts(T.bi[:, k:k + 1], T.pcol[:], x, op), s)
+    wait(V, "v7")
     v(ts(bf(RC), T.bi[:, 0:1], float(top + 8), A.add), "vb")
-    v(ts(bf(C4), T.bi[:, 2:3], 4.0, A.mult), "vb")
-    V.wait_ge(sem.gx, 1)
-    v(V.tensor_copy(out=T.cx[64:128, 0:128], in_=T.xr[64:128, 1:129]))
-    V.wait_ge(sem.vb, 2)
-    V.wait_ge(sem.ms, 1)
-    v(ts(T.cx[0:64, 0:128], T.zero[0:64, 0:128], T.bf[0:64, RC:RC + 1], A.add))
-    for c in range(2):
-        h = slice(64 * c, 64 * c + 64)
-        v(ts(T.spr[h], T.xr[h, 1 - c:145 - c], 2.0, A.mult, T.bf[h, C4:C4 + 1], A.is_equal), "spr")
-
-    dig = T.i1[:, 1024:1152]
-    V.wait_ge(sem.ldx, 16)
-    v(ts(T.wrap[64:128, 0:1], T.vi[64:128, 0:1], 0.0, A.is_lt, 128.0, A.mult), "ms")
-    v(ts(T.wrap[64:128, 1:2], T.vi[64:128, 127:128], 0.0, A.is_gt, -128.0, A.mult), "ms")
-    vs()
-    V.wait_ge(sem.ldy, 16)
-    v(V.tensor_tensor(out=T.i1[:, 1025:1151], in0=T.vi[:, 1:127], in1=T.cx[:, 1:127], op=A.add), "dg")
-    V.wait_ge(sem.ms, 3)
-    for k, x in enumerate((0, 127)):
-        v(ts(T.i1[:, 1024 + x:1025 + x], T.vi[:, x:x + 1], T.cx[:, x:x + 1], A.add, T.wrap[:, k:k + 1], A.add), "dg")
-    V.wait_ge(sem.g2, 1)
-    for e in range(2):
-        v(ts(T.lt[:, e, 0:128], T.r2[:, :, 32 * e:32 * e + 32], bf(C4), A.is_equal, bf(WT), A.mult), "lt")
-    v(ts(q16, T.pcol[:], 15, A.bitwise_and))
-    v(ts(bf(P15), T.pcol[:], 15.0, A.add))
-    vs()
+    wait(V, "v6")
+    v(ts(bf(C4), T.bi[:, 2:3], 4.0, A.mult), "c4")
+    v(ts(bf(C5), T.bi[:, 2:3], 4.0, A.mult, -32.0, A.add), "c5")
+    wait(V, "va")
     v(ts(bf(W0), q16, 0.0, A.is_equal, 127.0, A.mult))
-    v(ts(bf(KP), q16, -1.0, A.mult, bf(P15), A.add))
-    if edge:
-        for k in (1, 2):
-            v(ts(bf(WT + k), q16, 0.0, A.is_equal, float(-k if up else k), A.mult))
-    vs()
+    v(ts(bf(KP), T.bi[:, 3:4], 16.0, A.mult))
+    folds = sorted({x[4] for x in picks.values()})
+    wait(S, "fill")
+    const(T.w0[:, 1536:2048], T.w0[:, 1024:1536], 0.0, "fill")
+    S.wait_ge(sem.gx, 1)
+    const(T.cx[xs, 0:128], T.xr[xs, 1:129], 0.0, "sc")
+    wait(S, "vb")
+    const(T.cx[ys, 0:128], T.zero[ys, 0:128], bf(RC, ys), "sc")
+    for k in folds:
+        const(T.sel[:, k - 1, :], T.zero[:], 0.0, "keep")
+    wait(V, "c4")
+    V.wait_ge(sem.gx, 1)
+    for c, h in enumerate((ys, xs)):
+        v(ts(T.spr[h], T.xr[h, 1 - c:145 - c], 2.0, A.mult, bf(C4, h), A.is_equal), "spr")
+
+    def first_matrix(e):
+        wait(V, "g2", 1)
+        wait(V, "wt")
+        wait(V, "c5")
+        v(ts(T.lt[:, e, 0:128], T.r2[:], bf(C4 + e), A.is_equal, bf(WT), A.mult), "lt")
+
+    V.wait_ge(sem.ldx, 16)
+    v(ts(T.wrap[xs, 0:1], T.vi[xs, 0:1], 0.0, A.is_lt, 128.0, A.mult), "wr")
+    v(ts(T.wrap[xs, 1:2], T.vi[xs, 127:128], 0.0, A.is_gt, -128.0, A.mult), "wr")
+    wait(V, "sc")
+    V.wait_ge(sem.ldy, 16)
+    v(V.tensor_tensor(out=T.dig[:, 1:127], in0=T.vi[:, 1:127], in1=T.cx[:, 1:127], op=A.add), "dy")
+    v(ts(T.dig[ys, 0:128:127], T.vi[ys, 0:128:127], bf(RC, ys), A.add), "dy")
+    wait(V, "wr")
+    for k, x in enumerate((0, 127)):
+        v(ts(T.dig[xs, x:x + 1], T.vi[xs, x:x + 1], T.cx[xs, x:x + 1], A.add, T.wrap[xs, k:k + 1], A.add), "dg")
+    first_matrix(0)
+    first_matrix(1)
+    wait(V, "vc")
     v(ts(bf(WP), q16, 1.0, A.is_le, bf(W0), A.add))
+    if 2 in folds:
+        v(ts(bf(LO), q16, 8.0, A.is_lt, BIG, A.mult), "vl")
+    fill("fill2", fills[up])
+    wait(V, "vc")
+    wait(V, "keep")
+    for k, c in [(1, 7), (1, 15)] * (2 in folds) + [(0, 15)] * (1 in folds):
+        v(ts(T.sel[:, k, c:c + 128:16], T.xr[:, 1:129:16], bf(KP), A.is_equal, bf(WP), A.mult), "sel")
+    if edge:
+        for k in range(1, 3):
+            v(ts(bf(K1 + k), q16, 0.0, A.is_equal, float(-k if up else k), A.mult), "ve")
 
-    def spread(ps, ws, a, b, x):
-        a, b = R(a, b)
-        for i in range(a, b):
-            ins = TE.matmul(ps[:, 128 * (i - a):128 * (i - a + 1)], T.spr[:, 2 * (i - 8):2 * (i - 8) + 128], dig, True, True)
-        ins.then_inc(sem["t_" + x], 1)
-        S.wait_ge(sem["t_" + x], 1)
-        n = 128 * (b - a)
-        S.activation(out=ws[:, 0:n], in_=ps[:, 0:n], func=F.Copy).then_inc(sem["c_" + x], 1)
+    def keep():
+        const(T.keep[:, 0:64:2], T.zero[:, 0:32], -2 * BIG, "kp")
+        wait(S, "vl")
+        const(bf(HI), bf(LO), -BIG, "hi", 2.0)
+        wait(S, "hi")
+        const(T.keep[:, 1:64:2], T.zero[:, 0:32], bf(HI), "kp")
+
+    for h, x in enumerate(OWN_QUEUES):
+        q = S if x == "S" else SY
+        wait(q, "fill")
+        wait(q, "dy")
+        if h or not SPLIT_DG:
+            wait(q, "dg")
+        v(q.dma_start(out=T.w0[h:128:16, 1024:2048], in_=T.dig[64 * h:64 * h + 64]), "rs_o", 16)
+
+    def copy_out(x):
+        a, b, q, t = SPREAD[x]
+        ps, n = T["sp" + x], 128 * (b - a)
+        if q == "S":
+            S.wait_ge(sem["t_sp" + x], 1)
+            v(S.activation(out=rows(T[t], a, b), in_=ps[:, 0:n], func=F.Copy), "c_sp" + x)
+        else:
+            V.wait_ge(sem["t_sp" + x], 1)
+            v(V.tensor_copy(out=rows(T[t], a, b), in_=ps[:, 0:n]), "c_sp" + x)
+
+    def listed(out, src, base, name, less=None):
+        v(ts(out, src, -128.0 * base, A.add) if less is None else ts(out, src, -128.0 * base, A.add, less, A.subtract), name)
+
+    def sums(x):
+        if x == "0":
+            wait(V, "tr")
+            return 0, (8, 16), lambda c, d: T.tb[:, 8 * (c - 8):8 * (d - 8)], None
+        level, rr, ps, _, fold = picks[x]
+        a, k = R(*rr)[0], list(picks).index(x)
+        if fold == 1:
+            wait(V, "t_" + x)
+            return level, R(*rr), lambda c, d: T[ps][:, 8 * (c - a):8 * (d - a)], None
+        if "k_" + x not in cnt:
+            picked(x)
+        wait(V, "k_" + x)
+        return level, R(*rr), lambda c, d: T.kept[:, k, 16 * (c - a) + 1:16 * (d - a):2], bf(LO)
+
+    def lists(name, users=None):
+        level, (a, b), src, less = sums(name)
+        want = {}
+        for x, gt in gathers.items():
+            if gt[2] == level:
+                c, d = R(*gt[3])
+                want.setdefault((window(x, up, edge)[0], place(x, up, edge)), set()).update(range(max(a, c), min(b, d)))
+        for (w, at), have in sorted(want.items(), key=lambda x: -len(x[1])):
+            if have and (level, at, min(have)) not in made and (not users or at == place(users, up, edge)):
+                c, d, s = min(have), max(have) + 1, "l_%s%d" % (name, at // 192)
+                listed(T["l%d" % level][:, at + 8 * c:at + 8 * d], src(c, d), top + w, s, less)
+                for i in range(c, d):
+                    made[(level, at, i)] = s
+        if name == "F" and edge and "l_F4" not in cnt and users in ("", "jf"):
+            w, at = window("jf", up, edge)[0], place("jf", up, edge)
+            for k in range(1, 5):
+                i = R(8 - k, 9 - k)[0]
+                listed(T.l2[:, at + 8 * i:at + 8 * i + 8], src(*R(8, 9)), top + w + (k if up else -k), "l_F4", less)
+                made[(2, at, i)] = "l_F4"
+
+    def for_far(name):
+        _, _, src, less = sums(SENDS[name][0][1])
+        a, b = R(*SENDS[name][1])
+        to = fb if is_far(name) else nb
+        listed(T[name][:, 0:8 * (b - a)], src(a, b), 8 * T.rank_of(to) + window(USER[name], not up, to not in far)[0],
+               "c_" + name, less)
     TE.wait_ge(sem.spr, 2)
-    TE.wait_ge(sem.dg, 3)
-    spread(T.psn, T.wsn, 15, 16, "sn")
-    TE.wait_ge(sem.lt, 3)
-    for e in range(2):
-        for u in range(4):
-            ins = TE.matmul(T.blk[:, 0:2, 16 * e:16 * e + 16], T.lt[:, e, 3 - u:131 - u],
-                            T.i1[:, 1024 + 32 * u:1056 + 32 * u], u == 0, u == 3)
-    ins.then_inc(sem.t_b, 1)
-    if not edge:
-        spread(T.psf, T.wsf, 8, 8 + N0, "sf")
-    fill("fill2", fills)
-    V.wait_ge(sem.t_b, 1)
-    for w in range(2):
-        v(V.transpose(out=T.tb[:, w:64:2], in_=T.blk[:, w, :]))
-    vs()
-    v(ts(T.l0[:, 72:128], T.tb[:, 8:64], -128.0 * (top + 8), A.add), "lo")
-    if not edge:
-        a, b = R(8, 8 + NL0)
-        there = 8 * T.rank_of(fb) + (8 if up else low_row(True, False))
-        v(ts(T.s0[:, 0:8 * NL0], T.tb[:, 8 * (a - 8):8 * (b - 8)], -128.0 * there, A.add), "c_0")
-    v(ts(T.l0b[:, 64:80], T.tb[:, 0:16], -128.0 * (top + low), A.add), "lob")
-    v(ts(T.sel[:], T.xr[:, 1:145], bf(KP), A.is_equal, bf(WP), A.mult), "sel")
+    wait(TE, "dy")
+    wait(TE, "dg")
+    front = [x for x in FRONT.split() if x == "l" or not (edge and SPREAD[x][3] == "ws" and SPREAD[x][0] == 8)]
+    for x in front:
+        if x == "l":
+            TE.wait_ge(sem.lt, 3)
+            for e in range(2):
+                for u in range(4):
+                    ins = TE.matmul(T.blk[:, 0:2, 16 * e:16 * e + 16], T.lt[:, e, 3 - u:131 - u],
+                                    T.dig[:, 32 * u:32 * u + 32], u == 0, u == 3)
+            ins.then_inc(sem.t_b, 1)
+            V.wait_ge(sem.t_b, 1)
+            for w in range(2):
+                v(V.transpose(out=T.tb[:, w:64:2], in_=T.blk[:, w, :]), "tr")
+        else:
+            a, b = R(*SPREAD[x][:2])
+            for i in range(a, b):
+                ins = TE.matmul(T["sp" + x][:, 128 * (i - a):128 * (i - a + 1)], T.spr[:, 2 * (i - 8):2 * (i - 8) + 128],
+                                T.dig[:], True, True)
+            ins.then_inc(sem["t_sp" + x], 1)
+            copy_out(x)
+        if x == KEEP_AFTER and 2 in folds:
+            keep()
 
-    es = topo.engines(core, nb)
     groups = engine_groups(topo, near, far, relays, core)
+
+    def need(y):
+        if y == "own":
+            for name in ("lda", "ldb", "lde")[:3 if first else 2]:
+                if name in cnt:
+                    both(name)
+        elif y == "w0":
+            for name in ["rs_o"] if OWN_DMA else ["c_sp" + k for k in SPREAD]:
+                both(name)
+        elif y not in SENDS:
+            both("g_" + y)
+        elif is_far(y):
+            both(y, len(SENDS[y][3].split()) * len(topo.engines(relays[(fb, core)][0], core)))
+        else:
+            both(y, len(groups[SENDS[y][3]]) + (len(groups[EDGE_FIRST]) if y == "imgn" and nb not in far else 0))
+
+    def gather(x):
+        out, win, level, rr, _, needs = gathers[x]
+        a, b = R(*rr)
+        c, d = window(x, up, edge)
+        at = place(x, up, edge)
+        for i in range(a, b):
+            if (level, at, i) in made:
+                both(made[(level, at, i)])
+            else:
+                assert R(i, i + 1)[0] >= 16 or R(i, i + 1)[0] < 16 - SENDS["s%d" % level][1][0]
+        for t, e, f in fills[up]:
+            if t == win and R(e, f)[0] < d and c < R(e, f)[1]:
+                both("fill2")
+        for y in needs.split():
+            need(y)
+        lst, m = T["l%d" % level], 4 * (a + b) + (EDGE_MORE if edge else MORE).get(x, 0)
+        win = T[win][:, 128 * c:128 * d]
+        v(V.tensor_copy(out=T[out][:, 128 * a:16 * m], in_=win.indirect(lst[:, at + 8 * a:at + m])), "g_" + x)
+        v(S.activation(out=T[out][:, 16 * m:128 * b], in_=win.indirect(lst[:, at + m:at + 8 * b]), func=F.Copy), "g_" + x)
+
+    def pick(x):
+        level, rr, ps, needs, fold = picks[x]
+        a, b = R(*rr)
+        n = 16 // fold
+        wait(TE, "sel")
+        for y in needs.split():
+            wait(TE, "g_" + y)
+        for q in range(n):
+            ins = TE.matmul(T[ps][:, 0:8 * fold * (b - a)], T.sel[:, fold - 1, n - 1 - q:n + 127 - q],
+                            T["w%d" % level][:, 128 * a + q:128 * b:n], q == 0, q == n - 1)
+        v(ins, "t_" + x)
+
+    def picked(x):
+        level, rr, ps, _, _ = picks[x]
+        n, k = 16 * (rr[1] - rr[0]), list(picks).index(x)
+        wait(V, "t_" + x)
+        wait(V, "kp")
+        v(V.tensor_tensor_scan(T.kept[:, k, 0:n], T.keep[:, 0:n], T[ps][:, 0:n], 0.0, A.add, A.max), "k_" + x)
+
+    def beyond(level):
+        win = T["w%d" % level]
+        for k in range(1, 2 ** level + 1):
+            o, i = rows(win, 8 - k, 9 - k), rows(win, 8, 9)
+            if k % 2:
+                v(ts(o, i, bf(K1 + k), A.add), "g_v%d" % level)
+            else:
+                v(S.activation(out=o, in_=i, func=F.Identity, bias=bf(K1 + k)), "g_v%d" % level)
+
+    for x in steps.split():
+        if x in gathers:
+            gather(x)
+        elif x in picks:
+            pick(x)
+        elif x[0] == "k" and x[1] in picks:
+            if picks[x[1]][4] == 2 and "k_" + x[1] not in cnt:
+                picked(x[1])
+        elif x[0] == "l":
+            lists(x[1], x[2:])
+        elif x in USER:
+            for_far(x)
+        elif x == "vp":
+            need("own")
+            for k in range(8):
+                o, i = rows(T.pic, k, k + 1), rows(T.pic, 8, 9)
+                v(V.tensor_copy(out=o, in_=i) if k % 2 else S.activation(out=o, in_=i, func=F.Copy), "g_vp")
+        else:
+            both("ve")
+            need({"v0": "w0", "v1": "go"}[x])
+            beyond(int(x[1]))
+
     sent = 0
-    ready = {"early": [("lde" if first else "lda", 16)], "w0n": [("c_sn", 1)], "w0f": [("c_sf", 1)], "s0": [("c_0", 1)],
-             "img": [("lds", 32) if STAGE else ("lda", 16)], "rv": [("g_o", 2)], "w1n": [("g_o", 2), ("g_n", 2)], "k1": [("k_o", 2)],
-             "s1": [("c_s", 1)], "imgn": [("ldb", 16)], "jb": [("j_n", 2)]}
-    source = {"early": (T.pic, fa), "img": (T.pic, fa + EARLY), "w0f": (T.wsf, 0), "s0": (T.s0, 0), "s1": (T.s1, 0),
-              "rv": (T.w1, 128 * R(9, 10)[0]), "k1": (T.k1, 1280)}
-    to_near = {"w0n": (T.w0, 15), "w1n": (T.w1, 14), "imgn": (T.pic, 12), "jb": (T.jb, 12)}
-    for name in messages():
-        if edge and name in FAR:
+    for name in ORDER.split():
+        t, rr, ready, ways = SENDS[name]
+        if edge and is_far(name) and name != "early":
             continue
-        for s, k in ready[name]:
-            g.wait_ge(sem[s], k)
-        if name in FAR:
-            t, c = source[name]
-            ways = WAYS[name].split()
-            n = landing(T, name, up)[2] // len(ways)
+        for s in ready.split() + ["lde"] * (name == "imgn"):
+            if s in cnt:
+                wait(g, s)
+        if edge and name in ("early", "imgn"):
+            c, d = (fa, fa + EARLY) if name == "early" else (fa + EARLY, fa + 128 * (rr[1] - rr[0]))
+            o = 1024 * (1 + r - T.rank_of(nb))
+            rid, pid = topo.addr(nb, core)
+            es = groups[EDGE_FIRST if name == "early" else ways]
+            g.remote_dma(T.pic[:, c + o:d + o], T.pic[:, c + 1024:d + 1024], sem.imgn, sem.sent, pid, rid, bits(es))
+            sent += len(es)
+        elif is_far(name):
+            t, c, n = landing(T, name, not up)
+            t, c = (T[name], 0) if name in USER else (t, c - 1024 * (r - T.rank_of(fb)))
+            t = T.ws if name == "w0f" and OWN_DMA else t
+            ways = ways.split()
+            n //= len(ways)
             tr = []
             for k, way in enumerate(ways):
                 rid, pid = topo.addr(relays[(core, fb)][int(way[0])], core)
                 tr.append(RemoteDMATransfer(dst_ids=[DstId(rid=rid, pnc=pid)], dma_engine_mask=bits(groups[way[1:]]),
                                             remote_sem=sem["at_" + name], dst=held(T, name, n),
-                                            src=T.stage[k] if name == "img" and STAGE else t[:, c + k * n:c + (k + 1) * n]))
+                                            src=T.stage[k] if name == "img" else T.stage0[k] if name == "early" and not first
+                                            else t[:, c + k * n:c + (k + 1) * n]))
                 sent += len(groups[way[1:]])
             g.remote_dma_fused(tr, local_sem=sem.sent)
         else:
-            t, a = to_near[name]
-            c, d = R(a, 16)
+            c, d = R(*rr)
             o = 8 * (r - T.rank_of(nb))
             rid, pid = topo.addr(nb, core)
-            g.remote_dma(t[:, 128 * (c + o):128 * (d + o)], T.wsn[:] if name == "w0n" else rows(t, a, 16), sem[name],
-                         sem.sent, pid, rid, bits(es))
-            sent += len(es)
-
-    def came(name, q=None):
-        k = len(WAYS[name].split()) * len(topo.engines(relays[(fb, core)][0], core)) if name in FAR else len(es)
-        if name in messages():
-            for x in ((V, S) if q is None else (q,)):
-                x.wait_ge(sem[name], k)
-
-    SY.wait_ge(sem.fill, 2)
-    SY.wait_ge(sem.dg, 3)
-    for h in range(2):
-        SY.dma_start(out=T.w0[h:128:16, 1024:2048], in_=T.i1[64 * h:64 * h + 64, 1024:1152]).then_inc(sem.rs_o, 16)
-
-    def part(eng, out, win, lst, a, b, name):
-        o, i = out[:, 16 * a:16 * b], win.indirect(lst[:, a:b])
-        if eng is V:
-            V.tensor_copy(out=o, in_=i).then_inc(sem[name], 1)
-        else:
-            S.activation(out=o, in_=i, func=F.Copy).then_inc(sem[name], 1)
-
-    def gather(out, win, w, lst, rr, name):
-        a, b = 8 * rr[0], 8 * rr[1]
-        m = (a + b) // 2 + MORE.get(name, 0)
-        part(V, out, win[:, 128 * w[0]:128 * w[1]], lst, a, m, name)
-        part(S, out, win[:, 128 * w[0]:128 * w[1]], lst, m, b, name)
-
-    def pick(ps, w, rr, name):
-        for q in range(16):
-            ins = TE.matmul(ps[:, 0:8 * (rr[1] - rr[0])], T.sel[:, 15 - q:143 - q], w[:, 128 * rr[0] + q:128 * rr[1]:16],
-                            q == 0, q == 15)
-        ins.then_inc(sem[name], 1)
-
-    def listed(lst, rr, ps, first, base, name, at=None):
-        at = rr[0] if at is None else at
-        v(ts(lst[:, 8 * at:8 * (at + rr[1] - rr[0])], ps[:, 8 * (rr[0] - first):8 * (rr[1] - first)], -128.0 * base,
-             A.add), name)
-
-    def side(high, n, m=10):
-        return (T.l0, (8, 16 + n)) if high else (T.l0b, (low, m))
-
-    def beyond(win, k, name):
-        v(ts(rows(win, 8 - k, 9 - k), rows(win, 8, 9), T.bf[:, WT + k:WT + k + 1], A.add), name)
-
-    ro = R(8 if edge else 9, 16)
-    fw, nw = R(6 if edge else 2, 14), R(10, 18)
-    dw, ew = R(8, 20), R(0 if edge else 4, 16)
-    ra, rb = R(12, 16), R(8, 12)
-
-    both("lo", 1)
-
-    def twice(stage):
-        if stage == 0:
-            images(V)
-            images(S)
-            gather(T.i1, T.pic, (8, 16), T.l0, (9, 15), "i_o")
-        else:
-            both("i_o", 2)
-            gather(T.k1, T.i1, (8, 15), T.l0, (10, 14), "k_o")
-    for stage in range(0 if edge else I_FIRST):
-        twice(stage)
-    both("rs_o", 32)
-    gather(T.w1, T.w0, (8, 16), T.l0, (9, 15), "g_o")
-    both("lob", 1)
-    if edge:
-        beyond(T.w0, 1, "vir0")
-        both("vir0", 1)
-        l0, w = side(not up, 1)
-        gather(T.w1, T.w0, w, l0, R(8, 9), "g_e")
-    came("w0n")
-    l0, w = side(up, 1)
-    gather(T.w1, T.w0, w, l0, R(15, 16), "g_n")
-    TE.wait_ge(sem.sel, 1)
-    TE.wait_ge(sem.g_o, 2)
-    TE.wait_ge(sem.g_n, 2)
-    if edge:
-        TE.wait_ge(sem.g_e, 2)
-    pick(T.po, T.w1, ro, "t_o")
-    if edge:
-        images(V)
-        images(S)
-        V.wait_ge(sem.g_e, 2)
-        beyond(T.w1, 1, "vir1")
-        beyond(T.w1, 2, "vir1")
-        for k in range(8):
-            o, i = rows(T.pic, k, k + 1), rows(T.pic, 8, 9)
-            if k % 2:
-                v(V.tensor_copy(out=o, in_=i), "pv")
+            if name in USER:
+                at = place(USER[name], not up, nb not in far)
+                dst, src = T["l" + t[0]][:, at + 8 * (c + o):at + 8 * (d + o)], T[name][:, 0:8 * (d - c)]
             else:
-                S.activation(out=o, in_=i, func=F.Copy).then_inc(sem.pv, 1)
-    else:
-        for stage in range(I_FIRST, 2 if K_SHADOW else 1):
-            twice(stage)
-    V.wait_ge(sem.t_o, 1)
-    if not edge:
-        listed(T.s1, R(12 - NL1, 12), T.po, ro[0], 8 * T.rank_of(fb) + turned(not up, 2, 14)[0], "c_s", 0)
-    listed(T.l1n, ra, T.po, ro[0], top + nw[0], "c_o")
-    split = SPLIT and not edge
-    l1m, mw = (T.l1n if up else T.l1f, R(6, 14)) if split else (T.l1f, fw)
-    listed(l1m, R(8 if edge else 9, 12), T.po, ro[0], top + mw[0], "c_o")
-    if fills:
-        both("fill2", len(fills))
+                dst, src = T[t][:, 128 * (c + o):128 * (d + o)], rows(T.ws if name == "w0n" and OWN_DMA else T[t], *rr)
+            g.remote_dma(dst, src, sem[name], sem.sent, pid, rid, bits(groups[ways]))
+            sent += len(groups[ways])
 
-    def near_rows():
-        both("c_o", 2)
-        both("g_o", 2)
-        both("g_n", 2)
-        came("w1n")
-        gather(T.w2, T.w1, nw, T.l1n, ra, "h_n")
-        TE.wait_ge(sem.h_n, 2)
-        pick(T.pa, T.w2, ra, "t_a")
-
-    def shared():
-        both("c_d", 1)
-        came("imgn")
-        gather(T.jb, T.pic, dw, T.l2, ra, "j_n")
-    if edge:
-        near_rows()
-        both("vir1", 2)
-        both("g_e", 2)
-        gather(T.w2, T.w1, fw, T.l1f, rb, "h_e")
-        TE.wait_ge(sem.h_e, 2)
-        pick(T.pf, T.w2, rb, "t_f")
-        V.wait_ge(sem.t_a, 1)
-        listed(T.l2, ra, T.pa, ra[0], top + dw[0], "c_d")
-        shared()
-        V.wait_ge(sem.t_f, 1)
-        listed(T.l2, rb, T.pf, rb[0], top + ew[0], "c_e")
-        for k in range(1, 5):
-            listed(T.l2, R(8, 9), T.pf, rb[0], top + ew[0] + (k if up else -k), "c_e", R(8 - k, 9 - k)[0])
-        both("c_e", 5)
-        both("pv", 8)
-        gather(T.jb, T.pic, ew, T.l2, R(4, 12), "j_f")
-    else:
-        if not K_SHADOW and I_FIRST < 2:
-            twice(1)
-        if H_FIRST:
-            near_rows()
-        l0, w = side(not up, N0)
-        rm = R(9 - N0, 9)
-        came("s0")
-        came("w0f")
-        gather(T.w1, T.w0, w, l0, rm, "g_f")
-        TE.wait_ge(sem.g_f, 2)
-        pick(T.pm, T.w1, rm, "t_m")
-        if not H_FIRST:
-            near_rows()
-        hw, iw = (mw, (2, 12)) if up else (R(6, 14), R(4, 14))
-
-        def step(x):
-            if x == "i_f" and FARI:
-                came("early")
-                came("img")
-                both("k_o", 2)
-                V.wait_ge(sem.t_sf, 1)
-                gather(T.i1, T.pic, side(not up, 4)[1], l0, R(5, 9), "i_f")
-            elif x == "c_m":
-                V.wait_ge(sem.t_m, 1)
-                if split and up:
-                    listed(l1m, (8, 9), T.pm, rm[0], top + mw[0], "c_m")
-                    listed(T.l1f, (rm[0], 8), T.pm, rm[0], top + fw[0], "c_7")
-                else:
-                    listed(T.l1f, rm, T.pm, rm[0], top + fw[0], "c_m")
-            elif x == "k_b" and FARI:
-                both("i_f", 2)
-                gather(T.k1, T.i1, side(not up, 3, 11)[1], l0, R(6, 10), "k_b")
-            elif x == "c_d":
-                V.wait_ge(sem.t_a, 1)
-                listed(T.l2, ra, T.pa, ra[0], top + dw[0], "c_d")
-            elif x == "h_f":
-                both("g_f", 2)
-                came("rv")
-                both("c_m", 1)
-                gather(T.w2, T.w1, hw, l1m, rb, "h_f")
-                TE.wait_ge(sem.h_f, 2)
-                pick(T.pf, T.w2, rb, "t_f")
-            elif x == "k_1" and not FARI:
-                came("s1")
-                came("early")
-                came("img")
-                gather(T.k1, T.pic, iw, T.l1f, R(6, 10), "k_b")
-            elif x == "j_n":
-                shared()
-            elif x == "j_o" and split:
-                both("k_o", 2)
-                both("k_b", 2)
-                both("c_m", 1)
-                gather(T.jb, T.k1, mw, l1m, rb, "j_o")
-            elif x == "c_e":
-                V.wait_ge(sem.t_f, 1)
-                listed(T.l2, rb, T.pf, rb[0], top + ew[0], "c_e")
-            elif x == "j_f":
-                both("k_o", 2)
-                both("k_b", 2)
-                both("c_m", 1)
-                if split and up:
-                    both("c_7", 1)
-                came("s1")
-                came("k1")
-                gather(T.jb, T.k1, fw, T.l1f, R(4, 8 if split else 12), "j_f")
-            elif x == "y_b" and Y_B_FIRST:
-                both("j_o", 2)
-                both("j_n", 2)
-                came("jb")
-                gather(T.yo, T.jb, dw, T.l2, ra, "y_b")
-        for x in STEPS:
-            step(x)
-        both("c_e", 1)
-        if split:
-            both("j_o", 2)
-    both("j_f", 2)
-    both("j_n", 2)
-    pieces = ((rb, ew if up else R(4, 16), "a"), (ra, dw, "b"))
-    for rr, w, x in pieces:
-        if x == "b":
-            if Y_B_FIRST and not edge:
-                pieces = pieces[::-1]
-                break
-            came("jb")
-        gather(T.yo, T.jb, w, T.l2, rr, "y_" + x)
-    for rr, w, x in pieces:
-        SY.wait_ge(sem["y_" + x], 2)
-        SY.dma_start(out=T.y[:, 128 * (rr[0] - 8):128 * (rr[1] - 8)], in_=T.yo[:, 128 * rr[0]:128 * rr[1]]).then_inc(
-            sem["sty_" + x], 16)
+    last = [x for x in steps.split() if x[0] == "y"]
+    for x in last:
+        a, b = R(*gathers[x][3])
+        wait(SY, "g_" + x)
+        v(SY.dma_start(out=T.y[:, 128 * (a - 8):128 * (b - 8)], in_=T.yo[:, 128 * a:128 * b]), "sty_" + x, 16)
     g.wait_ge(sem.sent, sent)
-    for rr, w, x in pieces:
-        SY.wait_ge(sem["sty_" + x], 16)
+    for x in last:
+        wait(SY, "sty_" + x)
+    for x in cnt:
+        if not any(k[1] == x and k[2] == cnt[x] for k in seen) and x[:2] in ("l_", "ld", "g_", "vc", "fi"):
+            wait(SY, x)
 
 
 def engine_groups(topo, near, far, relays, core):
@@ -544,8 +577,8 @@ def hand_on(g, core, T, topo, s, d, i, up):
     rid, pid = topo.addr(d, core)
     groups = engine_groups(topo, *plan(T, topo), s)
     sent = 0
-    for name in messages():
-        ways = WAYS.get(name, "").split()
+    for name in ORDER.split():
+        ways = SENDS[name][3].split() if is_far(name) else []
         for k, way in enumerate(ways):
             if int(way[0]) == i:
                 t, c, n = landing(T, name, up)

from concourse.bass import DstId, RemoteDMATransfer
from concourse.mybir import AluOpType as A, ActivationFunctionType as F

BF, F32, I32, U16 = "bfloat16", "float32", "int32", "uint16"
SIM_CORES = 256
EARLY = 64
BIG = 16384.0
LOADS = "Sx Yy Se Ya Yb Ys"
FARIMG = 2
SPREAD = {"0": (8, 10, "S", "ws"), "1": (15, 16, "S", "ws")}
FRONT = "1 l 0"
KEEP_AFTER = "1"
EDGE_FIRST = "A"
OWN_QUEUES = "YS"
EARLY_DRAM = False
SPLIT_DG = False
OWN_DMA = True
GATHERS = {
    "ia": ("i1", "pic", 0, (9, 11), (8, 16), "own"),
    "io": ("i1", "pic", 0, (11, 15), (8, 16), "own"),
    "go": ("w1", "w0", 0, (9, 12), (8, 16), "w0"),
    "gn": ("w1", "w0", 0, (12, 16), (11, 17), "w0 w0n"),
    "ko": ("k1", "i1", 0, (10, 14), (9, 15), "io ia"),
    "hn": ("w2", "w1", 1, (12, 16), (10, 18), "go gn w1n"),
    "ha": ("w2", "w1", 1, (9, 12), (7, 14), "go gn gf"),
    "gf": ("w1", "w0", 0, (7, 9), (6, 10), "w0 s0 w0f"),
    "if": ("i1", "pic", 0, (7, 9), (6, 10), "own s0 early img ko"),
    "kb": ("k1", "i1", 0, (6, 10), (5, 11), "io ia if i1f s0"),
    "hf": ("w2", "w1", 1, (8, 9), (6, 11), "go gf rv"),
    "jn": ("jb", "pic", 2, (12, 16), (8, 20), "own imgn"),
    "jo": ("jb", "k1", 1, (9, 12), (7, 14), "ko kb"),
    "jf": ("jb", "k1", 1, (4, 9), (2, 11), "ko kb k1f s1"),
    "ya": ("yo", "jb", 2, (8, 12), (4, 16), "jn jo jf"),
    "yb": ("yo", "jb", 2, (12, 16), (8, 20), "jn jo jbn"),
}
STARTS = {True: {"gn": 8, "ko": 8, "gf": 5, "if": 5, "hf": 2},
          False: {"ko": 16, "gf": 16, "if": 16, "kb": 16, "jf": 14, "hf": 14}}
FILLS = {True: [("i1", 8, 9), ("w0", 5, 6), ("pic", 5, 6), ("w1", 2, 6)], False: [("i1", 15, 16)]}
PICKS = {"N": (1, (12, 16), "pa", "gn", 1), "O": (1, (9, 12), "pb", "go", 1), "M": (1, (7, 9), "cx", "gf", 2),
         "A": (2, (12, 16), "pc", "hn", 1), "F": (2, (8, 12), "sp2", "hf ha", 1)}
STEPS = "l0io s0 l0 ia gn N io go O ko lN gf M hn A if s1 lO kM kb lM ha lA hf F jn jo jf lF ya yb"
EDGE_GATHERS = {
    "go": ("w1", "w0", 0, (8, 12), (7, 13), "w0 v0"),
    "gn": ("w1", "w0", 0, (12, 16), (11, 17), "w0 w0n v0"),
    "hn": ("w2", "w1", 1, (12, 16), (10, 18), "go gn w1n"),
    "hf": ("w2", "w1", 1, (8, 12), (6, 14), "go gn v1"),
    "jn": ("jb", "pic", 2, (12, 16), (8, 20), "own imgn"),
    "jo": ("jb", "pic", 2, (8, 12), (0, 16), "own vp"),
    "jf": ("jb", "pic", 2, (4, 8), (0, 12), "own vp"),
    "ya": ("yo", "jb", 2, (8, 12), (0, 16), "jn jo jf"),
    "yb": ("yo", "jb", 2, (12, 16), (8, 20), "jn jo jbn"),
}
EDGE_STARTS = {True: {"gn": 7}, False: {"jf": 16}}
EDGE_FILLS = {True: [("jb", 0, 4)], False: [("jb", 0, 4)]}
EDGE_PICKS = {"N": (1, (12, 16), "pa", "gn", 1), "O": (1, (8, 12), "pb", "go", 1),
              "A": (2, (12, 16), "pc", "hn", 1), "F": (2, (8, 12), "sp2", "hf", 1)}
EDGE_STEPS = "l0 v0 gn N go O vp lN v1 hn A lO hf F lA jn lFjo lF jo jf yb ya"
SENDS = {"early": ("pic", None, "lde", "1L 0S"), "w0n": ("w0", (15, 16), "c_sp1", "A"), "w0f": ("w0", (8, 10), "c_sp0", "1L 0S"),
         "s0": ("00", (8, 10), "c_s0", "1L"), "img": ("pic", None, "lds", "1L 0S"), "i1f": ("i1", (9, 11), "g_ia", "1L 0S"),
         "rv": ("w1", (9, 10), "g_go", "0A"), "w1n": ("w1", (14, 16), "g_gn", "S"), "k1f": ("k1", (10, 14), "g_ko", "1L 0S"),
         "s1": ("1O", (9, 12), "c_s1", "1L"), "imgn": ("pic", (12, 16), "lda ldb", "S"), "jbn": ("jb", (12, 16), "g_jn", "A")}
ORDER = "early w0n w0f s0 img i1f w1n imgn rv k1f s1 jbn"
USER = {"s0": "kb", "s1": "jf"}
MORE = {"kb": -4}
EDGE_MORE = {}
GATHERS.pop("ia")
GATHERS.pop("ha")
GATHERS.update({'io': ('i1', 'pic', 0, (9, 15), (8, 16), 'own'), 'gn': ('w1', 'w0', 0, (14, 16), (13, 17), 'w0 w0n'), 'ko': ('k1', 'i1', 0, (10, 14), (9, 15), 'io'), 'hn': ('w2', 'w1', 1, (12, 16), (10, 18), 'go ga gn w1n'), 'kb': ('k1', 'i1', 0, (6, 10), (5, 11), 'io if i1f s0'), 'hf': ('w2', 'w1', 1, (8, 12), (6, 14), 'go ga gf rv'), 'jo': ('jb', 'k1', 1, (8, 12), (6, 14), 'ko kb'), 'jf': ('jb', 'k1', 1, (4, 8), (2, 10), 'ko kb k1f s1'), 'ga': ('w1', 'w0', 0, (12, 14), (8, 16), 'w0')})
STARTS = {True: {'gn': 8, 'ko': 8, 'gf': 5, 'if': 5}, False: {'ko': 16, 'gf': 16, 'if': 16, 'kb': 16, 'jf': 14}}
FILLS = {True: [('i1', 8, 9), ('w0', 5, 6), ('pic', 5, 6)], False: [('i1', 15, 16)]}
PICKS = {'N': (1, (12, 16), 'pa', 'ga gn', 1), 'O': (1, (9, 12), 'pb', 'go', 1), 'M': (1, (7, 9), 'cx', 'gf', 1), 'A': (2, (12, 16), 'pc', 'hn', 1), 'F': (2, (8, 12), 'sp2', 'hf', 1)}
EDGE_GATHERS.update({'gn': ('w1', 'w0', 0, (14, 16), (13, 17), 'w0 w0n'), 'hn': ('w2', 'w1', 1, (12, 16), (10, 18), 'go ga gn w1n'), 'hf': ('w2', 'w1', 1, (8, 12), (6, 14), 'go ga v1'), 'ga': ('w1', 'w0', 0, (12, 14), (11, 15), 'w0')})
EDGE_PICKS['N'] = PICKS['N']
SENDS = {'early': ('pic', None, 'lde', '1L1 0S1'), 'w0n': ('w0', (15, 16), 'c_sp1', 'A'), 'w0f': ('w0', (8, 10), 'c_sp0', '1L 0S'), 's0': ('00', (8, 10), 'c_s0', '0A'), 'img': ('pic', None, 'lds', '1L1 0S1'), 'i1f': ('i1', (9, 11), 'g_io', '1L 0S'), 'rv': ('w1', (9, 10), 'g_go', '1L'), 'w1n': ('w1', (14, 16), 'g_gn', 'A'), 'k1f': ('k1', (10, 14), 'g_ko', '1L 0S'), 's1': ('1O', (9, 12), 'c_s1', '0A'), 'imgn': ('pic', (12, 16), 'lda ldb', 'A'), 'jbn': ('jb', (12, 16), 'g_jn', 'A')}
EDGE_STARTS = {True: {'gn': 8, 'ga': 8}, False: {'ga': 16, 'go': 16, 'jf': 16}}
STEPS = 'l0io s0 l0 io ga gn N go O ko lN hn A s1 lO gf M if lA jn lM kb hf F jo jf lF yb ya'
EDGE_STEPS = 'l0 vp v0 ga gn N go O lN v1 hn A lO hf F lA jn lFjo lF jo jf yb ya'
ORDER = 'early w0n w0f s0 img i1f w1n rv imgn k1f s1 jbn'
MORE = {'jn': -2, 'gf': -2}
SPLIT_DG = True
EARLY_DRAM = True
LOADS = 'Sx Yy Se Yf Ya Yb Ys'
WIDE = ["w0", "w1", "w2", "pic", "i1", "k1", "jb", "yo"]
SCRATCH = {
    "vi": ("sbuf", [128, 128], I32), "xr": ("sbuf", [128, 160], BF), "r2": ("sbuf", [128, 128], BF),
    "pcol": ("sbuf", [128, 1], I32), "bi": ("sbuf", [128, 4], I32), "dig": ("sbuf", [128, 128], BF),
    "bf": ("sbuf", [128, 16], F32), "wrap": ("sbuf", [128, 4], F32), "zero": ("sbuf", [128, 144], BF),
    "lt": ("sbuf", [128, 2, 144], BF), "sel": ("sbuf", [128, 2, 144], BF), "spr": ("sbuf", [128, 144], BF),
    "keep": ("sbuf", [128, 64], F32), "kept": ("sbuf", [128, 8, 64], F32),
    "tb": ("sbuf", [128, 64], F32), "ws": ("sbuf", [128, 3072], BF),
    "s0n": ("sbuf", [128, 32], U16), "s0": ("sbuf", [128, 32], U16), "s1": ("sbuf", [128, 32], U16), "heldl": ("sbuf", [128, 64], U16),
    "l0": ("sbuf", [128, 960], U16), "l1": ("sbuf", [128, 960], U16), "l2": ("sbuf", [128, 960], U16),
    "held": ("sbuf", [128, 4096], BF), "stage": ("dram", [2, 128, (128 * FARIMG - EARLY) // 2], BF),
    "stage0": ("dram", [2, 128, EARLY // 2], BF),
    "cx": ("psum", [128, 512], F32), "blk": ("psum", [128, 16, 32], F32), "sp0": ("psum", [128, 512], F32),
    "sp1": ("psum", [128, 512], F32), "sp2": ("psum", [128, 512], F32), "pa": ("psum", [128, 512], F32),
    "pb": ("psum", [128, 512], F32), "pc": ("psum", [128, 512], F32),
}
SCRATCH.update({x: ("sbuf", [128, 3072], BF) for x in WIDE})
NAMES = ["early", "w0n", "w0f", "s0", "img", "i1f", "rv", "w1n", "k1f", "s1", "imgn", "jbn", "k1g", "s0n", "k1n"]
SEMAPHORES = (["vc", "gi", "gx", "g2", "ldy", "ldx", "lde", "lda", "ldb", "lds", "ms", "sel", "va", "vb", "lt", "spr", "dg",
               "t_b", "c_s0", "c_s1", "sent", "rsent", "sty_ya", "sty_yb", "sty_yc", "fill", "fill2", "rs_o", "keep",
               "sc", "vl", "wr", "ve", "hi", "kp", "tr", "wt", "c4", "c5", "v7", "v6", "dy"]
              + NAMES + ["at_" + x for x in NAMES if x[-1] != "n"] + ["c_s0n"]
              + ["g_" + x for x in "io ia in go ga gn ko kn ka ha hn gf if kb hf jn jo jf jc ya yb yc v0 v1 vp".split()]
              + [y + x for x in "NOMAF" for y in ("t_", "k_")] + [y + x for x in "012" for y in ("t_sp", "c_sp")]
              + ["l_%s%d" % (x, k) for x in "0NOMAF" for k in range(5)])


def plan(T, topo):
    cs = list(T.cores)
    near, far, flows = {}, {}, []
    for a, b in zip(cs, cs[1:]):
        if b in topo.cores_of(a):
            near[a], near[b] = b, a
        else:
            far[a], far[b] = b, a
            flows += [(a, b), (b, a)]
    relays, used = {}, set()
    for s, d in flows:
        mate = [x for x in range(0, SIM_CORES, len(topo.cores_of(d))) if topo.mates(x, d)][0]
        relays[(s, d)] = []
        for c, e in ((s, topo.die(s)), (mate, topo.die(d))) * 2:
            x = [x for x in topo.cores_of(c) if T.rank_of(x) is None and x not in used and topo.die(x) == e
                 and topo.may_write(x, d) and topo.may_write(s, x)][0]
            used.add(x)
            relays[(s, d)].append(x)
    return near, far, relays


def bits(engines):
    m = 0
    for e in engines:
        m |= 1 << e
    return m


def turned(up, a, b):
    return (a, b) if up else (24 - b, 24 - a)


def window(name, up, edge):
    a, b = (EDGE_GATHERS if edge else GATHERS)[name][4]
    x = (EDGE_STARTS if edge else STARTS)[up].get(name)
    return turned(up, *((a, b) if x is None else (x, b) if up else (a, x)))


def place(name, up, edge):
    gathers = EDGE_GATHERS if edge else GATHERS
    starts = sorted({window(x, up, edge)[0] for x in gathers if gathers[x][2] == gathers[name][2]})
    return 192 * starts.index(window(name, up, edge)[0])


def is_far(name):
    return SENDS[name][3][0] in "0123"


def landing(T, name, up):
    t, rr = SENDS[name][:2]
    if rr is None:
        c = 128 * turned(up, 8 - FARIMG, 8)[0]
        return (T.pic, c, EARLY) if name == "early" else (T.pic, c + EARLY, 128 * FARIMG - EARLY)
    a, b = turned(up, 16 - rr[1], 16 - rr[0])
    if name in USER:
        return T["l" + t[0]], place(USER[name], up, False) + 8 * a, 8 * (b - a)
    return T[t], 128 * a, 128 * (b - a)


def held(T, name, n):
    if name == "img":
        return T.stage[0]
    if name == "early" and EARLY_DRAM:
        return T.stage0[0]
    before = [x for x in SENDS if is_far(x) and x != "img" and (x in USER) == (name in USER)]
    c = sum(landing(T, x, True)[2] for x in before[:before.index(name)])
    return (T.heldl if name in USER else T.held)[:, c:c + n]


def rank_program(g, core, T, topo):
    near, far, relays = plan(T, topo)
    sem = T.sem
    if T.rank_of(core) is None:
        for (s, d), rel in relays.items():
            if core in rel:
                hand_on(g, core, T, topo, s, d, rel.index(core), T.rank_of(near[d]) > T.rank_of(d))
        return
    r = T.rank_of(core)
    nb, fb = near[core], far.get(core)
    up = T.rank_of(nb) > r
    edge = fb is None
    V, S, TE, SY = g.vector, g.scalar, g.tensor, g.sync
    top = 8 * r
    gathers, picks, steps, fills = (EDGE_GATHERS, EDGE_PICKS, EDGE_STEPS, EDGE_FILLS) if edge else (GATHERS, PICKS, STEPS, FILLS)
    cnt, seen, made = {}, set(), {}

    def R(a, b):
        return turned(up, a, b)

    def rows(t, a, b):
        a, b = R(a, b)
        return t[:, 128 * a:128 * b]

    def v(ins, name="vc", n=1):
        ins.then_inc(sem[name], n)
        cnt[name] = cnt.get(name, 0) + n

    def wait(q, name, k=None):
        k = cnt[name] if k is None else k
        key = ([x is q for x in (V, S, TE, SY, g)].index(True), name, k)
        if key not in seen:
            seen.add(key)
            q.wait_ge(sem[name], k)

    def ts(out, in0, s1, op0, s2=None, op1=None):
        if op1 is None:
            return V.tensor_scalar(out=out, in0=in0, scalar1=s1, scalar2=None, op0=op0)
        return V.tensor_scalar(out=out, in0=in0, scalar1=s1, scalar2=s2, op0=op0, op1=op1)

    def both(name, k=None):
        wait(V, name, k)
        wait(S, name, k)

    first = 0 if EARLY_DRAM and not edge else EARLY
    fa = 128 * (R(*SENDS["imgn"][1]) if edge else R(8, 8 + FARIMG))[0] - 1024
    cuts = [(0, fa), (fa + first, 1024)] if fa and first else [(first, 1024), (1024, 1024)]
    for x in LOADS.split():
        q = S if x[0] == "S" else SY
        if x[1] == "x":
            v(q.dma_start(out=T.vi[64:128], in_=T.vx[:]), "ldx", 16)
        elif x[1] == "y":
            v(q.dma_start(out=T.vi[0:64], in_=T.vy[:]), "ldy", 16)
        elif x[1] in "ef" and not first:
            k = "ef".index(x[1])
            c = fa + k * EARLY // 2
            v(q.dma_start(out=T.stage0[k], in_=T.img[:, c:c + EARLY // 2]), "lde", 16)
        elif x[1] == "e":
            v(q.dma_start(out=T.pic[:, 1024 + fa:1024 + fa + first], in_=T.img[:, fa:fa + first]), "lde", 16)
        elif x[1] in "ab":
            a, b = cuts["ab".index(x[1])]
            if a < b:
                v(q.dma_start(out=T.pic[:, 1024 + a:1024 + b], in_=T.img[:, a:b]), "ld" + x[1], 16)
        elif x[1] == "s" and not edge and "img" in SENDS:
            n = (128 * FARIMG - EARLY) // 2
            for k in range(2):
                c = fa + EARLY + k * n
                v(q.dma_start(out=T.stage[k], in_=T.img[:, c:c + n]), "lds", 16)

    def iota(out, pattern, base, cm, name):
        g.iota(out=out, pattern=pattern, base=base, channel_multiplier=cm,
               allow_small_or_imprecise_dtypes=True).then_inc(sem[name], 1)
    iota(T.pcol[:], [[1, 1]], 0, 1, "gi")
    iota(T.xr[:, 0:145], [[1, 145]], -1, 0, "gx")
    iota(T.r2[:], [[64, 4], [1, 32]], -3, 0, "g2")
    v(V.memset(T.zero[:], 0.0), "ms")
    v(V.memset(T.w0[:, 1024:1536], 0.0), "fill")
    S.wait_ge(sem.ms, 1)
    RC, WT, KP, W0, WP, C4, C5, HI, LO, K1 = range(10)

    def bf(k, h=slice(0, 128)):
        return T.bf[h, k:k + 1]

    def const(out, like, bias, name, scale=1.0):
        v(S.activation(out=out, in_=like, func=F.Identity, bias=bias, scale=scale), name)

    def fill(name, todo):
        for t, a, b in todo:
            v(V.memset(rows(T[t], a, b), 0.0), name)
    ys, xs = slice(0, 64), slice(64, 128)
    q16 = T.bi[:, 1:2]
    const(T.lt[:, :, 128:144], T.zero[:, 0:32], 0.0, "lt")
    const(bf(WT, ys), T.zero[ys, 0:1], 128.0, "wt")
    const(bf(WT, xs), T.zero[xs, 0:1], 1.0, "wt")
    V.wait_ge(sem.gi, 1)
    for k, x, op, s in ((0, 7, A.bitwise_and, "v7"), (2, 63, A.bitwise_and, "v6"), (1, 15, A.bitwise_and, "va"),
                        (3, 4, A.arith_shift_right, "va")):
        v(ts(T.bi[:, k:k + 1], T.pcol[:], x, op), s)
    wait(V, "v7")
    v(ts(bf(RC), T.bi[:, 0:1], float(top + 8), A.add), "vb")
    wait(V, "v6")
    v(ts(bf(C4), T.bi[:, 2:3], 4.0, A.mult), "c4")
    v(ts(bf(C5), T.bi[:, 2:3], 4.0, A.mult, -32.0, A.add), "c5")
    wait(V, "va")
    v(ts(bf(W0), q16, 0.0, A.is_equal, 127.0, A.mult))
    v(ts(bf(KP), T.bi[:, 3:4], 16.0, A.mult))
    folds = sorted({x[4] for x in picks.values()})
    wait(S, "fill")
    const(T.w0[:, 1536:2048], T.w0[:, 1024:1536], 0.0, "fill")
    S.wait_ge(sem.gx, 1)
    const(T.cx[xs, 0:128], T.xr[xs, 1:129], 0.0, "sc")
    wait(S, "vb")
    const(T.cx[ys, 0:128], T.zero[ys, 0:128], bf(RC, ys), "sc")
    for k in folds:
        const(T.sel[:, k - 1, :], T.zero[:], 0.0, "keep")
    wait(V, "c4")
    V.wait_ge(sem.gx, 1)
    for c, h in enumerate((ys, xs)):
        v(ts(T.spr[h], T.xr[h, 1 - c:145 - c], 2.0, A.mult, bf(C4, h), A.is_equal), "spr")

    def first_matrix(e):
        wait(V, "g2", 1)
        wait(V, "wt")
        wait(V, "c5")
        v(ts(T.lt[:, e, 0:128], T.r2[:], bf(C4 + e), A.is_equal, bf(WT), A.mult), "lt")

    V.wait_ge(sem.ldx, 16)
    v(ts(T.wrap[xs, 0:1], T.vi[xs, 0:1], 0.0, A.is_lt, 128.0, A.mult), "wr")
    v(ts(T.wrap[xs, 1:2], T.vi[xs, 127:128], 0.0, A.is_gt, -128.0, A.mult), "wr")
    wait(V, "sc")
    V.wait_ge(sem.ldy, 16)
    v(V.tensor_tensor(out=T.dig[:, 1:127], in0=T.vi[:, 1:127], in1=T.cx[:, 1:127], op=A.add), "dy")
    v(ts(T.dig[ys, 0:128:127], T.vi[ys, 0:128:127], bf(RC, ys), A.add), "dy")
    wait(V, "wr")
    for k, x in enumerate((0, 127)):
        v(ts(T.dig[xs, x:x + 1], T.vi[xs, x:x + 1], T.cx[xs, x:x + 1], A.add, T.wrap[xs, k:k + 1], A.add), "dg")
    first_matrix(0)
    first_matrix(1)
    wait(V, "vc")
    v(ts(bf(WP), q16, 1.0, A.is_le, bf(W0), A.add))
    if 2 in folds:
        v(ts(bf(LO), q16, 8.0, A.is_lt, BIG, A.mult), "vl")
    fill("fill2", fills[up])
    wait(V, "vc")
    wait(V, "keep")
    for k, c in [(1, 7), (1, 15)] * (2 in folds) + [(0, 15)] * (1 in folds):
        v(ts(T.sel[:, k, c:c + 128:16], T.xr[:, 1:129:16], bf(KP), A.is_equal, bf(WP), A.mult), "sel")
    if edge:
        for k in range(1, 3):
            v(ts(bf(K1 + k), q16, 0.0, A.is_equal, float(-k if up else k), A.mult), "ve")

    def keep():
        const(T.keep[:, 0:64:2], T.zero[:, 0:32], -2 * BIG, "kp")
        wait(S, "vl")
        const(bf(HI), bf(LO), -BIG, "hi", 2.0)
        wait(S, "hi")
        const(T.keep[:, 1:64:2], T.zero[:, 0:32], bf(HI), "kp")

    for h, x in enumerate(OWN_QUEUES):
        q = S if x == "S" else SY
        wait(q, "fill")
        wait(q, "dy")
        if h or not SPLIT_DG:
            wait(q, "dg")
        v(q.dma_start(out=T.w0[h:128:16, 1024:2048], in_=T.dig[64 * h:64 * h + 64]), "rs_o", 16)

    def copy_out(x):
        a, b, q, t = SPREAD[x]
        ps, n = T["sp" + x], 128 * (b - a)
        if q == "S":
            S.wait_ge(sem["t_sp" + x], 1)
            v(S.activation(out=rows(T[t], a, b), in_=ps[:, 0:n], func=F.Copy), "c_sp" + x)
        else:
            V.wait_ge(sem["t_sp" + x], 1)
            v(V.tensor_copy(out=rows(T[t], a, b), in_=ps[:, 0:n]), "c_sp" + x)

    def listed(out, src, base, name, less=None):
        v(ts(out, src, -128.0 * base, A.add) if less is None else ts(out, src, -128.0 * base, A.add, less, A.subtract), name)

    def sums(x):
        if x == "0":
            wait(V, "tr")
            return 0, (8, 16), lambda c, d: T.tb[:, 8 * (c - 8):8 * (d - 8)], None
        level, rr, ps, _, fold = picks[x]
        a, k = R(*rr)[0], list(picks).index(x)
        if fold == 1:
            wait(V, "t_" + x)
            return level, R(*rr), lambda c, d: T[ps][:, 8 * (c - a):8 * (d - a)], None
        if "k_" + x not in cnt:
            picked(x)
        wait(V, "k_" + x)
        return level, R(*rr), lambda c, d: T.kept[:, k, 16 * (c - a) + 1:16 * (d - a):2], bf(LO)

    def lists(name, users=None):
        level, (a, b), src, less = sums(name)
        want = {}
        for x, gt in gathers.items():
            if gt[2] == level:
                c, d = R(*gt[3])
                want.setdefault((window(x, up, edge)[0], place(x, up, edge)), set()).update(range(max(a, c), min(b, d)))
        for (w, at), have in sorted(want.items(), key=lambda x: -len(x[1])):
            if have and (level, at, min(have)) not in made and (not users or at == place(users, up, edge)):
                c, d, s = min(have), max(have) + 1, "l_%s%d" % (name, at // 192)
                listed(T["l%d" % level][:, at + 8 * c:at + 8 * d], src(c, d), top + w, s, less)
                for i in range(c, d):
                    made[(level, at, i)] = s
        if name == "F" and edge and "l_F4" not in cnt and users in ("", "jf"):
            w, at = window("jf", up, edge)[0], place("jf", up, edge)
            for k in range(1, 5):
                i = R(8 - k, 9 - k)[0]
                listed(T.l2[:, at + 8 * i:at + 8 * i + 8], src(*R(8, 9)), top + w + (k if up else -k), "l_F4", less)
                made[(2, at, i)] = "l_F4"

    def for_far(name):
        _, _, src, less = sums(SENDS[name][0][1])
        a, b = R(*SENDS[name][1])
        to = fb if is_far(name) else nb
        listed(T[name][:, 0:8 * (b - a)], src(a, b), 8 * T.rank_of(to) + window(USER[name], not up, to not in far)[0],
               "c_" + name, less)
    TE.wait_ge(sem.spr, 2)
    wait(TE, "dy")
    wait(TE, "dg")
    front = [x for x in FRONT.split() if x == "l" or not (edge and SPREAD[x][3] == "ws" and SPREAD[x][0] == 8)]
    for x in front:
        if x == "l":
            TE.wait_ge(sem.lt, 3)
            for e in range(2):
                for u in range(4):
                    ins = TE.matmul(T.blk[:, 0:2, 16 * e:16 * e + 16], T.lt[:, e, 3 - u:131 - u],
                                    T.dig[:, 32 * u:32 * u + 32], u == 0, u == 3)
            ins.then_inc(sem.t_b, 1)
            V.wait_ge(sem.t_b, 1)
            for w in range(2):
                v(V.transpose(out=T.tb[:, w:64:2], in_=T.blk[:, w, :]), "tr")
        else:
            a, b = R(*SPREAD[x][:2])
            for i in range(a, b):
                ins = TE.matmul(T["sp" + x][:, 128 * (i - a):128 * (i - a + 1)], T.spr[:, 2 * (i - 8):2 * (i - 8) + 128],
                                T.dig[:], True, True)
            ins.then_inc(sem["t_sp" + x], 1)
            copy_out(x)
        if x == KEEP_AFTER and 2 in folds:
            keep()

    groups = engine_groups(topo, near, far, relays, core)

    def need(y):
        if y == "own":
            for name in ("lda", "ldb", "lde")[:3 if first else 2]:
                if name in cnt:
                    both(name)
        elif y == "w0":
            for name in ["rs_o"] if OWN_DMA else ["c_sp" + k for k in SPREAD]:
                both(name)
        elif y not in SENDS:
            both("g_" + y)
        elif is_far(y):
            both(y, len(SENDS[y][3].split()) * len(topo.engines(relays[(fb, core)][0], core)))
        else:
            both(y, len(groups[SENDS[y][3]]) + (len(groups[EDGE_FIRST]) if y == "imgn" and nb not in far else 0))

    def gather(x):
        out, win, level, rr, _, needs = gathers[x]
        a, b = R(*rr)
        c, d = window(x, up, edge)
        at = place(x, up, edge)
        for i in range(a, b):
            if (level, at, i) in made:
                both(made[(level, at, i)])
            else:
                assert R(i, i + 1)[0] >= 16 or R(i, i + 1)[0] < 16 - SENDS["s%d" % level][1][0]
        for t, e, f in fills[up]:
            if t == win and R(e, f)[0] < d and c < R(e, f)[1]:
                both("fill2")
        for y in needs.split():
            need(y)
        lst, m = T["l%d" % level], 4 * (a + b) + (EDGE_MORE if edge else MORE).get(x, 0)
        win = T[win][:, 128 * c:128 * d]
        v(V.tensor_copy(out=T[out][:, 128 * a:16 * m], in_=win.indirect(lst[:, at + 8 * a:at + m])), "g_" + x)
        v(S.activation(out=T[out][:, 16 * m:128 * b], in_=win.indirect(lst[:, at + m:at + 8 * b]), func=F.Copy), "g_" + x)

    def pick(x):
        level, rr, ps, needs, fold = picks[x]
        a, b = R(*rr)
        n = 16 // fold
        wait(TE, "sel")
        for y in needs.split():
            wait(TE, "g_" + y)
        for q in range(n):
            ins = TE.matmul(T[ps][:, 0:8 * fold * (b - a)], T.sel[:, fold - 1, n - 1 - q:n + 127 - q],
                            T["w%d" % level][:, 128 * a + q:128 * b:n], q == 0, q == n - 1)
        v(ins, "t_" + x)

    def picked(x):
        level, rr, ps, _, _ = picks[x]
        n, k = 16 * (rr[1] - rr[0]), list(picks).index(x)
        wait(V, "t_" + x)
        wait(V, "kp")
        v(V.tensor_tensor_scan(T.kept[:, k, 0:n], T.keep[:, 0:n], T[ps][:, 0:n], 0.0, A.add, A.max), "k_" + x)

    def beyond(level):
        win = T["w%d" % level]
        for k in range(1, 2 ** level + 1):
            o, i = rows(win, 8 - k, 9 - k), rows(win, 8, 9)
            if k % 2:
                v(ts(o, i, bf(K1 + k), A.add), "g_v%d" % level)
            else:
                v(S.activation(out=o, in_=i, func=F.Identity, bias=bf(K1 + k)), "g_v%d" % level)

    for x in steps.split():
        if x in gathers:
            gather(x)
        elif x in picks:
            pick(x)
        elif x[0] == "k" and x[1] in picks:
            if picks[x[1]][4] == 2 and "k_" + x[1] not in cnt:
                picked(x[1])
        elif x[0] == "l":
            lists(x[1], x[2:])
        elif x in USER:
            for_far(x)
        elif x == "vp":
            need("own")
            for k in range(8):
                o, i = rows(T.pic, k, k + 1), rows(T.pic, 8, 9)
                v(V.tensor_copy(out=o, in_=i) if k % 2 else S.activation(out=o, in_=i, func=F.Copy), "g_vp")
        else:
            both("ve")
            need({"v0": "w0", "v1": "go"}[x])
            beyond(int(x[1]))

    sent = 0
    for name in ORDER.split():
        t, rr, ready, ways = SENDS[name]
        if edge and is_far(name) and name != "early":
            continue
        for s in ready.split() + ["lde"] * (name == "imgn"):
            if s in cnt:
                wait(g, s)
        if edge and name in ("early", "imgn"):
            c, d = (fa, fa + EARLY) if name == "early" else (fa + EARLY, fa + 128 * (rr[1] - rr[0]))
            o = 1024 * (1 + r - T.rank_of(nb))
            rid, pid = topo.addr(nb, core)
            es = groups[EDGE_FIRST if name == "early" else ways]
            g.remote_dma(T.pic[:, c + o:d + o], T.pic[:, c + 1024:d + 1024], sem.imgn, sem.sent, pid, rid, bits(es))
            sent += len(es)
        elif is_far(name):
            t, c, n = landing(T, name, not up)
            t, c = (T[name], 0) if name in USER else (t, c - 1024 * (r - T.rank_of(fb)))
            t = T.ws if name == "w0f" and OWN_DMA else t
            ways = ways.split()
            n //= len(ways)
            tr = []
            for k, way in enumerate(ways):
                rid, pid = topo.addr(relays[(core, fb)][int(way[0])], core)
                tr.append(RemoteDMATransfer(dst_ids=[DstId(rid=rid, pnc=pid)], dma_engine_mask=bits(groups[way[1:]]),
                                            remote_sem=sem["at_" + name], dst=held(T, name, n),
                                            src=T.stage[k] if name == "img" else T.stage0[k] if name == "early" and not first
                                            else t[:, c + k * n:c + (k + 1) * n]))
                sent += len(groups[way[1:]])
            g.remote_dma_fused(tr, local_sem=sem.sent)
        else:
            c, d = R(*rr)
            o = 8 * (r - T.rank_of(nb))
            rid, pid = topo.addr(nb, core)
            if name in USER:
                at = place(USER[name], not up, nb not in far)
                dst, src = T["l" + t[0]][:, at + 8 * (c + o):at + 8 * (d + o)], T[name][:, 0:8 * (d - c)]
            else:
                dst, src = T[t][:, 128 * (c + o):128 * (d + o)], rows(T.ws if name == "w0n" and OWN_DMA else T[t], *rr)
            g.remote_dma(dst, src, sem[name], sem.sent, pid, rid, bits(groups[ways]))
            sent += len(groups[ways])

    last = [x for x in steps.split() if x[0] == "y"]
    for x in last:
        a, b = R(*gathers[x][3])
        wait(SY, "g_" + x)
        v(SY.dma_start(out=T.y[:, 128 * (a - 8):128 * (b - 8)], in_=T.yo[:, 128 * a:128 * b]), "sty_" + x, 16)
    g.wait_ge(sem.sent, sent)
    for x in last:
        wait(SY, "sty_" + x)
    for x in cnt:
        if not any(k[1] == x and k[2] == cnt[x] for k in seen) and x[:2] in ("l_", "ld", "g_", "vc", "fi"):
            wait(SY, x)


def engine_groups(topo, near, far, relays, core):
    ref = core if core in far else near[core]
    leave = topo.engines(ref, relays[(ref, far[ref])][1])
    every = topo.engines(core, near[core])
    stay = [e for e in every if e not in leave]
    h = len(stay) // 2
    return {"L": leave, "S": stay, "A": every, "L1": leave[:h], "L2": leave[h:], "S1": stay[:h], "S2": stay[h:]}


def hand_on(g, core, T, topo, s, d, i, up):
    sem = T.sem
    es = topo.engines(core, d)
    rid, pid = topo.addr(d, core)
    groups = engine_groups(topo, *plan(T, topo), s)
    sent = 0
    for name in ORDER.split():
        ways = SENDS[name][3].split() if is_far(name) else []
        for k, way in enumerate(ways):
            if int(way[0]) == i:
                t, c, n = landing(T, name, up)
                n //= len(ways)
                g.wait_ge(sem["at_" + name], len(groups[way[1:]]))
                g.remote_dma(t[:, c + k * n:c + (k + 1) * n], held(T, name, n), sem[name], sem.rsent, pid, rid, bits(es))
                sent += len(es)
    if sent:
        g.wait_ge(sem.rsent, sent)
